import numpy as np, ml_dtypes
CORES = [9,25,41,57]
N = 4
import mx_ref
BF = ml_dtypes.bfloat16
def gcols(t, e):
    v = np.concatenate([t.reshape(8, 16, -1, 4), np.zeros((8, 16, 1, 4), BF)], axis=2)
    return np.ascontiguousarray(np.stack([v[g][:, e[g]] for g in range(8)])).reshape(128, -1)
def tile(rs):
    return np.stack(rs, axis=2).reshape(128, -1).astype(BF)
def pick(q, e):
    c = np.concatenate([q[0].reshape(128, -1, 4), np.zeros((128, 1, 4), np.uint8)], axis=1); s = np.concatenate([q[1], np.ones((16, 1), np.uint8)], axis=1)
    return (np.ascontiguousarray(c[:, e].reshape(128, -1)), np.ascontiguousarray(s[:, e]))
def join(*qs):
    return (np.concatenate([q[0] for q in qs], axis=1), np.concatenate([q[1] for q in qs], axis=1))
def put(q, e, v):
    c, s = q[0].reshape(128, -1, 4).copy(), q[1].copy(); c[:, e] = v[0].reshape(128, -1, 4); s[:, e] = v[1]
    return (c.reshape(128, -1), s)
def pk(c, s):
    return (np.ascontiguousarray(c), mx_ref.live(s))
def emit(q):
    return q[0], q[1]
def packed(v, rng):
    q = [mx_ref.quantize(np.ascontiguousarray(v[r])) for r in range(N)]
    return np.stack([a for a, b in q]), np.stack([mx_ref.plane(b, rng) for a, b in q])
def values_of_codes():
    e, c = np.zeros((128, 128, 4), np.float32), np.zeros((128, 2, 4), np.uint8)
    e[np.arange(128), np.arange(128), 0] = 1
    c[:127, :, 0] = np.arange(256).reshape(2, 128).T[:127]
    return mx_ref.matmul(mx_ref.quantize(e.reshape(128, 512).astype(BF)), (c.reshape(128, 8), np.full((16, 2), 127, np.uint8))).T.reshape(-1).astype(np.float64)
CODE_VALUE, SCALE_VALUE = values_of_codes(), 2.0 ** (np.arange(256) - 127.0)
def decode(q):
    return (CODE_VALUE[q[0]].reshape(16, 8, -1, 4) * SCALE_VALUE[q[1]][:, None, :, None] + 0.0).reshape(128, -1).astype(np.float32)
def f(rng, *shape):
    return mx_ref.flush((rng.standard_normal(shape, dtype=np.float32) * np.exp2(rng.integers(-2, 3, shape[:-1] + (1,)))).astype(BF))
def wide(rng, *shape, cols=0):
    v = rng.standard_normal(shape, dtype=np.float32) * np.exp2(rng.integers(-12, 13, shape)).astype(np.float32)
    if cols: v *= np.repeat(np.exp2(rng.integers(-cols, cols + 1, shape[:-2] + (1, shape[-1] // 4))) * (rng.random(shape[:-2] + (1, shape[-1] // 4)) > 0.0625), 4, axis=-1).astype(np.float32)
    return mx_ref.flush(v.astype(BF))
C, CAP = 320, 128
MASK = [1, 2, 3]
def big(v):
    v = v.astype(np.float32)
    v[np.abs(v) < np.float32(2.0 ** -16)] = 0
    return v.astype(BF)
def alike(u):
    return np.stack([np.reshape(u, (128, 512)).astype(np.float32).astype(BF)] * N)
def numbers_of(rng):
    return {"x": big(f(rng, N, 128, 4 * C)), "u": alike(f(rng, 128, 512)), "v": np.array(f(rng, N, 128, 512))}
def parts(d):
    u = d["u"][0].astype(np.float32).reshape(128, 128, 4)
    u[:, ::16] = 0
    u[:, 1::16] = 0
    return d["x"].astype(np.float32).reshape(N, 8, 16, C, 4), u
def back(x):
    return x.astype(np.float32).reshape(N, 128, 4 * C).astype(BF)
def weights(rng, still=[]):
    w = big(f(rng, N, 128, 2048)).reshape(N, 8, 16, 4, 8, 16, 4)
    for i in still:
        w[:, :, i] = 0
        w[:, :, :, :, :, i] = 0
    c, s = packed(w.reshape(N, 128, 2048), rng)
    return {"wc": c, "ws": s}
def setup_inputs(rng):
    return {**numbers_of(rng), **weights(rng)}
def setup_inputs_ties(rng):
    d = numbers_of(rng)
    x, u = parts(d)
    e = rng.permutation(N)
    k = rng.integers(0, 3, (N, 8, C))
    s = rng.integers(-1, 2, (N, 8, C))
    k[e[0]] = 0
    k[e[1]] *= -1
    k[e[3]] = np.arange(C) // 128
    s[e[0]] = 0
    s[e[2]] = 1
    s[e[3]] = -1
    x[:, :, :2] = 0
    x[:, :, 0, :, 0] = k
    x[:, :, 1, :, 0] = s
    for h in range(0, 128, 16):
        u[h, h, 0] = 1
        u[h + 1, h + 1, 0] = 1
    return {"x": back(x), "u": alike(u), "v": d["v"], **weights(rng, [0, 1])}
def setup_inputs_near(rng):
    d = numbers_of(rng)
    x, u = parts(d)
    x[:, :, 0] = 0
    x[:, :, 8:] = 0
    o = rng.permutation(8)
    s = rng.integers(0, 16, (N, 8, C))
    sign = rng.integers(-1, 2, (N, 8, C))
    for g in range(8):
        h, kind = 16 * g, o[g] // 2
        if kind < 3:
            c = 2.0 ** -30 if kind == 2 else 1.0
            x[:, g, 0, :, 0] = 1.0 if kind == 0 else -1.0 if kind == 1 else rng.integers(0, 2, (N, C)) * 2.0 - 1.0
            x[:, g, 8] = ((s[:, g, :, None] >> np.arange(4)) & 1) * np.exp2(np.arange(4) - 23.0)
            x[:, g, 11, :, 0] = 2.0 ** -10
            x[:, g, 9, :, 0] = sign[:, g] * 2.0 ** -23
            u[h, h, 0] = c
            u[h + 8, h] = c
            u[h + 11, h, 0] = c
            u[h + 9, h + 1, 0] = 2.0 ** -30
        else:
            t = s[:, g] // 4 % 2
            x[:, g, 10, :, 0] = np.where(s[:, g] < 8, -1.0, 1.0) * (1.0 + (s[:, g] % 4) * 0.125) * 2.0 ** -30
            x[:, g, 12, :, 0] = -t * (1.25 * 2.0 ** -30)
            x[:, g, 13, :, 0] = t * (1.125 * 2.0 ** -30)
            x[:, g, 9, :, 0] = sign[:, g] * (1.125 * 2.0 ** -30)
            x[:, g, 14, :, 0] = -sign[:, g] * (1.25 * 2.0 ** -30)
            u[h + 10, h, 0] = 2.0 ** -30
            u[h + 12, h, 0] = 2.0 ** -30
            u[h + 13, h, 0] = 1.125 * 2.0 ** -30
            u[h + 9, h + 1, 0] = 1.125 * 2.0 ** -30
            u[h + 14, h + 1, 0] = 2.0 ** -30
        if o[g] % 2:
            for r in range(N): x[r, g, 0 if kind < 3 else 10, rng.integers(C), 0] = 2.0 ** 29 * (rng.integers(0, 2) * 2.0 - 1.0)
    return {"x": back(x), "u": alike(u), "v": d["v"], **weights(rng, [0, 8, 9, 10, 11, 12, 13, 14, 15])}
def setup_inputs_caps(rng):
    d = numbers_of(rng)
    x, u = parts(d)
    k = rng.permutation([0, 1, CAP - 1, CAP, CAP + 1, 257, C - 1, C])
    x[:, :, 0] = 0
    x[:, :, 0, :, 0] = np.where(np.arange(C) < k[:, None], 1.0, -1.0) * (1.0 + 0.125 * rng.integers(0, 8, (N, 8, C)))
    x[:, :, 0, :, 1:3] = rng.integers(-3, 4, (N, 8, C, 2)) * 0.03125
    a = (1.125 + 0.25 * rng.integers(0, 4, (N, 8, C, 32))) * np.exp2(-rng.integers(8, 15, (N, 8, C, 32)).astype(np.float32))
    np.put_along_axis(a, rng.integers(0, 32, (N, 8, C, 1)), 1.96875, axis=3)
    a *= (rng.integers(0, 2, a.shape) * 2.0 - 1.0) * np.exp2(rng.integers(-3, 4, (N, 8, C, 1)).astype(np.float32))
    x[:, :, 8:] = a.reshape(N, 8, C, 8, 4).transpose(0, 1, 3, 2, 4)
    for h in range(0, 128, 16):
        u[h, h, :3] = 1
        u[h, h + 1, 0] = 1
    return {"x": back(x), "u": alike(u), "v": d["v"], **weights(rng, [0])}
def setup_inputs_huge(rng):
    d = numbers_of(rng)
    x, u = parts(d)
    h = rng.permutation(8)
    x = (0.75 + 0.2 * rng.random((N, 8, 16, C, 4))) * 2.0 ** 30
    x[:, h[:4]] *= -1.0
    x[:, h[4:]] *= rng.integers(0, 2, (N, 1, 1, C, 1)) * 2.0 - 1.0
    for i in range(8):
        g = 16 * h[i]
        for a in (h[:4] if i < 2 else h[4:] if i in (4, 5) else h[i:i + 1]): u[16 * a:16 * a + 16, g] = 2.0 ** 30 * (1.0 - 0.1 * rng.random((16, 4)))
        if i == 1:
            for a in h[4:]: u[16 * a:16 * a + 16, g] = 0.875 * 2.0 ** 30 * (1.0 - 0.1 * rng.random((16, 4)))
        a = 16 * h[4 + i % 4]
        u[a:a + 16, g + 1] = 2.0 ** 30 * (1.0 - 0.1 * rng.random((16, 4))) * (rng.integers(0, 2) * 2.0 - 1.0)
    w = np.zeros((N, 128, 4, 128, 4), np.float32)
    i = np.arange(128)
    for b in range(4): w[:, i, b, i, b] = -1
    c, s = packed(w.reshape(N, 128, 2048).astype(BF), rng)
    return {"x": back(x), "u": alike(u), "v": d["v"], "wc": c, "ws": s}
def setup_inputs_spread(rng):
    d = setup_inputs(rng)
    d["x"] = big(wide(rng, N, 128, 4 * C, cols=6))
    return d
def check_inputs(d):
    b = []
    for k in ("x", "u", "v"):
        a = np.abs(d[k].astype(np.float32))
        if not (np.isfinite(a).all() and ((a == 0) | (a >= 2.0 ** -30) & (a <= 2.0 ** 30)).all()): b.append("a value of " + k)
    if (d["u"].astype(np.float32) != d["u"][:1].astype(np.float32)).any(): b.append("u isn't the same on all ranks")
    none, least, most = [emit(mx_ref.quantize(np.full((128, 16), k, np.float32).astype(BF)))[1][0, 0] for k in (0.0, 2.0 ** -30, 2.0 ** 30)]
    for r in range(N):
        if ((d["wc"][r] == 0x7F) | (d["wc"][r] == 0xFF)).any(): b.append("wc: a code that is no number")
        s = mx_ref.live(d["ws"][r])
        if ((s != none) & ((s < least) | (s > most))).any(): b.append("ws: a scale out of range")
    return b
def reference(x, u, v, wc, ws):
    qu = [mx_ref.quantize(u[r]) for r in range(N)]
    lay = [pk(wc[r], ws[r]) for r in range(N)]
    now = [x[r] for r in range(N)]
    before = np.arange(C)[:, None] < np.arange(C)
    for m in MASK:
        q = [mx_ref.quantize(now[r]) for r in range(N)]
        tab, take = np.zeros((N, 8, C), np.int64), np.zeros((N, 8, C), bool)
        for r in range(N):
            s = mx_ref.matmul(qu[r], q[r])
            k = s[::16] + np.float32(0.0)
            tab[r] = np.count_nonzero((k[:, :, None] >= k[:, None, :]) & before, axis=1)
            want = s[1::16] > 0
            np.put_along_axis(take[r], np.argsort(~want, axis=1, kind="stable")[:, :CAP], True, axis=1)
            take[r] &= want
        e = np.arange(N) ^ m
        mixed = np.where(take, tab[e], tab)
        place = np.zeros((N, 8, C), np.int64)
        for i in range(C):
            place[:, :, :i] += place[:, :, :i] >= mixed[:, :, i:i + 1]
            place[:, :, i] = mixed[:, :, i]
        o = np.argsort(place, axis=2, kind="stable")
        name = o + C * np.take_along_axis(take, o, axis=2)
        made = []
        for r in range(N):
            z = gcols(np.concatenate([now[r], decode(q[e[r]]).astype(BF)], axis=1), name[r])
            qz = mx_ref.quantize(z)
            made.append(tile([mx_ref.matmul(pick(lay[r], np.arange(128 * b, 128 * b + 128)), qz) * np.float32(0.03125) + z[:, b::4].astype(np.float32) for b in range(4)]))
        now = made
    y, od = np.zeros((N, 128, C), np.float32), np.zeros((N, 8, C), np.float32)
    oc, osc = np.zeros((N, 128, 4 * C), np.uint8), np.zeros((N, 16, C), np.uint8)
    for r in range(N):
        q = mx_ref.quantize(now[r])
        y[r] = mx_ref.matmul(mx_ref.quantize(v[r]), q)
        od[r] = name[r]
        oc[r], osc[r] = emit(q)
    return {"y": y, "od": od, "oc": oc, "osc": osc}

@@ -1,0 +1,421 @@
+import numpy as np
+from concourse.mybir import dt, AluOpType as OP, ActivationFunctionType as AF
+
+C = 320
+NB = C // 16
+ROUNDS = [1, 2, 3]
+CAP = 128.0
+BIG = 1e29
+HALF = "float16"
+
+GROW = 1027.0 / 1024.0
+UNIT = 2.0 ** -9
+B1, B2 = 8283.0, 8288.0
+MV1, MV2, MV3 = 239, 260, 334
+SEG = 162
+STEPS = 2 * SEG
+
+
+def _bases(b):
+    f = np.float32
+    x, out = f(b), []
+    for _ in range(SEG):
+        x = f(f(GROW) * x)
+        out.append(int(np.rint(x)))
+    drift = 0
+    for j in range(1, SEG):
+        drift += 1027 * out[j - 1] - 1024 * out[j]
+    return out, drift
+
+
+N1, DRIFT1 = _bases(B1)
+N2, DRIFT2 = _bases(B2)
+REBASE = 1024 * N2[0] - MV2 - 1027 * N1[-1] + MV1
+LEAVE = -(1027 * N2[-1] + 171 - MV3 + 160)
+
+Q0 = [0, 64, 128, 192, 192]
+CB = [0, 320, 576, 768, 896]
+PAD = [52, 52, 52, 52, 116]
+KS = 11
+HEAD = 64
+
+X4 = "float8_e4m3fn_x4"
+SCRATCH = {
+    "x0": ("sbuf", [128, 4 * C], "bfloat16"), "xn": ("sbuf", [128, 4 * C], "bfloat16"),
+    "ut": ("sbuf", [128, 512], "bfloat16"), "vt": ("sbuf", [128, 512], "bfloat16"),
+    "uq": ("sbuf", [128, 128], X4), "us": ("sbuf", [128, 128], "uint8"),
+    "pq": ("sbuf", [128, 256], X4), "ps": ("sbuf", [128, 256], "uint8"),
+    "vq": ("sbuf", [128, 128], X4), "vs": ("sbuf", [128, 128], "uint8"),
+    "wq": ("sbuf", [128, 512], X4), "wp": ("sbuf", [128, 512], "uint8"),
+    "et": ("sbuf", [128, 2048], "bfloat16"), "eq": ("sbuf", [128, 512], X4), "es": ("sbuf", [128, 512], "uint8"),
+    "gt": ("sbuf", [128, 512], "bfloat16"), "gq": ("sbuf", [128, 128], X4), "gs": ("sbuf", [128, 128], "uint8"),
+    "ct": ("sbuf", [128, 4096], "bfloat16"), "cq": ("sbuf", [128, 5 * C], X4), "cs": ("sbuf", [128, 5 * C], "uint8"),
+    "zt": ("sbuf", [128, 4 * C], "bfloat16"), "zq": ("sbuf", [128, C], X4), "zs": ("sbuf", [128, C], "uint8"),
+    "z32": ("sbuf", [128, 4 * C], "bfloat16"),
+    "zb": ("sbuf", [128, 768], "bfloat16"), "ones": ("sbuf", [128, 128], "bfloat16"),
+    "ident": ("sbuf", [128, 128], "bfloat16"), "gidx": ("sbuf", [128, 128], "bfloat16"),
+    "pi": ("sbuf", [128, 4], "int32"), "pf": ("sbuf", [128, 8], "float32"), "cv": ("sbuf", [128, 4], "float32"),
+    "oi": ("sbuf", [128, 36], "int32"), "off": ("sbuf", [128, 36], "uint16"),
+    "cmod": ("sbuf", [128, C], "bfloat16"), "mk": ("sbuf", [128, C], "bfloat16"), "r0": ("sbuf", [128, C], "bfloat16"),
+    "wa": ("sbuf", [128, C], "bfloat16"), "wb": ("sbuf", [128, C], "bfloat16"), "wn": ("sbuf", [128, C], "bfloat16"),
+    "cap": ("sbuf", [128, C], "bfloat16"), "io1": ("sbuf", [128, C], "float32"),
+    "gr": ("sbuf", [128, SEG], "float32"), "xb": ("sbuf", [128, STEPS], "float32"), "yb": ("sbuf", [128, STEPS], "float32"),
+    "d0": ("sbuf", [128, STEPS], "float32"), "d1": ("sbuf", [128, STEPS], "float32"),
+    "ik": ("sbuf", [128, C], "float32"), "ikt": ("sbuf", [128, C], "float32"), "kk": ("sbuf", [128, C], "float32"),
+    "k0": ("sbuf", [128, NB], "float32"), "k1": ("sbuf", [128, NB], "float32"),
+    "ca": ("sbuf", [128, 16], "float32"), "cb": ("sbuf", [128, 16], "float32"),
+    "mul": ("sbuf", [128, STEPS], HALF),
+    "t1": ("sbuf", [128, C], "float32"), "a1": ("sbuf", [128, C + 4], "float32"),
+    "lt": ("sbuf", [128, C], "float32"),
+    "want": ("sbuf", [128, C], "bfloat16"), "cum": ("sbuf", [128, C + 4], "bfloat16"),
+    "take": ("sbuf", [128, C], "bfloat16"), "tkt": ("sbuf", [128, C], "bfloat16"),
+    "t320": ("sbuf", [128, C], "float32"), "val": ("sbuf", [128, C], "float32"),
+    "own": ("sbuf", [128, NB], "float32"), "o1": ("sbuf", [128, NB], "float32"), "lo": ("sbuf", [128, NB], "float32"),
+    "tt": ("sbuf", [128, NB], "float32"), "mm": ("sbuf", [128, NB], "float32"),
+    "bc": ("sbuf", [128, C], HALF), "mb": ("sbuf", [128, 328], HALF), "stp": ("sbuf", [128, STEPS], HALF),
+    "so": ("sbuf", [128, NB * STEPS], "bfloat16"), "po": ("sbuf", [128, NB], "uint16"),
+    "nm": ("sbuf", [128, C], "float32"), "ns": ("sbuf", [128, C], "float32"), "zo": ("sbuf", [128, NB], "uint16"),
+    "odb": ("sbuf", [128, C], "float32"), "ysb": ("sbuf", [128, C], "float32"),
+}
+for _b in range(4):
+    SCRATCH["win%d" % _b] = ("sbuf", [128, 2 * C], "bfloat16")
+    SCRATCH["xq%d" % _b] = ("sbuf", [128, C], X4)
+    SCRATCH["xs%d" % _b] = ("sbuf", [128, C], "uint8")
+    SCRATCH["p%d" % _b] = ("psum", [128, 512], "float32")
+for _t in range(3):
+    SCRATCH["aq%d" % _t] = ("sbuf", [128, C], X4)
+    SCRATCH["as%d" % _t] = ("sbuf", [128, C], "uint8")
+    SCRATCH["snd%d" % _t] = ("sbuf", [128, NB], "float32")
+    SCRATCH["land%d" % _t] = ("sbuf", [128, NB], "float32")
+for _n in ("pa", "ph", "pb", "pl"):
+    SCRATCH[_n] = ("psum", [128, 512], "float32")
+
+SEMAPHORES = (["v", "s", "lx", "lu", "lv", "lw", "g0", "g1", "g2", "g3", "g4", "one", "zb", "pad", "xb", "dd", "uq", "of",
+               "pk", "pks", "gq", "ma", "mh", "mb", "a0", "a1", "sg0", "sg1", "sg2", "f0", "c0", "c1", "c2", "c3", "c4",
+               "ml", "et", "eq", "dun", "nm", "zo", "zv", "zg", "zq", "xs", "vq", "my", "ys", "od", "out", "left"]
+              + ["%s%d" % (n, b) for n in ("md", "r", "z", "e", "xq") for b in range(4)]
+              + ["%s%d" % (n, t) for n in ("aq", "at", "sn") for t in range(3)])
+
+
+def rank_program(g, core, T, topo):
+    rank = T.rank_of(core)
+    if rank is None:
+        return
+    V, S, PE, SY = g.vector, g.scalar, g.tensor, g.sync
+    queue = {"g": g, "v": V, "s": S, "p": PE, "y": SY}
+    cnt = {n: 0 for n in SEMAPHORES}
+    seen = {}
+
+    def sig(ins, name, n=1):
+        ins.then_inc(T.sem[name], n)
+        cnt[name] += n
+
+    def wait(q, *names):
+        for n in names:
+            if seen.get((q, n), 0) < cnt[n]:
+                queue[q].wait_ge(T.sem[n], cnt[n])
+                seen[(q, n)] = cnt[n]
+
+    def ts(out, in0, s1, op0, s2=None, op1=None, to="v"):
+        if op1 is None:
+            sig(V.tensor_scalar(out, in0, s1, None, op0), to)
+        else:
+            sig(V.tensor_scalar(out, in0, s1, s2, op0, op1), to)
+
+    def tt(out, in0, in1, op, to="v"):
+        sig(V.tensor_tensor(out, in0, in1, op), to)
+
+    def scan(out, d0, d1, init, op0, op1, to="v"):
+        sig(V.tensor_tensor_scan(out, d0, d1, init, op0, op1), to)
+
+    def fill(ap, c, to="v"):
+        sig(V.memset(ap, c), to)
+
+    def quant(q, s, tile, to="v"):
+        sig(V.quantize_mx(q, s, tile), to)
+
+    def act(out, in_, func, to, **kw):
+        sig(S.activation(out, in_, func, **kw), to)
+
+    def iota(out, pattern, base, to):
+        sig(g.iota(out, pattern, base, 0, allow_small_or_imprecise_dtypes=True), to)
+
+    def mx(out, a, b, to=None, start=True, stop=True):
+        ins = PE.matmul_mx(out, a[0], a[1], b[0], b[1], start, stop)
+        if to:
+            sig(ins, to)
+
+    def slot(sg, i0):
+        m, e = divmod(sg, 4)
+        return T.ct[:, 4 * (CB[m] + i0 - Q0[m]) + e:4 * (CB[m] + C - Q0[m]):4]
+
+    def quant_tile(m):
+        quant(T.cq[:, C * m + Q0[m]:C * m + C], T.cs[:, C * m + Q0[m]:C * m + C],
+              T.ct[:, 4 * CB[m]:4 * (CB[m] + C - Q0[m])], "c%d" % m)
+
+    r_col, g_col, r1_col, sc_col = (T.pf[:, j:j + 1] for j in range(4))
+
+    sig(SY.dma_start(T.x0[:], T.x[:]), "lx", 16)
+    sig(S.dma_start(T.ut[:], T.u[:]), "lu", 16)
+    sig(SY.dma_start(T.wq[:].bitcast(dt.uint8), T.wc[:]), "lw", 16)
+    sig(SY.dma_start(T.wp[:], T.ws[:]), "lw", 16)
+    sig(SY.dma_start(T.vt[:], T.v[:]), "lv", 16)
+
+    fill(T.zb[:], 0.0, "zb")
+    fill(T.ones[:], 1.0, "one")
+    fill(T.gr[:], GROW)
+    fill(T.a1[:, 0:1], BIG)
+    sig(g.iota(T.pi[:, 0:1], [[0, 1]], 0, 1), "g0")
+    sig(g.iota(T.oi[:, 0:16], [[1, 2], [16, 8]], 0, 0), "g0")
+    sig(g.iota(T.oi[:, 16:36], [[1, NB]], 0, 0), "g0")
+    iota(T.cmod[:], [[0, NB], [1, 16]], 0, "g1")
+    iota(T.gidx[:], [[1, 8], [0, 16]], 0, "g2")
+    wait("g", "one")
+    sig(g.affine_select(T.ident[:], T.ones[:], [[-1, 128]], OP.is_equal, 0.0, 0, 1), "g3")
+    wait("s", "zb")
+    for m in range(5):
+        act(T.ct[:, 4 * CB[m]:4 * (CB[m] + PAD[m])], T.zb[:, 0:4 * PAD[m]], AF.Copy, "pad")
+    wait("v", "v", "zb")
+    scan(T.xb[:, 0:SEG], T.gr[:], T.zb[:, 0:SEG], B1, OP.mult, OP.add, "xb")
+    scan(T.xb[:, SEG:STEPS], T.gr[:], T.zb[:, 0:SEG], B2, OP.mult, OP.add, "xb")
+    wait("v", "g0")
+    sig(V.tensor_copy(T.off[:], T.oi[:]), "of")
+    ts(T.pi[:, 1:2], T.pi[:, 0:1], 15, OP.bitwise_and)
+    ts(T.pi[:, 2:3], T.pi[:, 0:1], 4, OP.arith_shift_right)
+    for m in range(1, 5):
+        n = max(128, Q0[m])
+        quant(T.cq[:, C * m:C * m + n], T.cs[:, C * m:C * m + n], T.zb[:, 0:4 * n])
+    wait("v", "v")
+    sig(V.tensor_copy(T.pf[:, 0:2], T.pi[:, 1:3]), "v")
+    wait("v", "lu")
+    quant(T.uq[:], T.us[:], T.ut[:], "uq")
+    wait("v", "v", "g1")
+    ts(T.mk[:], T.cmod[:], r_col, OP.not_equal, BIG, OP.mult)
+    wait("v", "uq", "of")
+    sig(V.tensor_copy(T.pq[:].bitcast(dt.uint32), T.uq[:].bitcast(dt.uint32).indirect(T.off[:, 0:16])), "pk")
+    wait("s", "uq", "of")
+    act(T.ps[:], T.us[:].indirect(T.off[:, 0:16]), AF.Copy, "pks")
+    wait("s", "xb")
+    magic = 1.5 * 2.0 ** 23
+    act(T.yb[:], T.xb[:], AF.Identity, "s", bias=magic)
+    wait("s", "s")
+    act(T.d0[:], T.yb[:], AF.Identity, "s", bias=1024.0 * magic, scale=-1024.0)
+    wait("s", "s")
+    act(T.d1[:], T.d0[:], AF.Identity, "dd", bias=1.0, scale=-GROW)
+    wait("v", "lx")
+    quant(T.xq0[:], T.xs0[:], T.x0[:], "xq0")
+    ts(T.r0[:], T.cmod[:], 0.0, OP.is_equal, BIG, OP.mult)
+    wait("v", "g2")
+    for e in range(4):
+        ts(T.gt[:, e:512:4], T.gidx[:], g_col, OP.is_equal)
+
+    def later_constants():
+        ts(r1_col, r_col, 1.0, OP.add)
+        ts(sc_col, r_col, 15.0, OP.is_equal, 2.0 ** -40, OP.max)
+        ts(T.ca[:], T.cmod[:, 0:16], r_col, OP.is_gt, GROW - 1.0, OP.mult)
+        ts(T.cb[:], T.cmod[:, 0:16], r_col, OP.not_equal, 2.0 ** -12, OP.max)
+        ts(T.mul[:, 16:STEPS], T.zb[:, 16:STEPS], GROW, OP.add)
+        ts(T.mb[:, 1:325:323], T.zb[:, 0:2], (MV3 + DRIFT2) * UNIT, OP.add)
+        wait("v", "g4", "dd")
+        ts(T.mb[:, 162:164], T.cv[:, 0:2], UNIT, OP.mult)
+        ts(T.stp[:, SEG - 1:STEPS:SEG], T.cv[:, 2:4], 4096.0 * UNIT, OP.mult)
+        scan(T.ik[:, 0:160], T.d0[:, 1:161], T.d1[:, 0:160], -1.0, OP.add, OP.add)
+        scan(T.ik[:, 160:C], T.d0[:, SEG + 1:SEG + 161], T.d1[:, SEG:SEG + 160], 159.0, OP.add, OP.add)
+        wait("v", "v")
+        ts(T.wa[:], T.cmod[:], r1_col, OP.is_gt)
+        ts(T.wb[:], T.cmod[:], r1_col, OP.is_equal, 2.0 ** 40, OP.mult)
+        tt(T.mul[:, 0:16], T.ca[:], T.cb[:], OP.add)
+        sig(V.transpose(T.ikt[:], T.ik[:]), "v")
+        wait("v", "v")
+        tt(T.wn[:], T.wa[:], T.wb[:], OP.add)
+        tt(T.take[:], T.cum[:, 1:C + 1], T.cum[:, 0:C], OP.subtract)
+        wait("v", "v")
+        scan(T.kk[:, 0:160], T.wn[:, 0:160], T.d1[:, 1:161], 0.0, OP.mult, OP.add)
+        scan(T.kk[:, 160:C], T.wn[:, 0:160], T.d1[:, SEG + 1:SEG + 161], 0.0, OP.mult, OP.add)
+
+    for t, mask_t in enumerate(ROUNDS):
+        peer = T.cores[rank ^ mask_t]
+        rid, pid = topo.addr(peer)[0:2]
+        mask, ne = topo.mask(core, peer), len(topo.engines(core, peer))
+        xq = (T["xq%d" % t][:], T["xs%d" % t][:])
+        aq = (T["aq%d" % t][:], T["as%d" % t][:])
+        snd, land = T["snd%d" % t], T["land%d" % t]
+        last = t == len(ROUNDS) - 1
+
+        wait("g", "xq%d" % t)
+        g.remote_dma(aq[0].bitcast(dt.uint8), xq[0].bitcast(dt.uint8), T.sem["aq%d" % t], T.sem.left, pid, rid, mask)
+        g.remote_dma(aq[1], xq[1], T.sem["aq%d" % t], T.sem.left, pid, rid, mask)
+        cnt["aq%d" % t] += 2 * ne
+        cnt["left"] += 2 * ne
+        if t == 0:
+            iota(T.cv[:, 0:2], [[MV2 - MV1 - DRIFT1, 2]], MV1 + DRIFT1, "g4")
+            iota(T.cv[:, 2:4], [[(LEAVE - REBASE) // 4096, 2]], REBASE // 4096, "g4")
+            iota(T.io1[:], [[1, C]], 1, "g4")
+
+        wait("p", "pk", "pks", "xq%d" % t)
+        mx(T.pa[:, 0:C], (T.pq[:, 0:128], T.ps[:, 0:128]), xq, "ma")
+        mx(T.ph[:, 0:C], (T.pq[:, 0:128], T.ps[:, 0:128]), xq, "mh")
+        mx(T.pb[:, 0:C], (T.pq[:, 128:256], T.ps[:, 128:256]), xq, "mb")
+
+        wait("v", "ma", "v")
+        tt(T.t1[:, 0:HEAD], T.pa[:, 0:HEAD], T.mk[:, 0:HEAD], OP.add, "a0")
+        tt(T.t1[:, HEAD:C], T.pa[:, HEAD:C], T.mk[:, HEAD:C], OP.add)
+        wait("v", "a0")
+        scan(T.a1[:, 1:HEAD + 1], T.r0[:, 0:HEAD], T.t1[:, 0:HEAD], BIG, OP.add, OP.min, "a0")
+        wait("v", "v")
+        scan(T.a1[:, HEAD + 1:C + 1], T.r0[:, HEAD:C], T.t1[:, HEAD:C], BIG, OP.add, OP.min, "a1")
+        if t == 0:
+            quant(T.gq[:], T.gs[:], T.gt[:], "gq")
+        wait("v", "a0", "a1", "pad")
+        wait("s", "a0", "mh", "pad")
+        for k in range(KS):
+            if 16 * k + 16 > HEAD:
+                wait("s", "a1")
+            act(slot(k + 1, 16 * k + 17), T.ph[:, 16 * k + 17:C], AF.Sign, "sg%d" % ((k + 1) // 4),
+                bias=T.a1[:, 16 * k + 16:16 * k + 17], scale=-1.0)
+        wait("s", "sg0")
+        for k in range(3):
+            act(slot(k + 1, 16 * k + 17), slot(k + 1, 16 * k + 17), AF.Relu, "f0", scale=-1.0)
+        for k in range(KS, NB - 1):
+            ts(slot(k + 1, 16 * k + 17), T.pa[:, 16 * k + 17:C], T.a1[:, 16 * k + 16:16 * k + 17], OP.is_gt)
+        tt(slot(0, 0), T.a1[:, 0:C], T.pa[:, 0:C], OP.is_lt)
+        wait("v", "v")
+        quant_tile(4)
+        quant_tile(3)
+        for m in (1, 2):
+            wait("v", "sg%d" % m)
+            whole = T.ct[:, 4 * CB[m]:4 * (CB[m] + C - Q0[m])]
+            ts(whole, whole, 0.0, OP.is_lt)
+            wait("v", "v")
+            quant_tile(m)
+        wait("v", "f0")
+        quant_tile(0)
+        wait("p", "gq")
+        for m in (4, 3, 1, 2, 0):
+            wait("p", "c%d" % m)
+            mx(T.pl[:, 0:C], (T.gq[:], T.gs[:]), (T.cq[:, C * m:C * m + C], T.cs[:, C * m:C * m + C]),
+               "ml" if m == 0 else None, m == 4, m == 0)
+        wait("v", "mb")
+        ts(T.want[:], T.pb[:, 0:C], 0.0, OP.is_gt)
+        wait("v", "ml")
+        sig(V.transpose(T.lt[:], T.pl[:, 0:C]), "v")
+        wait("v", "v")
+        sig(V.tensor_copy(snd[:], T.lt[:, 0:C:16]), "sn%d" % t)
+        wait("g", "sn%d" % t)
+        g.remote_dma(land[:], snd[:], T.sem["at%d" % t], T.sem.left, pid, rid, mask)
+        cnt["at%d" % t] += ne
+        cnt["left"] += ne
+
+        if t == 0:
+            wait("s", "g3")
+            for b in range(4):
+                for e in range(4):
+                    act(T.et[:, 512 * b + e:512 * b + 512:4], T.ident[:], AF.Copy, "et", scale=1.0 if b == e else 0.0)
+            wait("s", "lx")
+            for b in range(4):
+                act(T["win%d" % b][:, 0:C], T.x0[:, b:4 * C:4], AF.Copy, "dun", scale=32.0)
+            fill(T.cap[:], CAP)
+            fill(T.cum[:, 0:1], 0.0)
+            wait("v", "v")
+        scan(T.cum[:, 1:C + 1], T.want[:], T.cap[:], 0.0, OP.add, OP.min)
+        if t == 0:
+            later_constants()
+        else:
+            wait("v", "v")
+            tt(T.take[:], T.cum[:, 1:C + 1], T.cum[:, 0:C], OP.subtract)
+            wait("v", "v")
+        sig(V.transpose(T.tkt[:], T.take[:]), "v")
+        ts(T.t320[:], T.take[:], float(C), OP.mult)
+        wait("v", "v")
+        ts(T.own[:], T.tkt[:, 0:C:16], -1.0, OP.mult, 1.0, OP.add)
+        if t == 0:
+            ts(T.k1[:], T.kk[:, 15:C:16], sc_col, OP.mult, 170.0, OP.add)
+        tt(T.val[:], T.t320[:], T.io1[:], OP.add)
+        wait("v", "v", "sn%d" % t)
+        tt(T.o1[:], snd[:], T.own[:], OP.mult)
+        if t == 0:
+            ts(T.k0[:], T.k1[:], 2.0 ** 12 * UNIT, OP.mult)
+        wait("v", "v")
+        tt(T.lo[:], T.ikt[:, 0:C:16], T.o1[:], OP.subtract)
+        if t == 0:
+            wait("v", "et")
+            quant(T.eq[:], T.es[:], T.et[:], "eq")
+        wait("p", "eq", "aq%d" % t)
+        for b in range(4):
+            mx(T["p%d" % b][:, 0:C], (T.eq[:, 128 * b:128 * b + 128], T.es[:, 128 * b:128 * b + 128]), aq, "md%d" % b)
+            wait("s", "md%d" % b)
+            act(T["win%d" % b][:, C:2 * C], T["p%d" % b][:, 0:C], AF.Copy, "dun", scale=32.0)
+
+        wait("v", "at%d" % t)
+        tt(T.tt[:], land[:], T.tkt[:, 0:C:16], OP.mult)
+        wait("v", "v")
+        tt(T.mm[:], T.lo[:], T.tt[:], OP.subtract)
+        wait("v", "v")
+        ts(T.bc[:], T.mm[:].indirect(T.off[:, 16:36]), UNIT, OP.mult)
+        wait("v", "v")
+        sig(V.transpose(T.mb[:, 2:162], T.bc[:, 0:160]), "v")
+        sig(V.transpose(T.mb[:, 164:324], T.bc[:, 160:C]), "v")
+        wait("v", "v")
+        tt(T.stp[:, 0:161], T.mb[:, 1:162], T.mb[:, 2:163], OP.subtract)
+        tt(T.stp[:, SEG:SEG + 161], T.mb[:, 163:324], T.mb[:, 164:325], OP.subtract)
+        wait("v", "v")
+        for k in range(NB):
+            s0 = 16 * k + (2 if k >= NB // 2 else 0)
+            scan(T.so[:, STEPS * k + s0:STEPS * (k + 1)], T.stp[:, s0:STEPS], T.mul[:, 0:STEPS - s0],
+                 T.k0[:, k:k + 1], OP.add, OP.mult)
+        wait("v", "v")
+        ts(T.po[:], T.so[:, STEPS - 1:NB * STEPS:STEPS], 1.0 / (UNIT * GROW), OP.mult, 160.0, OP.add)
+        wait("v", "v")
+        sig(V.tensor_copy(T.nm[:].indirect(T.po[:]), T.val[:]), "nm")
+        wait("v", "nm")
+        scan(T.ns[:], T.wn[:], T.nm[:], 0.0, OP.mult, OP.add)
+        wait("v", "v")
+        ts(T.zo[:], T.ns[:, 15:C:16], sc_col, OP.mult, -1.0, OP.add, "zo")
+        if last:
+            wait("s", "nm")
+            act(T.odb[:], T.nm[:], AF.Identity, "od", bias=-1.0)
+            wait("y", "od")
+            for k in range(8):
+                sig(SY.dma_start(T.od[k:k + 1, :], T.odb[16 * k:16 * k + 1, :]), "out", 16)
+
+        wait("v", "zo", "dun")
+        wait("s", "zo", "dun")
+        for b in (0, 1):
+            ts(T.zt[:, b:4 * C:4], T["win%d" % b][:].indirect(T.zo[:]), 2.0 ** -5, OP.mult, to="zv")
+            act(T.zt[:, b + 2:4 * C:4], T["win%d" % (b + 2)][:].indirect(T.zo[:]), AF.Copy, "zg", scale=2.0 ** -5)
+        wait("v", "zv", "zg")
+        quant(T.zq[:], T.zs[:], T.zt[:], "zq")
+        wait("s", "zv", "zg")
+        wait("p", "lw", "zq")
+        for b in range(4):
+            act(T.z32[:, C * b:C * b + C], T.zt[:, b:4 * C:4], AF.Copy, "z%d" % b, scale=32.0)
+            mx(T["p%d" % b][:, 0:C], (T.wq[:, 128 * b:128 * b + 128], T.wp[:, 128 * b:128 * b + 128]),
+               (T.zq[:], T.zs[:]), "r%d" % b)
+        if t == 0:
+            wait("v", "lv")
+            quant(T.vq[:], T.vs[:], T.vt[:], "vq")
+
+        for b in range(4):
+            wait("v", "r%d" % b, "z%d" % b)
+            tt(T["win%d" % b][:, 0:C], T["p%d" % b][:, 0:C], T.z32[:, C * b:C * b + C], OP.add, "e%d" % b)
+        for b in (0, 1):
+            wait("s", "e%d" % b)
+            act(T.xn[:, b:4 * C:4], T["win%d" % b][:, 0:C], AF.Copy, "xs", scale=2.0 ** -5)
+        for b in (2, 3):
+            wait("v", "e%d" % b)
+            ts(T.xn[:, b:4 * C:4], T["win%d" % b][:, 0:C], 2.0 ** -5, OP.mult)
+        wait("v", "v", "xs")
+        quant(T["xq%d" % (t + 1)][:], T["xs%d" % (t + 1)][:], T.xn[:], "xq%d" % (t + 1))
+
+    wait("p", "vq", "xq3")
+    mx(T.pa[:, 0:C], (T.vq[:], T.vs[:]), (T.xq3[:], T.xs3[:]), "my")
+    wait("y", "xq3")
+    wait("s", "xq3")
+    sig(SY.dma_start(T.oc[:], T.xq3[:].bitcast(dt.uint8)), "out", 16)
+    for k in range(4):
+        sig(S.dma_start(T.osc[4 * k:4 * k + 4, :], T.xs3[32 * k:32 * k + 4, :]), "out", 16)
+    wait("v", "my")
+    sig(V.tensor_copy(T.ysb[:], T.pa[:, 0:C]), "ys")
+    wait("y", "ys")
+    sig(SY.dma_start(T.y[:], T.ysb[:]), "out", 16)
+    wait("g", *SEMAPHORES)

@@ -2,11 +2,13 @@ import numpy as np
 from concourse.mybir import dt, AluOpType as OP, ActivationFunctionType as AF
 
 C = 320
+H = C // 2
 NB = C // 16
 ROUNDS = [1, 2, 3]
 CAP = 128.0
 BIG = 1e29
 HALF = "float16"
+NAME0 = C + 1
 
 GROW = 1027.0 / 1024.0
 UNIT = 2.0 ** -9
@@ -40,60 +42,38 @@ KS = 11
 HEAD = 64
 
 X4 = "float8_e4m3fn_x4"
-SCRATCH = {
-    "x0": ("sbuf", [128, 4 * C], "bfloat16"), "xn": ("sbuf", [128, 4 * C], "bfloat16"),
-    "ut": ("sbuf", [128, 512], "bfloat16"), "vt": ("sbuf", [128, 512], "bfloat16"),
-    "uq": ("sbuf", [128, 128], X4), "us": ("sbuf", [128, 128], "uint8"),
-    "pq": ("sbuf", [128, 256], X4), "ps": ("sbuf", [128, 256], "uint8"),
-    "vq": ("sbuf", [128, 128], X4), "vs": ("sbuf", [128, 128], "uint8"),
-    "wq": ("sbuf", [128, 512], X4), "wp": ("sbuf", [128, 512], "uint8"),
-    "et": ("sbuf", [128, 2048], "bfloat16"), "eq": ("sbuf", [128, 512], X4), "es": ("sbuf", [128, 512], "uint8"),
-    "gt": ("sbuf", [128, 512], "bfloat16"), "gq": ("sbuf", [128, 128], X4), "gs": ("sbuf", [128, 128], "uint8"),
-    "ct": ("sbuf", [128, 4096], "bfloat16"), "cq": ("sbuf", [128, 5 * C], X4), "cs": ("sbuf", [128, 5 * C], "uint8"),
-    "zt": ("sbuf", [128, 4 * C], "bfloat16"), "zq": ("sbuf", [128, C], X4), "zs": ("sbuf", [128, C], "uint8"),
-    "z32": ("sbuf", [128, 4 * C], "bfloat16"),
-    "zb": ("sbuf", [128, 768], "bfloat16"), "ones": ("sbuf", [128, 128], "bfloat16"),
-    "ident": ("sbuf", [128, 128], "bfloat16"), "gidx": ("sbuf", [128, 128], "bfloat16"),
-    "pi": ("sbuf", [128, 4], "int32"), "pf": ("sbuf", [128, 8], "float32"), "cv": ("sbuf", [128, 4], "float32"),
-    "oi": ("sbuf", [128, 36], "int32"), "off": ("sbuf", [128, 36], "uint16"),
-    "cmod": ("sbuf", [128, C], "bfloat16"), "mk": ("sbuf", [128, C], "bfloat16"), "r0": ("sbuf", [128, C], "bfloat16"),
-    "wa": ("sbuf", [128, C], "bfloat16"), "wb": ("sbuf", [128, C], "bfloat16"), "wn": ("sbuf", [128, C], "bfloat16"),
-    "cap": ("sbuf", [128, C], "bfloat16"), "io1": ("sbuf", [128, C], "float32"),
-    "gr": ("sbuf", [128, SEG], "float32"), "xb": ("sbuf", [128, STEPS], "float32"), "yb": ("sbuf", [128, STEPS], "float32"),
-    "d0": ("sbuf", [128, STEPS], "float32"), "d1": ("sbuf", [128, STEPS], "float32"),
-    "ik": ("sbuf", [128, C], "float32"), "ikt": ("sbuf", [128, C], "float32"), "kk": ("sbuf", [128, C], "float32"),
-    "k0": ("sbuf", [128, NB], "float32"), "k1": ("sbuf", [128, NB], "float32"),
-    "ca": ("sbuf", [128, 16], "float32"), "cb": ("sbuf", [128, 16], "float32"),
-    "mul": ("sbuf", [128, STEPS], HALF),
-    "t1": ("sbuf", [128, C], "float32"), "a1": ("sbuf", [128, C + 4], "float32"),
-    "lt": ("sbuf", [128, C], "float32"),
-    "want": ("sbuf", [128, C], "bfloat16"), "cum": ("sbuf", [128, C + 4], "bfloat16"),
-    "take": ("sbuf", [128, C], "bfloat16"), "tkt": ("sbuf", [128, C], "bfloat16"),
-    "t320": ("sbuf", [128, C], "float32"), "val": ("sbuf", [128, C], "float32"),
-    "own": ("sbuf", [128, NB], "float32"), "o1": ("sbuf", [128, NB], "float32"), "lo": ("sbuf", [128, NB], "float32"),
-    "tt": ("sbuf", [128, NB], "float32"), "mm": ("sbuf", [128, NB], "float32"),
-    "bc": ("sbuf", [128, C], HALF), "mb": ("sbuf", [128, 328], HALF), "stp": ("sbuf", [128, STEPS], HALF),
-    "so": ("sbuf", [128, NB * STEPS], "bfloat16"), "po": ("sbuf", [128, NB], "uint16"),
-    "nm": ("sbuf", [128, C], "float32"), "ns": ("sbuf", [128, C], "float32"), "zo": ("sbuf", [128, NB], "uint16"),
-    "odb": ("sbuf", [128, C], "float32"), "ysb": ("sbuf", [128, C], "float32"),
-}
-for _b in range(4):
-    SCRATCH["win%d" % _b] = ("sbuf", [128, 2 * C], "bfloat16")
-    SCRATCH["xq%d" % _b] = ("sbuf", [128, C], X4)
-    SCRATCH["xs%d" % _b] = ("sbuf", [128, C], "uint8")
-    SCRATCH["p%d" % _b] = ("psum", [128, 512], "float32")
-for _t in range(3):
-    SCRATCH["aq%d" % _t] = ("sbuf", [128, C], X4)
-    SCRATCH["as%d" % _t] = ("sbuf", [128, C], "uint8")
-    SCRATCH["snd%d" % _t] = ("sbuf", [128, NB], "float32")
-    SCRATCH["land%d" % _t] = ("sbuf", [128, NB], "float32")
-for _n in ("pa", "ph", "pb", "pl"):
+SCRATCH = {}
+for _dt, _list in (
+        ("bfloat16", (("x0", 4 * C), ("xn", 4 * C), ("ut", 512), ("vt", 512), ("et", 2048), ("gt", 512), ("ct", 4096),
+                      ("zt", 4 * C), ("z32", 4 * C), ("zb", 768), ("ones", 128), ("ident", 128), ("gidx", 128),
+                      ("cmod", C), ("mk", C), ("r0", C), ("wa", C), ("wb", C), ("wn", C), ("cap", C), ("want", C),
+                      ("cum", C + 4), ("take", C), ("tkt", C), ("t320", C), ("so", NB * STEPS),
+                      ("win0", 2 * C), ("win1", 2 * C), ("win2", 2 * C), ("win3", 2 * C))),
+        ("float32", (("pf", 8), ("cv", 4), ("io1", C), ("gr", SEG), ("xb", STEPS), ("yb", STEPS), ("d0", STEPS),
+                     ("d1", STEPS), ("ik", C), ("ikt", C), ("kk", C), ("k0", NB), ("k1", NB), ("ca", 16), ("cb", 16),
+                     ("t1", C), ("a1", C + 4), ("lt", C), ("val", C), ("own", NB), ("o1", NB), ("lo", NB), ("tt", NB),
+                     ("mm", NB), ("nm", C), ("ns", C), ("odb", C), ("ysb", C), ("snd0", NB), ("snd1", NB), ("snd2", NB),
+                     ("land0", NB), ("land1", NB), ("land2", NB))),
+        (HALF, (("mul", STEPS), ("bc", C), ("mb", 328), ("stp", STEPS))),
+        ("int32", (("pi", 4), ("oi", 36))),
+        ("uint16", (("off", 36), ("po", NB), ("zo", NB)))):
+    for _n, _w in _list:
+        SCRATCH[_n] = ("sbuf", [128, _w], _dt)
+for _q, _s, _w in (("uq", "us", 128), ("pq", "ps", 256), ("vq", "vs", 128), ("wq", "wp", 512), ("eq", "es", 512),
+                   ("gq", "gs", 128), ("cq", "cs", 5 * C), ("zq", "zs", C), ("xq0", "xs0", C), ("xq1", "xs1", C),
+                   ("xq2", "xs2", C), ("xq3", "xs3", C), ("aq0", "as0", C), ("aq1", "as1", C), ("aq2", "as2", C)):
+    SCRATCH[_q] = ("sbuf", [128, _w], X4)
+    SCRATCH[_s] = ("sbuf", [128, _w], "uint8")
+BANKS = ("p0", "p1", "p2", "p3", "pa", "ph", "pb", "pl")
+for _n in BANKS:
     SCRATCH[_n] = ("psum", [128, 512], "float32")
 
-SEMAPHORES = (["v", "s", "lx", "lu", "lv", "lw", "g0", "g1", "g2", "g3", "g4", "one", "zb", "pad", "xb", "dd", "uq", "of",
-               "pk", "pks", "gq", "ma", "mh", "mb", "a0", "a1", "sg0", "sg1", "sg2", "f0", "c0", "c1", "c2", "c3", "c4",
-               "ml", "et", "eq", "dun", "nm", "zo", "zv", "zg", "zq", "xs", "vq", "my", "ys", "od", "out", "left"]
-              + ["%s%d" % (n, b) for n in ("md", "r", "z", "e", "xq") for b in range(4)]
+SEMAPHORES = (["v", "va", "vb", "vc", "vd", "s", "lx", "lu", "lv", "lw", "g0", "g1", "g2", "g3", "g4", "one", "zb", "pad", "xb",
+               "dd", "uq", "of", "pk", "pks", "gq", "ma", "mh", "mb", "a0", "a1", "sg0", "sg1", "sg2", "f0", "c0", "c1",
+               "c2", "c3", "c4", "ml", "et", "eq", "dun", "nm", "zo", "zv", "zg", "zq0", "zq1", "xs", "vq", "my", "ys",
+               "od", "out", "left"]
+              + ["%s%d" % (n, b) for n in ("md", "xq") for b in range(4)]
+              + ["%s%d" % (n, b) for n in ("r", "z", "e") for b in range(8)]
               + ["%s%d" % (n, t) for n in ("aq", "at", "sn") for t in range(3)])
 
 
@@ -153,7 +133,11 @@ def rank_program(g, core, T, topo):
         quant(T.cq[:, C * m + Q0[m]:C * m + C], T.cs[:, C * m + Q0[m]:C * m + C],
               T.ct[:, 4 * CB[m]:4 * (CB[m] + C - Q0[m])], "c%d" % m)
 
+    def elem(tile, b, h):
+        return tile[:, 4 * H * h + b:4 * H * (h + 1):4]
+
     r_col, g_col, r1_col, sc_col = (T.pf[:, j:j + 1] for j in range(4))
+    win = [T["win%d" % b] for b in range(4)]
 
     sig(SY.dma_start(T.x0[:], T.x[:]), "lx", 16)
     sig(S.dma_start(T.ut[:], T.u[:]), "lu", 16)
@@ -210,28 +194,32 @@ def rank_program(g, core, T, topo):
         ts(T.gt[:, e:512:4], T.gidx[:], g_col, OP.is_equal)
 
     def later_constants():
-        ts(r1_col, r_col, 1.0, OP.add)
+        ts(r1_col, r_col, 1.0, OP.add, to="vb")
         ts(sc_col, r_col, 15.0, OP.is_equal, 2.0 ** -40, OP.max)
-        ts(T.ca[:], T.cmod[:, 0:16], r_col, OP.is_gt, GROW - 1.0, OP.mult)
-        ts(T.cb[:], T.cmod[:, 0:16], r_col, OP.not_equal, 2.0 ** -12, OP.max)
-        ts(T.mul[:, 16:STEPS], T.zb[:, 16:STEPS], GROW, OP.add)
-        ts(T.mb[:, 1:325:323], T.zb[:, 0:2], (MV3 + DRIFT2) * UNIT, OP.add)
+        ts(T.ca[:], T.cmod[:, 0:16], r_col, OP.is_gt, GROW - 1.0, OP.mult, "vb")
+        ts(T.cb[:], T.cmod[:, 0:16], r_col, OP.not_equal, 2.0 ** -12, OP.max, "vb")
         wait("v", "g4", "dd")
-        ts(T.mb[:, 162:164], T.cv[:, 0:2], UNIT, OP.mult)
-        ts(T.stp[:, SEG - 1:STEPS:SEG], T.cv[:, 2:4], 4096.0 * UNIT, OP.mult)
-        scan(T.ik[:, 0:160], T.d0[:, 1:161], T.d1[:, 0:160], -1.0, OP.add, OP.add)
-        scan(T.ik[:, 160:C], T.d0[:, SEG + 1:SEG + 161], T.d1[:, SEG:SEG + 160], 159.0, OP.add, OP.add)
-        wait("v", "v")
-        ts(T.wa[:], T.cmod[:], r1_col, OP.is_gt)
-        ts(T.wb[:], T.cmod[:], r1_col, OP.is_equal, 2.0 ** 40, OP.mult)
-        tt(T.mul[:, 0:16], T.ca[:], T.cb[:], OP.add)
+        scan(T.ik[:, 0:H], T.d0[:, 1:H + 1], T.d1[:, 0:H], -1.0, OP.add, OP.add, "vc")
+        scan(T.ik[:, H:C], T.d0[:, SEG + 1:SEG + H + 1], T.d1[:, SEG:SEG + H], H - 1.0, OP.add, OP.add, "vc")
+        wait("v", "vb")
+        ts(T.wa[:], T.cmod[:], r1_col, OP.is_gt, to="vb")
+        ts(T.wb[:], T.cmod[:], r1_col, OP.is_equal, 2.0 ** 40, OP.mult, "vb")
+        wait("v", "vc")
         sig(V.transpose(T.ikt[:], T.ik[:]), "v")
-        wait("v", "v")
-        tt(T.wn[:], T.wa[:], T.wb[:], OP.add)
-        tt(T.take[:], T.cum[:, 1:C + 1], T.cum[:, 0:C], OP.subtract)
-        wait("v", "v")
-        scan(T.kk[:, 0:160], T.wn[:, 0:160], T.d1[:, 1:161], 0.0, OP.mult, OP.add)
-        scan(T.kk[:, 160:C], T.wn[:, 0:160], T.d1[:, SEG + 1:SEG + 161], 0.0, OP.mult, OP.add)
+        wait("v", "vb")
+        tt(T.wn[:], T.wa[:], T.wb[:], OP.add, "vb")
+        tt(T.mul[:, 0:16], T.ca[:], T.cb[:], OP.add)
+        ts(T.mul[:, 16:STEPS], T.zb[:, 16:STEPS], GROW, OP.add)
+        wait("v", "vb")
+        scan(T.kk[:, 0:H], T.wn[:, 0:H], T.d1[:, 1:H + 1], 0.0, OP.mult, OP.add, "vb")
+        scan(T.kk[:, H:C], T.wn[:, 0:H], T.d1[:, SEG + 1:SEG + H + 1], 0.0, OP.mult, OP.add, "vb")
+        ts(T.mb[:, 1:325:323], T.zb[:, 0:2], (MV3 + DRIFT2) * UNIT, OP.add)
+        ts(T.mb[:, 162:164], T.cv[:, 0:2], UNIT, OP.mult)
+        wait("v", "vb", "v")
+        ts(T.k1[:], T.kk[:, 15:C:16], sc_col, OP.mult, 170.0, OP.add, "vb")
+        ts(T.stp[:, SEG - 1:STEPS:SEG], T.cv[:, 2:4], 4096.0 * UNIT, OP.mult)
+        wait("v", "vb")
+        ts(T.k0[:], T.k1[:], 2.0 ** 12 * UNIT, OP.mult)
 
     for t, mask_t in enumerate(ROUNDS):
         peer = T.cores[rank ^ mask_t]
@@ -250,7 +238,7 @@ def rank_program(g, core, T, topo):
         if t == 0:
             iota(T.cv[:, 0:2], [[MV2 - MV1 - DRIFT1, 2]], MV1 + DRIFT1, "g4")
             iota(T.cv[:, 2:4], [[(LEAVE - REBASE) // 4096, 2]], REBASE // 4096, "g4")
-            iota(T.io1[:], [[1, C]], 1, "g4")
+            iota(T.io1[:], [[1, C]], NAME0, "g4")
 
         wait("p", "pk", "pks", "xq%d" % t)
         mx(T.pa[:, 0:C], (T.pq[:, 0:128], T.ps[:, 0:128]), xq, "ma")
@@ -266,6 +254,8 @@ def rank_program(g, core, T, topo):
         scan(T.a1[:, HEAD + 1:C + 1], T.r0[:, HEAD:C], T.t1[:, HEAD:C], BIG, OP.add, OP.min, "a1")
         if t == 0:
             quant(T.gq[:], T.gs[:], T.gt[:], "gq")
+            fill(T.cap[:], CAP, "vd")
+            fill(T.cum[:, 0:1], 0.0, "vd")
         wait("v", "a0", "a1", "pad")
         wait("s", "a0", "mh", "pad")
         for k in range(KS):
@@ -276,30 +266,40 @@ def rank_program(g, core, T, topo):
         wait("s", "sg0")
         for k in range(3):
             act(slot(k + 1, 16 * k + 17), slot(k + 1, 16 * k + 17), AF.Relu, "f0", scale=-1.0)
-        for k in range(KS, NB - 1):
-            ts(slot(k + 1, 16 * k + 17), T.pa[:, 16 * k + 17:C], T.a1[:, 16 * k + 16:16 * k + 17], OP.is_gt)
-        tt(slot(0, 0), T.a1[:, 0:C], T.pa[:, 0:C], OP.is_lt)
-        wait("v", "v")
+        for k in reversed(range(KS, NB - 1)):
+            ts(slot(k + 1, 16 * k + 17), T.pa[:, 16 * k + 17:C], T.a1[:, 16 * k + 16:16 * k + 17], OP.is_gt,
+               to="va" if k >= 15 else "vb")
+        tt(slot(0, 0), T.a1[:, 0:C], T.pa[:, 0:C], OP.is_lt, "vc")
+        wait("v", "va")
         quant_tile(4)
+        wait("v", "vb")
         quant_tile(3)
         for m in (1, 2):
             wait("v", "sg%d" % m)
             whole = T.ct[:, 4 * CB[m]:4 * (CB[m] + C - Q0[m])]
-            ts(whole, whole, 0.0, OP.is_lt)
-            wait("v", "v")
+            ts(whole, whole, 0.0, OP.is_lt, to="va")
+            if m == 1:
+                wait("v", "mb")
+                ts(T.want[:], T.pb[:, 0:C], 0.0, OP.is_gt, to="vd")
+            else:
+                wait("v", "vd")
+                scan(T.cum[:, 1:C + 1], T.want[:], T.cap[:], 0.0, OP.add, OP.min, "vd")
+            wait("v", "va")
             quant_tile(m)
-        wait("v", "f0")
+        wait("v", "f0", "vc")
         quant_tile(0)
         wait("p", "gq")
         for m in (4, 3, 1, 2, 0):
             wait("p", "c%d" % m)
             mx(T.pl[:, 0:C], (T.gq[:], T.gs[:]), (T.cq[:, C * m:C * m + C], T.cs[:, C * m:C * m + C]),
                "ml" if m == 0 else None, m == 4, m == 0)
-        wait("v", "mb")
-        ts(T.want[:], T.pb[:, 0:C], 0.0, OP.is_gt)
+        wait("v", "vd")
+        scan(T.take[:], T.cum[:, 1:C + 1], T.cum[:, 0:C], 0.0, OP.max, OP.subtract, "vd")
         wait("v", "ml")
-        sig(V.transpose(T.lt[:], T.pl[:, 0:C]), "v")
-        wait("v", "v")
+        sig(V.transpose(T.lt[:], T.pl[:, 0:C]), "va")
+        wait("v", "vd")
+        sig(V.transpose(T.tkt[:], T.take[:]), "vd")
+        wait("v", "va")
         sig(V.tensor_copy(snd[:], T.lt[:, 0:C:16]), "sn%d" % t)
         wait("g", "sn%d" % t)
         g.remote_dma(land[:], snd[:], T.sem["at%d" % t], T.sem.left, pid, rid, mask)
@@ -313,97 +313,105 @@ def rank_program(g, core, T, topo):
                     act(T.et[:, 512 * b + e:512 * b + 512:4], T.ident[:], AF.Copy, "et", scale=1.0 if b == e else 0.0)
             wait("s", "lx")
             for b in range(4):
-                act(T["win%d" % b][:, 0:C], T.x0[:, b:4 * C:4], AF.Copy, "dun", scale=32.0)
-            fill(T.cap[:], CAP)
-            fill(T.cum[:, 0:1], 0.0)
-            wait("v", "v")
-        scan(T.cum[:, 1:C + 1], T.want[:], T.cap[:], 0.0, OP.add, OP.min)
-        if t == 0:
+                act(win[b][:, 0:C], T.x0[:, b:4 * C:4], AF.Copy, "dun", scale=32.0)
             later_constants()
-        else:
-            wait("v", "v")
-            tt(T.take[:], T.cum[:, 1:C + 1], T.cum[:, 0:C], OP.subtract)
-            wait("v", "v")
-        sig(V.transpose(T.tkt[:], T.take[:]), "v")
-        ts(T.t320[:], T.take[:], float(C), OP.mult)
-        wait("v", "v")
-        ts(T.own[:], T.tkt[:, 0:C:16], -1.0, OP.mult, 1.0, OP.add)
-        if t == 0:
-            ts(T.k1[:], T.kk[:, 15:C:16], sc_col, OP.mult, 170.0, OP.add)
-        tt(T.val[:], T.t320[:], T.io1[:], OP.add)
-        wait("v", "v", "sn%d" % t)
-        tt(T.o1[:], snd[:], T.own[:], OP.mult)
-        if t == 0:
-            ts(T.k0[:], T.k1[:], 2.0 ** 12 * UNIT, OP.mult)
-        wait("v", "v")
+        wait("v", "vd")
+        ts(T.own[:], T.tkt[:, 0:C:16], -1.0, OP.mult, 1.0, OP.add, "va")
+        ts(T.t320[:], T.take[:], float(C), OP.mult, to="vd")
+        wait("v", "va", "sn%d" % t)
+        tt(T.o1[:], snd[:], T.own[:], OP.mult, "va")
+        wait("v", "vd")
+        scan(T.val[:], T.t320[:], T.io1[:], 2.0 * C, OP.min, OP.add, "vd")
+        wait("v", "va", "v")
         tt(T.lo[:], T.ikt[:, 0:C:16], T.o1[:], OP.subtract)
         if t == 0:
             wait("v", "et")
             quant(T.eq[:], T.es[:], T.et[:], "eq")
         wait("p", "eq", "aq%d" % t)
         for b in range(4):
-            mx(T["p%d" % b][:, 0:C], (T.eq[:, 128 * b:128 * b + 128], T.es[:, 128 * b:128 * b + 128]), aq, "md%d" % b)
+            mx(T[BANKS[b]][:, 0:C], (T.eq[:, 128 * b:128 * b + 128], T.es[:, 128 * b:128 * b + 128]), aq, "md%d" % b)
             wait("s", "md%d" % b)
-            act(T["win%d" % b][:, C:2 * C], T["p%d" % b][:, 0:C], AF.Copy, "dun", scale=32.0)
+            act(win[b][:, C:2 * C], T[BANKS[b]][:, 0:C], AF.Copy, "dun", scale=32.0)
 
         wait("v", "at%d" % t)
         tt(T.tt[:], land[:], T.tkt[:, 0:C:16], OP.mult)
         wait("v", "v")
         tt(T.mm[:], T.lo[:], T.tt[:], OP.subtract)
         wait("v", "v")
-        ts(T.bc[:], T.mm[:].indirect(T.off[:, 16:36]), UNIT, OP.mult)
-        wait("v", "v")
-        sig(V.transpose(T.mb[:, 2:162], T.bc[:, 0:160]), "v")
-        sig(V.transpose(T.mb[:, 164:324], T.bc[:, 160:C]), "v")
-        wait("v", "v")
-        tt(T.stp[:, 0:161], T.mb[:, 1:162], T.mb[:, 2:163], OP.subtract)
-        tt(T.stp[:, SEG:SEG + 161], T.mb[:, 163:324], T.mb[:, 164:325], OP.subtract)
-        wait("v", "v")
-        for k in range(NB):
+        ts(T.bc[:, H:C], T.mm[:].indirect(T.off[:, 26:36]), UNIT, OP.mult, to="va")
+        ts(T.bc[:, 0:H], T.mm[:].indirect(T.off[:, 16:26]), UNIT, OP.mult, to="vb")
+        wait("v", "va")
+        sig(V.transpose(T.mb[:, 164:324], T.bc[:, H:C]), "va")
+        wait("v", "vb")
+        sig(V.transpose(T.mb[:, 2:162], T.bc[:, 0:H]), "vb")
+        wait("v", "va")
+        tt(T.stp[:, SEG:SEG + 161], T.mb[:, 163:324], T.mb[:, 164:325], OP.subtract, "va")
+        wait("v", "vb")
+        tt(T.stp[:, 0:161], T.mb[:, 1:162], T.mb[:, 2:163], OP.subtract, "vb")
+
+        def order_scan(k, to):
             s0 = 16 * k + (2 if k >= NB // 2 else 0)
             scan(T.so[:, STEPS * k + s0:STEPS * (k + 1)], T.stp[:, s0:STEPS], T.mul[:, 0:STEPS - s0],
-                 T.k0[:, k:k + 1], OP.add, OP.mult)
-        wait("v", "v")
-        ts(T.po[:], T.so[:, STEPS - 1:NB * STEPS:STEPS], 1.0 / (UNIT * GROW), OP.mult, 160.0, OP.add)
-        wait("v", "v")
-        sig(V.tensor_copy(T.nm[:].indirect(T.po[:]), T.val[:]), "nm")
+                 T.k0[:, k:k + 1], OP.add, OP.mult, to)
+
+        def places(a, b):
+            ts(T.po[:, a:b], T.so[:, STEPS * (a + 1) - 1:STEPS * b:STEPS], 1.0 / (UNIT * GROW), OP.mult, 160.0, OP.add, "vc")
+
+        wait("v", "va")
+        for k in range(10, NB):
+            order_scan(k, "va")
+        wait("v", "vb")
+        for k in range(0, 5):
+            order_scan(k, "vb")
+        wait("v", "va")
+        places(10, NB)
+        for k in range(5, 10):
+            order_scan(k, "vb")
+        wait("v", "vc", "vd")
+        sig(V.tensor_copy(T.nm[:].indirect(T.po[:, 10:NB]), T.val[:, H:C]), "nm")
+        wait("v", "vb")
+        places(0, 10)
+        wait("v", "vc", "nm")
+        sig(V.tensor_copy(T.nm[:].indirect(T.po[:, 0:10]), T.val[:, 0:H]), "nm")
         wait("v", "nm")
         scan(T.ns[:], T.wn[:], T.nm[:], 0.0, OP.mult, OP.add)
         wait("v", "v")
-        ts(T.zo[:], T.ns[:, 15:C:16], sc_col, OP.mult, -1.0, OP.add, "zo")
+        ts(T.zo[:], T.ns[:, 15:C:16], sc_col, OP.mult, -float(NAME0), OP.add, "zo")
         if last:
             wait("s", "nm")
-            act(T.odb[:], T.nm[:], AF.Identity, "od", bias=-1.0)
+            act(T.odb[:], T.nm[:], AF.Identity, "od", bias=-float(NAME0))
             wait("y", "od")
             for k in range(8):
                 sig(SY.dma_start(T.od[k:k + 1, :], T.odb[16 * k:16 * k + 1, :]), "out", 16)
 
         wait("v", "zo", "dun")
         wait("s", "zo", "dun")
-        for b in (0, 1):
-            ts(T.zt[:, b:4 * C:4], T["win%d" % b][:].indirect(T.zo[:]), 2.0 ** -5, OP.mult, to="zv")
-            act(T.zt[:, b + 2:4 * C:4], T["win%d" % (b + 2)][:].indirect(T.zo[:]), AF.Copy, "zg", scale=2.0 ** -5)
-        wait("v", "zv", "zg")
-        quant(T.zq[:], T.zs[:], T.zt[:], "zq")
-        wait("s", "zv", "zg")
-        wait("p", "lw", "zq")
         for b in range(4):
-            act(T.z32[:, C * b:C * b + C], T.zt[:, b:4 * C:4], AF.Copy, "z%d" % b, scale=32.0)
-            mx(T["p%d" % b][:, 0:C], (T.wq[:, 128 * b:128 * b + 128], T.wp[:, 128 * b:128 * b + 128]),
-               (T.zq[:], T.zs[:]), "r%d" % b)
+            ts(elem(T.zt, b, 0), win[b][:].indirect(T.zo[:, 0:10]), 2.0 ** -5, OP.mult, to="zv")
+            act(elem(T.zt, b, 1), win[b][:].indirect(T.zo[:, 10:NB]), AF.Copy, "zg", scale=2.0 ** -5)
+        wait("p", "lw")
+        for h, made in enumerate(("zv", "zg")):
+            wait("v", made)
+            quant(T.zq[:, H * h:H * h + H], T.zs[:, H * h:H * h + H], T.zt[:, 4 * H * h:4 * H * (h + 1)], "zq%d" % h)
+            wait("s", made)
+            wait("p", "zq%d" % h)
+            for b in range(4):
+                j = 4 * h + b
+                act(T.z32[:, H * j:H * j + H], elem(T.zt, b, h), AF.Copy, "z%d" % j, scale=32.0)
+                mx(T[BANKS[j]][:, 0:H], (T.wq[:, 128 * b:128 * b + 128], T.wp[:, 128 * b:128 * b + 128]),
+                   (T.zq[:, H * h:H * h + H], T.zs[:, H * h:H * h + H]), "r%d" % j)
         if t == 0:
             wait("v", "lv")
             quant(T.vq[:], T.vs[:], T.vt[:], "vq")
-
+        for j in range(8):
+            h, b = divmod(j, 4)
+            wait("v", "r%d" % j, "z%d" % j)
+            tt(win[b][:, H * h:H * h + H], T[BANKS[j]][:, 0:H], T.z32[:, H * j:H * j + H], OP.add, "e%d" % j)
         for b in range(4):
-            wait("v", "r%d" % b, "z%d" % b)
-            tt(T["win%d" % b][:, 0:C], T["p%d" % b][:, 0:C], T.z32[:, C * b:C * b + C], OP.add, "e%d" % b)
-        for b in (0, 1):
             wait("s", "e%d" % b)
-            act(T.xn[:, b:4 * C:4], T["win%d" % b][:, 0:C], AF.Copy, "xs", scale=2.0 ** -5)
-        for b in (2, 3):
-            wait("v", "e%d" % b)
-            ts(T.xn[:, b:4 * C:4], T["win%d" % b][:, 0:C], 2.0 ** -5, OP.mult)
+            act(elem(T.xn, b, 0), win[b][:, 0:H], AF.Copy, "xs", scale=2.0 ** -5)
+            wait("v", "e%d" % (4 + b))
+            ts(elem(T.xn, b, 1), win[b][:, H:C], 2.0 ** -5, OP.mult)
         wait("v", "v", "xs")
         quant(T["xq%d" % (t + 1)][:], T["xs%d" % (t + 1)][:], T.xn[:], "xq%d" % (t + 1))
 

@@ -5,73 +5,72 @@ C = 320
 H = C // 2
 NB = C // 16
 ROUNDS = [1, 2, 3]
-CAP = 128.0
-BIG = 1e29
-HALF = "float16"
+CAP = 128
 NAME0 = C + 1
+HALF = "float16"
 
-GROW = 1027.0 / 1024.0
+GROW = 513.0 / 512.0
 UNIT = 2.0 ** -9
-B1, B2 = 8283.0, 8288.0
-MV1, MV2, MV3 = 239, 260, 334
-SEG = 162
-STEPS = 2 * SEG
+W0 = 8522306.0
+KAPPA0 = 1152
+STEPS = C + 2
+TINY = 2.0 ** -30
 
 
-def _bases(b):
+def _ends():
     f = np.float32
-    x, out = f(b), []
-    for _ in range(SEG):
+    x, w = f(W0), []
+    for _ in range(STEPS):
         x = f(f(GROW) * x)
-        out.append(int(np.rint(x)))
-    drift = 0
-    for j in range(1, SEG):
-        drift += 1027 * out[j - 1] - 1024 * out[j]
-    return out, drift
+        w.append(int(x))
+    b1 = int(f(f(513 * int(np.rint(w[C] / 512.0))) + f(257.5)))
+    behind = (b1 - 1 + H) % 8192
+    return behind + w[C + 1] - b1 - KAPPA0, -(b1 - 1 - behind + H)
 
 
-N1, DRIFT1 = _bases(B1)
-N2, DRIFT2 = _bases(B2)
-REBASE = 1024 * N2[0] - MV2 - 1027 * N1[-1] + MV1
-LEAVE = -(1027 * N2[-1] + 171 - MV3 + 160)
+LAST, LEAVE = _ends()
 
-Q0 = [0, 64, 128, 192, 192]
-CB = [0, 320, 576, 768, 896]
-PAD = [52, 52, 52, 52, 116]
-KS = 11
-HEAD = 64
+B0 = 6
+OVER = 32
+J = [0] * (2 * B0) + [32 * (c // 2) - OVER for c in range(2 * B0, NB)]
+LEN = [32 * (c // 2) + 32 - J[c] for c in range(NB)]
+AT = [sum(LEN[:c]) + c for c in range(NB + 1)]
+SW = 32 * 9 - OVER + 2
+NS = NB - 2 * B0
+UP = 32 * B0
 
 X4 = "float8_e4m3fn_x4"
 SCRATCH = {}
 for _dt, _list in (
-        ("bfloat16", (("x0", 4 * C), ("xn", 4 * C), ("ut", 512), ("vt", 512), ("et", 2048), ("gt", 512), ("ct", 4096),
-                      ("zt", 4 * C), ("z32", 4 * C), ("zb", 768), ("ones", 128), ("ident", 128), ("gidx", 128),
-                      ("cmod", C), ("mk", C), ("r0", C), ("wa", C), ("wb", C), ("wn", C), ("cap", C), ("want", C),
-                      ("cum", C + 4), ("take", C), ("tkt", C), ("t320", C), ("so", NB * STEPS),
+        ("bfloat16", (("x0", 4 * C), ("xn", 4 * C), ("ut", 512), ("vt", 512), ("et", 2048),
+                      ("zt", 4 * C), ("z32", 4 * C), ("zb", 336), ("ones", 512), ("cmod", C), ("c32", 34), ("p33", 34),
+                      ("w16", 48), ("wn", C), ("cmp", AT[NB] + 1), ("hold", AT[NB] + 1), ("cnt", AT[NB] + 1),
+                      ("sg", NS * SW), ("sr", NS * SW), ("so", NB * STEPS),
                       ("win0", 2 * C), ("win1", 2 * C), ("win2", 2 * C), ("win3", 2 * C))),
-        ("float32", (("pf", 8), ("cv", 4), ("io1", C), ("gr", SEG), ("xb", STEPS), ("yb", STEPS), ("d0", STEPS),
-                     ("d1", STEPS), ("ik", C), ("ikt", C), ("kk", C), ("k0", NB), ("k1", NB), ("ca", 16), ("cb", 16),
-                     ("t1", C), ("a1", C + 4), ("lt", C), ("val", C), ("own", NB), ("o1", NB), ("lo", NB), ("tt", NB),
-                     ("mm", NB), ("nm", C), ("ns", C), ("odb", C), ("ysb", C), ("snd0", NB), ("snd1", NB), ("snd2", NB),
+        ("float32", (("pf", 8), ("wb", STEPS), ("yb", STEPS), ("nb", STEPS), ("b1", STEPS), ("kr", C), ("krt", C),
+                     ("kk", C), ("k0", NB), ("ca", 16), ("cb", 16), ("inc", 32), ("ends", 32), ("ew", 32), ("jr", NS),
+                     ("st", NS), ("acc", 32), ("tc", C), ("lo", NB), ("hi", NB), ("mid", NB), ("nm", C), ("ns", C),
+                     ("odb", C), ("ysb", C), ("io1", C), ("snd0", 32), ("snd1", 32), ("snd2", 32),
                      ("land0", NB), ("land1", NB), ("land2", NB))),
-        (HALF, (("mul", STEPS), ("bc", C), ("mb", 328), ("stp", STEPS))),
-        ("int32", (("pi", 4), ("oi", 36))),
-        ("uint16", (("off", 36), ("po", NB), ("zo", NB)))):
+        (HALF, (("gr", STEPS), ("mul", STEPS), ("rp", C), ("rz", C), ("bc", C), ("mb", C + 2), ("stp", STEPS),
+                ("cap", C), ("want", C), ("cum", C + 2), ("take", C), ("tkt", C), ("val", C), ("iou", C))),
+        ("int32", (("pi", 4), ("oi", 32))),
+        ("uint16", (("off", 32), ("rep", NB), ("eo", 2), ("po", NB), ("zo", NB)))):
     for _n, _w in _list:
         SCRATCH[_n] = ("sbuf", [128, _w], _dt)
-for _q, _s, _w in (("uq", "us", 128), ("pq", "ps", 256), ("vq", "vs", 128), ("wq", "wp", 512), ("eq", "es", 512),
-                   ("gq", "gs", 128), ("cq", "cs", 5 * C), ("zq", "zs", C), ("xq0", "xs0", C), ("xq1", "xs1", C),
+for _q, _s, _w in (("uq", "us", 128), ("pq", "ps", 512), ("vq", "vs", 128), ("wq", "wp", 512), ("eq", "es", 512),
+                   ("zq", "zs", C), ("xq0", "xs0", C), ("xq1", "xs1", C),
                    ("xq2", "xs2", C), ("xq3", "xs3", C), ("aq0", "as0", C), ("aq1", "as1", C), ("aq2", "as2", C)):
     SCRATCH[_q] = ("sbuf", [128, _w], X4)
     SCRATCH[_s] = ("sbuf", [128, _w], "uint8")
-BANKS = ("p0", "p1", "p2", "p3", "pa", "ph", "pb", "pl")
+BANKS = ["p%d" % _b for _b in range(8)]
 for _n in BANKS:
     SCRATCH[_n] = ("psum", [128, 512], "float32")
 
-SEMAPHORES = (["v", "va", "vb", "vc", "vd", "s", "lx", "lu", "lv", "lw", "g0", "g1", "g2", "g3", "g4", "one", "zb", "pad", "xb",
-               "dd", "uq", "of", "pk", "pks", "gq", "ma", "mh", "mb", "a0", "a1", "sg0", "sg1", "sg2", "f0", "c0", "c1",
-               "c2", "c3", "c4", "ml", "et", "eq", "dun", "nm", "zo", "zv", "zg", "zq0", "zq1", "xs", "vq", "my", "ys",
-               "od", "out", "left"]
+SEMAPHORES = (["v", "va", "vb", "vc", "vd", "ve", "s", "sa", "sb", "sr", "lx", "lu", "lv", "lw", "g0", "g1", "g2", "g3",
+               "one", "hd", "hp", "p33", "wb", "b1", "w16", "wn", "st", "uq", "of", "pk", "pks", "mu", "ml", "mes", "mos",
+               "mev", "mov", "mw", "tu", "tl", "et", "eq", "dun", "nm", "zo0", "zo1", "zv", "zg", "zq0", "zq1", "xs",
+               "vq", "my", "ys", "od", "out", "left"]
               + ["%s%d" % (n, b) for n in ("md", "xq") for b in range(4)]
               + ["%s%d" % (n, b) for n in ("r", "z", "e") for b in range(8)]
               + ["%s%d" % (n, t) for n in ("aq", "at", "sn") for t in range(3)])
@@ -114,278 +113,297 @@ def rank_program(g, core, T, topo):
     def quant(q, s, tile, to="v"):
         sig(V.quantize_mx(q, s, tile), to)
 
+    def turn(out, in_, to="v"):
+        sig(V.transpose(out, in_), to)
+
     def act(out, in_, func, to, **kw):
         sig(S.activation(out, in_, func, **kw), to)
 
     def iota(out, pattern, base, to):
         sig(g.iota(out, pattern, base, 0, allow_small_or_imprecise_dtypes=True), to)
 
-    def mx(out, a, b, to=None, start=True, stop=True):
-        ins = PE.matmul_mx(out, a[0], a[1], b[0], b[1], start, stop)
-        if to:
-            sig(ins, to)
+    def mx(out, a, b, to):
+        sig(PE.matmul_mx(out, a[0], a[1], b[0], b[1], True, True), to)
 
-    def slot(sg, i0):
-        m, e = divmod(sg, 4)
-        return T.ct[:, 4 * (CB[m] + i0 - Q0[m]) + e:4 * (CB[m] + C - Q0[m]):4]
-
-    def quant_tile(m):
-        quant(T.cq[:, C * m + Q0[m]:C * m + C], T.cs[:, C * m + Q0[m]:C * m + C],
-              T.ct[:, 4 * CB[m]:4 * (CB[m] + C - Q0[m])], "c%d" % m)
+    def cols(q, a, b):
+        return (q[0][:, a:b], q[1][:, a:b])
 
     def elem(tile, b, h):
         return tile[:, 4 * H * h + b:4 * H * (h + 1):4]
 
-    r_col, g_col, r1_col, sc_col = (T.pf[:, j:j + 1] for j in range(4))
+    r_col, x_col, r1_col, sc_col, sc8_col, scu_col = (T.pf[:, j:j + 1] for j in range(6))
     win = [T["win%d" % b] for b in range(4)]
+    bank = [T[n] for n in BANKS]
+    pq, eq, wq = (T.pq, T.ps), (T.eq, T.es), (T.wq, T.wp)
 
     sig(SY.dma_start(T.x0[:], T.x[:]), "lx", 16)
     sig(S.dma_start(T.ut[:], T.u[:]), "lu", 16)
+    wait("y", "lx")
     sig(SY.dma_start(T.wq[:].bitcast(dt.uint8), T.wc[:]), "lw", 16)
     sig(SY.dma_start(T.wp[:], T.ws[:]), "lw", 16)
     sig(SY.dma_start(T.vt[:], T.v[:]), "lv", 16)
 
-    fill(T.zb[:], 0.0, "zb")
-    fill(T.ones[:], 1.0, "one")
-    fill(T.gr[:], GROW)
-    fill(T.a1[:, 0:1], BIG)
     sig(g.iota(T.pi[:, 0:1], [[0, 1]], 0, 1), "g0")
-    sig(g.iota(T.oi[:, 0:16], [[1, 2], [16, 8]], 0, 0), "g0")
-    sig(g.iota(T.oi[:, 16:36], [[1, NB]], 0, 0), "g0")
-    iota(T.cmod[:], [[0, NB], [1, 16]], 0, "g1")
-    iota(T.gidx[:], [[1, 8], [0, 16]], 0, "g2")
-    wait("g", "one")
-    sig(g.affine_select(T.ident[:], T.ones[:], [[-1, 128]], OP.is_equal, 0.0, 0, 1), "g3")
-    wait("s", "zb")
-    for m in range(5):
-        act(T.ct[:, 4 * CB[m]:4 * (CB[m] + PAD[m])], T.zb[:, 0:4 * PAD[m]], AF.Copy, "pad")
-    wait("v", "v", "zb")
-    scan(T.xb[:, 0:SEG], T.gr[:], T.zb[:, 0:SEG], B1, OP.mult, OP.add, "xb")
-    scan(T.xb[:, SEG:STEPS], T.gr[:], T.zb[:, 0:SEG], B2, OP.mult, OP.add, "xb")
+    iota(T.c32[:], [[1, 34]], 0, "g0")
+    for j, (pattern, base) in enumerate((([[16, 8]], 0), ([[32, 4], [0, 2]], 0), ([[32, 4], [0, 2]], 16), ([[16, 8]], 1))):
+        sig(g.iota(T.oi[:, 8 * j:8 * j + 8], pattern, base, 0), "g1")
+    iota(T.inc[:, 0:2 * B0], [[32, B0], [0, 2]], 33, "g2")
+    iota(T.jr[:], [[-32, NS // 2], [0, 2]], 1 + KAPPA0 - J[2 * B0], "g2")
+    fill(T.zb[:], 0.0)
+    fill(T.gr[:], GROW)
+    fill(T.ones[:], 1.0, "one")
+    fill(T.hold[:], 1.0, "hd")
+    wait("v", "v")
+    scan(T.wb[:], T.gr[:], T.zb[:, 0:STEPS], W0, OP.mult, OP.add, "wb")
     wait("v", "g0")
-    sig(V.tensor_copy(T.off[:], T.oi[:]), "of")
     ts(T.pi[:, 1:2], T.pi[:, 0:1], 15, OP.bitwise_and)
-    ts(T.pi[:, 2:3], T.pi[:, 0:1], 4, OP.arith_shift_right)
-    for m in range(1, 5):
-        n = max(128, Q0[m])
-        quant(T.cq[:, C * m:C * m + n], T.cs[:, C * m:C * m + n], T.zb[:, 0:4 * n])
+    ts(T.pi[:, 2:3], T.pi[:, 0:1], 31, OP.bitwise_and)
+    fill(T.inc[:, 2 * B0:NB], float(LEN[NB - 1] + 1), "va")
+    fill(T.inc[:, NB:32], 0.0, "va")
     wait("v", "v")
     sig(V.tensor_copy(T.pf[:, 0:2], T.pi[:, 1:3]), "v")
+    wait("v", "g1")
+    sig(V.tensor_copy(T.off[:], T.oi[:]), "of")
+    wait("v", "v")
+    ts(T.p33[:, 0:32], T.c32[:, 0:32], x_col, OP.is_equal, 1.0 / TINY, OP.mult, "p33")
+    fill(T.p33[:, 32:34], -1.0, "p33")
+    ts(r1_col, r_col, 1.0, OP.add, to="vb")
+    ts(sc_col, r_col, 15.0, OP.is_equal, 2.0 ** -40, OP.max, "vb")
+    ts(T.rep[:], T.zb[:, 0:NB], r_col, OP.add, to="w16")
     wait("v", "lu")
     quant(T.uq[:], T.us[:], T.ut[:], "uq")
-    wait("v", "v", "g1")
-    ts(T.mk[:], T.cmod[:], r_col, OP.not_equal, BIG, OP.mult)
+    wait("v", "vb")
+    ts(T.w16[:, 16:32], T.c32[:, 0:16], r1_col, OP.is_gt, to="vc")
+    ts(T.w16[:, 32:48], T.c32[:, 0:16], r1_col, OP.is_equal, 2.0 ** 40, OP.mult, "vc")
     wait("v", "uq", "of")
-    sig(V.tensor_copy(T.pq[:].bitcast(dt.uint32), T.uq[:].bitcast(dt.uint32).indirect(T.off[:, 0:16])), "pk")
-    wait("s", "uq", "of")
-    act(T.ps[:], T.us[:].indirect(T.off[:, 0:16]), AF.Copy, "pks")
-    wait("s", "xb")
+    sig(V.tensor_copy(T.pq[:].bitcast(dt.uint32), T.uq[:].bitcast(dt.uint32).indirect(T.off[:])), "pk")
+    wait("v", "vc")
+    tt(T.w16[:, 0:16], T.w16[:, 16:32], T.w16[:, 32:48], OP.add, "w16")
     magic = 1.5 * 2.0 ** 23
-    act(T.yb[:], T.xb[:], AF.Identity, "s", bias=magic)
+    wait("s", "wb")
+    act(T.yb[:], T.wb[:], AF.Identity, "s", bias=magic, scale=1.0 / 512)
     wait("s", "s")
-    act(T.d0[:], T.yb[:], AF.Identity, "s", bias=1024.0 * magic, scale=-1024.0)
+    act(T.nb[:], T.yb[:], AF.Identity, "s", bias=-512.0 * magic, scale=512.0)
     wait("s", "s")
-    act(T.d1[:], T.d0[:], AF.Identity, "dd", bias=1.0, scale=-GROW)
+    act(T.b1[:], T.nb[:], AF.Identity, "b1", bias=257.5, scale=GROW)
+    wait("s", "uq", "of")
+    act(T.ps[:], T.us[:].indirect(T.off[:]), AF.Copy, "pks")
+    wait("s", "w16")
+    act(T.wn[:], T.w16[:, 0:16].indirect(T.rep[:]), AF.Copy, "wn")
+    wait("s", "p33", "hd")
+    for c in reversed(range(NB)):
+        act(T.hold[:, AT[c + 1] - 32:AT[c + 1] + 1], T.p33[:, 0:33], AF.Identity, "hp", bias=1.0)
+    wait("g", "one")
+    for b in range(4):
+        if b == 2:
+            iota(T.cmod[:], [[0, NB], [1, 16]], 0, "g3")
+        sig(g.affine_select(T.et[:, 512 * b:512 * b + 512], T.ones[:], [[-1, 128], [1000, 4]], OP.is_equal, 0.0, -1000 * b, 1), "et")
+    wait("v", "b1", "va", "g2")
+    scan(T.kr[:], T.wb[:, 1:C + 1], T.b1[:, 0:C], 0.0, OP.max, OP.subtract, "va")
+    scan(T.ends[:], T.inc[:], T.zb[:, 0:32], -1.0, OP.add, OP.add, "vb")
+    wait("v", "va")
+    turn(T.krt[:], T.kr[:], "va")
     wait("v", "lx")
     quant(T.xq0[:], T.xs0[:], T.x0[:], "xq0")
-    ts(T.r0[:], T.cmod[:], 0.0, OP.is_equal, BIG, OP.mult)
-    wait("v", "g2")
-    for e in range(4):
-        ts(T.gt[:, e:512:4], T.gidx[:], g_col, OP.is_equal)
+    wait("v", "va", "vb", "wn")
+    tt(T.st[:], T.jr[:], T.krt[:, 16 * 2 * B0:C:16], OP.subtract, "va")
+    scan(T.ew[:], T.wn[:, 0:32], T.ends[:], 0.0, OP.mult, OP.add, "vb")
+    ts(T.acc[:, 0:2 * B0], T.krt[:, 0:16 * 2 * B0:16], -UNIT, OP.mult, (1 + KAPPA0) * UNIT, OP.add)
+    wait("v", "va")
+    ts(T.sg[:, 0:NS * SW:SW], T.st[:], -8.0, OP.add, to="va")
+    fill(T.acc[:, NB:32], 0.0)
+    wait("v", "va", "vb")
+    tt(T.sg[:, 1:NS * SW:SW], T.st[:], T.sg[:, 0:NS * SW:SW], OP.subtract, "st")
+    ts(T.eo[:], T.ew[:, 15:32:16], sc_col, OP.mult)
+    fill(T.cmp[:, AT[NB - 1] - 1:AT[NB]:LEN[NB - 1] + 1], 0.0)
 
     def later_constants():
-        ts(r1_col, r_col, 1.0, OP.add, to="vb")
-        ts(sc_col, r_col, 15.0, OP.is_equal, 2.0 ** -40, OP.max)
-        ts(T.ca[:], T.cmod[:, 0:16], r_col, OP.is_gt, GROW - 1.0, OP.mult, "vb")
-        ts(T.cb[:], T.cmod[:, 0:16], r_col, OP.not_equal, 2.0 ** -12, OP.max, "vb")
-        wait("v", "g4", "dd")
-        scan(T.ik[:, 0:H], T.d0[:, 1:H + 1], T.d1[:, 0:H], -1.0, OP.add, OP.add, "vc")
-        scan(T.ik[:, H:C], T.d0[:, SEG + 1:SEG + H + 1], T.d1[:, SEG:SEG + H], H - 1.0, OP.add, OP.add, "vc")
-        wait("v", "vb")
-        ts(T.wa[:], T.cmod[:], r1_col, OP.is_gt, to="vb")
-        ts(T.wb[:], T.cmod[:], r1_col, OP.is_equal, 2.0 ** 40, OP.mult, "vb")
-        wait("v", "vc")
-        sig(V.transpose(T.ikt[:], T.ik[:]), "v")
-        wait("v", "vb")
-        tt(T.wn[:], T.wa[:], T.wb[:], OP.add, "vb")
-        tt(T.mul[:, 0:16], T.ca[:], T.cb[:], OP.add)
+        wait("v", "g3")
+        ts(T.ca[:], T.c32[:, 0:16], r_col, OP.is_gt, GROW - 1.0, OP.mult, "vb")
+        ts(T.cb[:], T.c32[:, 0:16], r_col, OP.not_equal, 2.0 ** -12, OP.max, "vb")
+        ts(sc8_col, sc_col, 2.0 ** 12 * UNIT, OP.mult, to="vb")
+        scan(T.kk[:], T.wn[:], T.b1[:, 0:C], 0.0, OP.mult, OP.add, "vb")
+        ts(T.rz[:], T.cmod[:], 0.0, OP.not_equal)
+        ts(T.rp[:], T.zb[:, 0:C], 0.0, OP.add)
         ts(T.mul[:, 16:STEPS], T.zb[:, 16:STEPS], GROW, OP.add)
+        ts(T.mb[:, C:C + 1], T.zb[:, 0:1], LAST * UNIT, OP.add)
+        ts(T.stp[:, 0:1], T.zb[:, 0:1], 0.0, OP.add)
+        ts(T.stp[:, STEPS - 1:STEPS], T.zb[:, 0:1], LEAVE * UNIT, OP.add)
+        ts(scu_col, sc_col, 1.0 / UNIT, OP.mult)
         wait("v", "vb")
-        scan(T.kk[:, 0:H], T.wn[:, 0:H], T.d1[:, 1:H + 1], 0.0, OP.mult, OP.add, "vb")
-        scan(T.kk[:, H:C], T.wn[:, 0:H], T.d1[:, SEG + 1:SEG + H + 1], 0.0, OP.mult, OP.add, "vb")
-        ts(T.mb[:, 1:325:323], T.zb[:, 0:2], (MV3 + DRIFT2) * UNIT, OP.add)
-        ts(T.mb[:, 162:164], T.cv[:, 0:2], UNIT, OP.mult)
-        wait("v", "vb", "v")
-        ts(T.k1[:], T.kk[:, 15:C:16], sc_col, OP.mult, 170.0, OP.add, "vb")
-        ts(T.stp[:, SEG - 1:STEPS:SEG], T.cv[:, 2:4], 4096.0 * UNIT, OP.mult)
-        wait("v", "vb")
-        ts(T.k0[:], T.k1[:], 2.0 ** 12 * UNIT, OP.mult)
+        tt(T.mul[:, 0:16], T.ca[:], T.cb[:], OP.add)
+        ts(T.k0[:], T.kk[:, 15:C:16], sc8_col, OP.mult, -2.0 ** 12 * UNIT, OP.add)
 
     for t, mask_t in enumerate(ROUNDS):
         peer = T.cores[rank ^ mask_t]
         rid, pid = topo.addr(peer)[0:2]
         mask, ne = topo.mask(core, peer), len(topo.engines(core, peer))
-        xq = (T["xq%d" % t][:], T["xs%d" % t][:])
-        aq = (T["aq%d" % t][:], T["as%d" % t][:])
+        xq = (T["xq%d" % t], T["xs%d" % t])
+        aq = (T["aq%d" % t], T["as%d" % t])
         snd, land = T["snd%d" % t], T["land%d" % t]
         last = t == len(ROUNDS) - 1
 
         wait("g", "xq%d" % t)
-        g.remote_dma(aq[0].bitcast(dt.uint8), xq[0].bitcast(dt.uint8), T.sem["aq%d" % t], T.sem.left, pid, rid, mask)
-        g.remote_dma(aq[1], xq[1], T.sem["aq%d" % t], T.sem.left, pid, rid, mask)
+        g.remote_dma(aq[0][:].bitcast(dt.uint8), xq[0][:].bitcast(dt.uint8), T.sem["aq%d" % t], T.sem.left, pid, rid, mask)
+        g.remote_dma(aq[1][:], xq[1][:], T.sem["aq%d" % t], T.sem.left, pid, rid, mask)
         cnt["aq%d" % t] += 2 * ne
         cnt["left"] += 2 * ne
         if t == 0:
-            iota(T.cv[:, 0:2], [[MV2 - MV1 - DRIFT1, 2]], MV1 + DRIFT1, "g4")
-            iota(T.cv[:, 2:4], [[(LEAVE - REBASE) // 4096, 2]], REBASE // 4096, "g4")
-            iota(T.io1[:], [[1, C]], NAME0, "g4")
+            iota(T.io1[:], [[1, C]], NAME0, "g3")
 
+        ju = max(J)
         wait("p", "pk", "pks", "xq%d" % t)
-        mx(T.pa[:, 0:C], (T.pq[:, 0:128], T.ps[:, 0:128]), xq, "ma")
-        mx(T.ph[:, 0:C], (T.pq[:, 0:128], T.ps[:, 0:128]), xq, "mh")
-        mx(T.pb[:, 0:C], (T.pq[:, 128:256], T.ps[:, 128:256]), xq, "mb")
+        mx(bank[0][:, 0:C - UP], cols(pq, 0, 128), cols(xq, UP, C), "mu")
+        mx(bank[1][:, 0:ju], cols(pq, 128, 256), cols(xq, 0, ju), "mes")
+        mx(bank[3][:, 0:UP], cols(pq, 0, 128), cols(xq, 0, UP), "ml")
+        mx(bank[2][:, 0:C], cols(pq, 128, 256), cols(xq, 0, C), "mev")
+        mx(bank[4][:, 0:ju], cols(pq, 256, 384), cols(xq, 0, ju), "mos")
+        mx(bank[5][:, 0:C], cols(pq, 256, 384), cols(xq, 0, C), "mov")
+        mx(bank[6][:, 0:C], cols(pq, 384, 512), cols(xq, 0, C), "mw")
 
-        wait("v", "ma", "v")
-        tt(T.t1[:, 0:HEAD], T.pa[:, 0:HEAD], T.mk[:, 0:HEAD], OP.add, "a0")
-        tt(T.t1[:, HEAD:C], T.pa[:, HEAD:C], T.mk[:, HEAD:C], OP.add)
-        wait("v", "a0")
-        scan(T.a1[:, 1:HEAD + 1], T.r0[:, 0:HEAD], T.t1[:, 0:HEAD], BIG, OP.add, OP.min, "a0")
-        wait("v", "v")
-        scan(T.a1[:, HEAD + 1:C + 1], T.r0[:, HEAD:C], T.t1[:, HEAD:C], BIG, OP.add, OP.min, "a1")
-        if t == 0:
-            quant(T.gq[:], T.gs[:], T.gt[:], "gq")
-            fill(T.cap[:], CAP, "vd")
-            fill(T.cum[:, 0:1], 0.0, "vd")
-        wait("v", "a0", "a1", "pad")
-        wait("s", "a0", "mh", "pad")
-        for k in range(KS):
-            if 16 * k + 16 > HEAD:
-                wait("s", "a1")
-            act(slot(k + 1, 16 * k + 17), T.ph[:, 16 * k + 17:C], AF.Sign, "sg%d" % ((k + 1) // 4),
-                bias=T.a1[:, 16 * k + 16:16 * k + 17], scale=-1.0)
-        wait("s", "sg0")
-        for k in range(3):
-            act(slot(k + 1, 16 * k + 17), slot(k + 1, 16 * k + 17), AF.Relu, "f0", scale=-1.0)
-        for k in reversed(range(KS, NB - 1)):
-            ts(slot(k + 1, 16 * k + 17), T.pa[:, 16 * k + 17:C], T.a1[:, 16 * k + 16:16 * k + 17], OP.is_gt,
-               to="va" if k >= 15 else "vb")
-        tt(slot(0, 0), T.a1[:, 0:C], T.pa[:, 0:C], OP.is_lt, "vc")
-        wait("v", "va")
-        quant_tile(4)
-        wait("v", "vb")
-        quant_tile(3)
-        for m in (1, 2):
-            wait("v", "sg%d" % m)
-            whole = T.ct[:, 4 * CB[m]:4 * (CB[m] + C - Q0[m])]
-            ts(whole, whole, 0.0, OP.is_lt, to="va")
-            if m == 1:
-                wait("v", "mb")
-                ts(T.want[:], T.pb[:, 0:C], 0.0, OP.is_gt, to="vd")
-            else:
-                wait("v", "vd")
-                scan(T.cum[:, 1:C + 1], T.want[:], T.cap[:], 0.0, OP.add, OP.min, "vd")
-            wait("v", "va")
-            quant_tile(m)
-        wait("v", "f0", "vc")
-        quant_tile(0)
-        wait("p", "gq")
-        for m in (4, 3, 1, 2, 0):
-            wait("p", "c%d" % m)
-            mx(T.pl[:, 0:C], (T.gq[:], T.gs[:]), (T.cq[:, C * m:C * m + C], T.cs[:, C * m:C * m + C]),
-               "ml" if m == 0 else None, m == 4, m == 0)
-        wait("v", "vd")
-        scan(T.take[:], T.cum[:, 1:C + 1], T.cum[:, 0:C], 0.0, OP.max, OP.subtract, "vd")
+        wait("v", "mu", "v")
+        turn(T.tc[:, UP:C], bank[0][:, 0:C - UP], "tu")
         wait("v", "ml")
-        sig(V.transpose(T.lt[:], T.pl[:, 0:C]), "va")
-        wait("v", "vd")
-        sig(V.transpose(T.tkt[:], T.take[:]), "vd")
-        wait("v", "va")
-        sig(V.tensor_copy(snd[:], T.lt[:, 0:C:16]), "sn%d" % t)
+        turn(T.tc[:, 0:UP], bank[3][:, 0:UP], "tl")
+
+        def own(c):
+            return T.tc[:, 16 * c:16 * c + 1]
+
+        order = [c for h in range(2) for c in reversed(range(2 * B0 + h, NB, 2))]
+        wait("s", "tu", "mes")
+        for n in range(NS + 1):
+            if n < NS:
+                c = order[n]
+                if c % 2:
+                    wait("s", "mos")
+                a = SW * (c - 2 * B0)
+                act(T.sg[:, a + 2:a + 2 + J[c]], bank[1 + 3 * (c % 2)][:, 0:J[c]], AF.Sign, "sa" if n % 2 else "sb",
+                    bias=own(c), scale=-1.0)
+            if n > 0:
+                c = order[n - 1]
+                a = SW * (c - 2 * B0)
+                wait("s", "sb" if n % 2 else "sa", "st")
+                act(T.sr[:, a:a + 2 + J[c]], T.sg[:, a:a + 2 + J[c]], AF.Relu, "sr", scale=UNIT, accum_out=T.acc[:, c:c + 1])
+
+        def compare(c, to):
+            n = min(LEN[c] + 1, C - J[c])
+            ts(T.cmp[:, AT[c]:AT[c] + n], bank[2 + 3 * (c % 2)][:, J[c]:J[c] + n], own(c), OP.is_ge, TINY * UNIT, OP.mult, to)
+
+        def count(a, b, to):
+            scan(T.cnt[:, AT[a]:AT[b]], T.hold[:, AT[a]:AT[b]], T.cmp[:, AT[a]:AT[b]], 0.0, OP.mult, OP.add, to)
+
+        wait("v", "tu", "mev")
+        for c in range(2 * B0, NB, 2):
+            compare(c, "va")
+        wait("v", "tl")
+        for c in range(0, 2 * B0, 2):
+            compare(c, "vc" if c < 8 else "vb")
+        wait("v", "mov")
+        for c in range(2 * B0 + 1, NB, 2):
+            compare(c, "va")
+        for c in range(9, 2 * B0, 2):
+            compare(c, "vb")
+        wait("v", "va", "hp")
+        count(2 * B0, NB, "vd")
+        for c in range(1, 8, 2):
+            compare(c, "vc")
+        wait("v", "vb")
+        count(8, 2 * B0, "vd")
+        wait("v", "vc")
+        count(0, 8, "vd")
+        if t == 0:
+            ts(T.cap[:], T.zb[:, 0:C], CAP * C * UNIT, OP.add, to="ve")
+            ts(T.cum[:, 0:1], T.zb[:, 0:1], 0.0, OP.add, to="ve")
+        wait("v", "mw")
+        ts(T.want[:], bank[6][:, 0:C], 0.0, OP.is_gt, C * UNIT, OP.mult, "ve")
+        wait("v", "vd", "sr", "v")
+        tt(snd[:], T.cnt[:, 0:AT[NB]].indirect(T.eo[:]), T.acc[:], OP.subtract, "sn%d" % t)
         wait("g", "sn%d" % t)
-        g.remote_dma(land[:], snd[:], T.sem["at%d" % t], T.sem.left, pid, rid, mask)
+        g.remote_dma(land[:], snd[:, 0:NB], T.sem["at%d" % t], T.sem.left, pid, rid, mask)
         cnt["at%d" % t] += ne
         cnt["left"] += ne
 
+        wait("v", "ve")
+        scan(T.cum[:, 1:C + 1], T.want[:], T.cap[:], 0.0, OP.add, OP.min, "ve")
         if t == 0:
-            wait("s", "g3")
-            for b in range(4):
-                for e in range(4):
-                    act(T.et[:, 512 * b + e:512 * b + 512:4], T.ident[:], AF.Copy, "et", scale=1.0 if b == e else 0.0)
             wait("s", "lx")
             for b in range(4):
                 act(win[b][:, 0:C], T.x0[:, b:4 * C:4], AF.Copy, "dun", scale=32.0)
-            later_constants()
-        wait("v", "vd")
-        ts(T.own[:], T.tkt[:, 0:C:16], -1.0, OP.mult, 1.0, OP.add, "va")
-        ts(T.t320[:], T.take[:], float(C), OP.mult, to="vd")
-        wait("v", "va", "sn%d" % t)
-        tt(T.o1[:], snd[:], T.own[:], OP.mult, "va")
-        wait("v", "vd")
-        scan(T.val[:], T.t320[:], T.io1[:], 2.0 * C, OP.min, OP.add, "vd")
-        wait("v", "va", "v")
-        tt(T.lo[:], T.ikt[:, 0:C:16], T.o1[:], OP.subtract)
-        if t == 0:
-            wait("v", "et")
+            wait("v", "et", "g3")
             quant(T.eq[:], T.es[:], T.et[:], "eq")
-        wait("p", "eq", "aq%d" % t)
-        for b in range(4):
-            mx(T[BANKS[b]][:, 0:C], (T.eq[:, 128 * b:128 * b + 128], T.es[:, 128 * b:128 * b + 128]), aq, "md%d" % b)
+            ts(T.iou[:], T.io1[:], UNIT, OP.mult, to="vc")
+        wait("v", "ve")
+        scan(T.take[:], T.cum[:, 1:C + 1], T.cum[:, 0:C], 0.0, OP.max, OP.subtract, "ve")
+        if t == 0:
+            later_constants()
+        wait("v", "ve", "vc")
+        turn(T.tkt[:], T.take[:], "va")
+        scan(T.val[:], T.take[:], T.iou[:], 2.0, OP.min, OP.add, "ve")
+        wait("v", "va", "sn%d" % t)
+        tt(T.hi[:], snd[:, 0:NB], T.tkt[:, 0:C:16], OP.add, "va")
+        tt(T.lo[:], snd[:, 0:NB], T.tkt[:, 0:C:16], OP.subtract, "va")
+        wait("p", "eq", "aq%d" % t, "tu", "tl")
+        for b, k in enumerate((7, 0, 3, 1)):
+            if k == 1:
+                wait("p", "sa", "sb")
+            mx(bank[k][:, 0:C], cols(eq, 128 * b, 128 * b + 128), cols(aq, 0, C), "md%d" % b)
             wait("s", "md%d" % b)
-            act(win[b][:, C:2 * C], T[BANKS[b]][:, 0:C], AF.Copy, "dun", scale=32.0)
+            act(win[b][:, C:2 * C], bank[k][:, 0:C], AF.Copy, "dun", scale=32.0)
 
-        wait("v", "at%d" % t)
-        tt(T.tt[:], land[:], T.tkt[:, 0:C:16], OP.mult)
+        wait("v", "at%d" % t, "va", "v")
+        tt(T.mid[:], land[:], T.hi[:], OP.min)
         wait("v", "v")
-        tt(T.mm[:], T.lo[:], T.tt[:], OP.subtract)
-        wait("v", "v")
-        ts(T.bc[:, H:C], T.mm[:].indirect(T.off[:, 26:36]), UNIT, OP.mult, to="va")
-        ts(T.bc[:, 0:H], T.mm[:].indirect(T.off[:, 16:26]), UNIT, OP.mult, to="vb")
-        wait("v", "va")
-        sig(V.transpose(T.mb[:, 164:324], T.bc[:, H:C]), "va")
-        wait("v", "vb")
-        sig(V.transpose(T.mb[:, 2:162], T.bc[:, 0:H]), "vb")
-        wait("v", "va")
-        tt(T.stp[:, SEG:SEG + 161], T.mb[:, 163:324], T.mb[:, 164:325], OP.subtract, "va")
-        wait("v", "vb")
-        tt(T.stp[:, 0:161], T.mb[:, 1:162], T.mb[:, 2:163], OP.subtract, "vb")
+        tt(T.rp[:, H:C:16], T.mid[:, 10:NB], T.lo[:, 10:NB], OP.max, "va")
+        tt(T.rp[:, 0:H:16], T.mid[:, 0:10], T.lo[:, 0:10], OP.max, "vb")
+        for a, to in ((H, "va"), (0, "vb")):
+            wait("v", to)
+            scan(T.bc[:, a:a + H], T.rz[:, 0:H], T.rp[:, a:a + H], 0.0, OP.mult, OP.add, to)
+        for a, to in ((H, "va"), (0, "vb")):
+            wait("v", to)
+            turn(T.mb[:, a:a + H], T.bc[:, a:a + H], to)
+        for a, to in ((H, "va"), (0, "vb")):
+            wait("v", to)
+            scan(T.stp[:, a + 1:a + H + 1], T.mb[:, a:a + H], T.mb[:, a + 1:a + H + 1], 0.0, OP.min, OP.subtract, to)
 
         def order_scan(k, to):
-            s0 = 16 * k + (2 if k >= NB // 2 else 0)
-            scan(T.so[:, STEPS * k + s0:STEPS * (k + 1)], T.stp[:, s0:STEPS], T.mul[:, 0:STEPS - s0],
+            scan(T.so[:, STEPS * k + 16 * k:STEPS * (k + 1)], T.stp[:, 16 * k:STEPS], T.mul[:, 0:STEPS - 16 * k],
                  T.k0[:, k:k + 1], OP.add, OP.mult, to)
 
         def places(a, b):
-            ts(T.po[:, a:b], T.so[:, STEPS * (a + 1) - 1:STEPS * b:STEPS], 1.0 / (UNIT * GROW), OP.mult, 160.0, OP.add, "vc")
+            ts(T.po[:, a:b], T.so[:, STEPS * (a + 1) - 1:STEPS * b:STEPS], 1.0 / (UNIT * GROW), OP.mult, float(H), OP.add, "vc")
 
         wait("v", "va")
-        for k in range(10, NB):
+        for k in range(11, NB):
             order_scan(k, "va")
         wait("v", "vb")
+        order_scan(10, "va")
         for k in range(0, 5):
             order_scan(k, "vb")
         wait("v", "va")
         places(10, NB)
         for k in range(5, 10):
             order_scan(k, "vb")
-        wait("v", "vc", "vd")
+        wait("v", "vc", "ve")
         sig(V.tensor_copy(T.nm[:].indirect(T.po[:, 10:NB]), T.val[:, H:C]), "nm")
         wait("v", "vb")
         places(0, 10)
         wait("v", "vc", "nm")
         sig(V.tensor_copy(T.nm[:].indirect(T.po[:, 0:10]), T.val[:, 0:H]), "nm")
         wait("v", "nm")
-        scan(T.ns[:], T.wn[:], T.nm[:], 0.0, OP.mult, OP.add)
-        wait("v", "v")
-        ts(T.zo[:], T.ns[:, 15:C:16], sc_col, OP.mult, -float(NAME0), OP.add, "zo")
+        for a, to in ((0, "va"), (H, "vb")):
+            scan(T.ns[:, a:a + H], T.wn[:, 0:H], T.nm[:, a:a + H], 0.0, OP.mult, OP.add, to)
+        for h, to in ((0, "va"), (1, "vb")):
+            wait("v", to)
+            ts(T.zo[:, 10 * h:10 * h + 10], T.ns[:, H * h + 15:H * h + H:16], scu_col, OP.mult, -float(NAME0), OP.add, "zo%d" % h)
         if last:
             wait("s", "nm")
-            act(T.odb[:], T.nm[:], AF.Identity, "od", bias=-float(NAME0))
+            act(T.odb[:], T.nm[:], AF.Identity, "od", bias=-float(NAME0), scale=1.0 / UNIT)
             wait("y", "od")
             for k in range(8):
                 sig(SY.dma_start(T.od[k:k + 1, :], T.odb[16 * k:16 * k + 1, :]), "out", 16)
 
-        wait("v", "zo", "dun")
-        wait("s", "zo", "dun")
+        wait("v", "zo0", "dun")
+        wait("s", "zo1", "dun")
         for b in range(4):
             ts(elem(T.zt, b, 0), win[b][:].indirect(T.zo[:, 0:10]), 2.0 ** -5, OP.mult, to="zv")
             act(elem(T.zt, b, 1), win[b][:].indirect(T.zo[:, 10:NB]), AF.Copy, "zg", scale=2.0 ** -5)
@@ -398,15 +416,14 @@ def rank_program(g, core, T, topo):
             for b in range(4):
                 j = 4 * h + b
                 act(T.z32[:, H * j:H * j + H], elem(T.zt, b, h), AF.Copy, "z%d" % j, scale=32.0)
-                mx(T[BANKS[j]][:, 0:H], (T.wq[:, 128 * b:128 * b + 128], T.wp[:, 128 * b:128 * b + 128]),
-                   (T.zq[:, H * h:H * h + H], T.zs[:, H * h:H * h + H]), "r%d" % j)
+                mx(bank[j][:, 0:H], cols(wq, 128 * b, 128 * b + 128), cols((T.zq, T.zs), H * h, H * h + H), "r%d" % j)
         if t == 0:
             wait("v", "lv")
             quant(T.vq[:], T.vs[:], T.vt[:], "vq")
         for j in range(8):
             h, b = divmod(j, 4)
             wait("v", "r%d" % j, "z%d" % j)
-            tt(win[b][:, H * h:H * h + H], T[BANKS[j]][:, 0:H], T.z32[:, H * j:H * j + H], OP.add, "e%d" % j)
+            tt(win[b][:, H * h:H * h + H], bank[j][:, 0:H], T.z32[:, H * j:H * j + H], OP.add, "e%d" % j)
         for b in range(4):
             wait("s", "e%d" % b)
             act(elem(T.xn, b, 0), win[b][:, 0:H], AF.Copy, "xs", scale=2.0 ** -5)
@@ -416,14 +433,14 @@ def rank_program(g, core, T, topo):
         quant(T["xq%d" % (t + 1)][:], T["xs%d" % (t + 1)][:], T.xn[:], "xq%d" % (t + 1))
 
     wait("p", "vq", "xq3")
-    mx(T.pa[:, 0:C], (T.vq[:], T.vs[:]), (T.xq3[:], T.xs3[:]), "my")
+    mx(bank[0][:, 0:C], (T.vq[:], T.vs[:]), (T.xq3[:], T.xs3[:]), "my")
     wait("y", "xq3")
     wait("s", "xq3")
     sig(SY.dma_start(T.oc[:], T.xq3[:].bitcast(dt.uint8)), "out", 16)
     for k in range(4):
         sig(S.dma_start(T.osc[4 * k:4 * k + 4, :], T.xs3[32 * k:32 * k + 4, :]), "out", 16)
     wait("v", "my")
-    sig(V.tensor_copy(T.ysb[:], T.pa[:, 0:C]), "ys")
+    sig(V.tensor_copy(T.ysb[:], bank[0][:, 0:C]), "ys")
     wait("y", "ys")
     sig(SY.dma_start(T.y[:], T.ysb[:]), "out", 16)
     wait("g", *SEMAPHORES)

@@ -15,6 +15,7 @@ W0 = 8522306.0
 KAPPA0 = 1152
 STEPS = C + 2
 TINY = 2.0 ** -30
+MAGIC = 1.5 * 2.0 ** 23
 
 
 def _ends():
@@ -30,32 +31,35 @@ def _ends():
 
 LAST, LEAVE = _ends()
 
-B0 = 6
-OVER = 32
+B0 = 7
+OVER = 48
 J = [0] * (2 * B0) + [32 * (c // 2) - OVER for c in range(2 * B0, NB)]
 LEN = [32 * (c // 2) + 32 - J[c] for c in range(NB)]
 AT = [sum(LEN[:c]) + c for c in range(NB + 1)]
-SW = 32 * 9 - OVER + 2
+SW = max(J) + 2
 NS = NB - 2 * B0
-UP = 32 * B0
+A = 128
+CA = A // 16
+GATHER = (64, 208)
+EARLY = 160
 
 X4 = "float8_e4m3fn_x4"
 SCRATCH = {}
 for _dt, _list in (
-        ("bfloat16", (("x0", 4 * C), ("xn", 4 * C), ("ut", 512), ("vt", 512), ("et", 2048),
-                      ("zt", 4 * C), ("z32", 4 * C), ("zb", 336), ("ones", 512), ("cmod", C), ("c32", 34), ("p33", 34),
-                      ("w16", 48), ("wn", C), ("cmp", AT[NB] + 1), ("hold", AT[NB] + 1), ("cnt", AT[NB] + 1),
-                      ("sg", NS * SW), ("sr", NS * SW), ("so", NB * STEPS),
-                      ("win0", 2 * C), ("win1", 2 * C), ("win2", 2 * C), ("win3", 2 * C))),
-        ("float32", (("pf", 8), ("wb", STEPS), ("yb", STEPS), ("nb", STEPS), ("b1", STEPS), ("kr", C), ("krt", C),
-                     ("kk", C), ("k0", NB), ("ca", 16), ("cb", 16), ("inc", 32), ("ends", 32), ("ew", 32), ("jr", NS),
-                     ("st", NS), ("acc", 32), ("tc", C), ("lo", NB), ("hi", NB), ("mid", NB), ("nm", C), ("ns", C),
-                     ("odb", C), ("ysb", C), ("io1", C), ("snd0", 32), ("snd1", 32), ("snd2", 32),
+        ("bfloat16", (("x0", 4 * C), ("xn", 4 * C), ("ut", 512), ("vt", 512), ("et", 2048), ("zt", 4 * C), ("z32", 4 * C),
+                      ("zb", 512), ("rz16", 16), ("rz", H), ("c32", 34), ("c16", 32), ("c4", 16), ("p33", 34),
+                      ("w32", 96), ("w4", 48), ("wn", C), ("wn4", C), ("cmp", AT[NB] + 1), ("hold", AT[NB] + 1),
+                      ("cnt", AT[NB] + 1), ("sg", NS * SW), ("sr", NS * SW), ("so", NB * STEPS),
+                      ("win0", 8 * C), ("win1", 8 * C))),
+        ("float32", (("pf", 12), ("wb", STEPS), ("wt", C), ("ka", 4 * NB), ("kb", 4 * NB), ("kr", NB), ("kk", C),
+                     ("k0", NB), ("ca", 16), ("cb", 16), ("inc", 32), ("ends", 32), ("ew", 32), ("jr", NB),
+                     ("st", NB), ("acc", 32), ("tc", C), ("lo", NB), ("hi", NB), ("mid", NB), ("nm", C), ("ns", C),
+                     ("odb", C), ("ysb", C), ("snd0", 32), ("snd1", 32), ("snd2", 32),
                      ("land0", NB), ("land1", NB), ("land2", NB))),
-        (HALF, (("gr", STEPS), ("mul", STEPS), ("rp", C), ("rz", C), ("bc", C), ("mb", C + 2), ("stp", STEPS),
+        (HALF, (("mul", STEPS), ("rp", C), ("un", C), ("bc", C), ("mb", C + 2), ("stp", STEPS),
                 ("cap", C), ("want", C), ("cum", C + 2), ("take", C), ("tkt", C), ("val", C), ("iou", C))),
-        ("int32", (("pi", 4), ("oi", 32))),
-        ("uint16", (("off", 32), ("rep", NB), ("eo", 2), ("po", NB), ("zo", NB)))):
+        ("int32", (("pi", 6), ("oi", 32))),
+        ("uint16", (("off", 32), ("rep", NB), ("eo", 2), ("po", NB), ("zo", C // 4)))):
     for _n, _w in _list:
         SCRATCH[_n] = ("sbuf", [128, _w], _dt)
 for _q, _s, _w in (("uq", "us", 128), ("pq", "ps", 512), ("vq", "vs", 128), ("wq", "wp", 512), ("eq", "es", 512),
@@ -67,13 +71,9 @@ BANKS = ["p%d" % _b for _b in range(8)]
 for _n in BANKS:
     SCRATCH[_n] = ("psum", [128, 512], "float32")
 
-SEMAPHORES = (["v", "va", "vb", "vc", "vd", "ve", "s", "sa", "sb", "sr", "lx", "lu", "lv", "lw", "g0", "g1", "g2", "g3",
-               "one", "hd", "hp", "p33", "wb", "b1", "w16", "wn", "st", "uq", "of", "pk", "pks", "mu", "ml", "mes", "mos",
-               "mev", "mov", "mw", "tu", "tl", "et", "eq", "dun", "nm", "zo0", "zo1", "zv", "zg", "zq0", "zq1", "xs",
-               "vq", "my", "ys", "od", "out", "left"]
-              + ["%s%d" % (n, b) for n in ("md", "xq") for b in range(4)]
-              + ["%s%d" % (n, b) for n in ("r", "z", "e") for b in range(8)]
-              + ["%s%d" % (n, t) for n in ("aq", "at", "sn") for t in range(3)])
+POOL = ["c%d" % _b for _b in range(130)]
+SEMAPHORES = (POOL + ["lx", "lu", "lv", "lw", "out", "left"]
+              + ["%s%d" % (n, t) for n in ("aq", "at") for t in range(3)])
 
 
 def rank_program(g, core, T, topo):
@@ -82,365 +82,446 @@ def rank_program(g, core, T, topo):
         return
     V, S, PE, SY = g.vector, g.scalar, g.tensor, g.sync
     queue = {"g": g, "v": V, "s": S, "p": PE, "y": SY}
-    cnt = {n: 0 for n in SEMAPHORES}
-    seen = {}
 
-    def sig(ins, name, n=1):
+    cnt = {n: 0 for n in SEMAPHORES}
+    known = {q: {} for q in queue}
+    free = list(POOL)
+
+    def wait(q, *marks):
+        for m in marks:
+            if isinstance(m, list):
+                wait(q, *m)
+            elif known[q].get(m[0], 0) < m[1]:
+                queue[q].wait_ge(T.sem[m[0]], m[1])
+                known[q][m[0]] = m[1]
+                for n, c in m[2].items():
+                    known[q][n] = max(known[q].get(n, 0), c)
+
+    def mark(q, ins, join=None, name=None, n=1):
+        if name is None:
+            name = join[0] if join else [s for s in free if known[q].get(s, 0) == cnt[s]][0]
+            free.remove(name)
+            free.append(name)
         ins.then_inc(T.sem[name], n)
         cnt[name] += n
+        return (name, cnt[name], dict(known[q]))
 
-    def wait(q, *names):
-        for n in names:
-            if seen.get((q, n), 0) < cnt[n]:
-                queue[q].wait_ge(T.sem[n], cnt[n])
-                seen[(q, n)] = cnt[n]
-
-    def ts(out, in0, s1, op0, s2=None, op1=None, to="v"):
+    def ts(out, in0, s1, op0, s2=None, op1=None, join=None):
         if op1 is None:
-            sig(V.tensor_scalar(out, in0, s1, None, op0), to)
-        else:
-            sig(V.tensor_scalar(out, in0, s1, s2, op0, op1), to)
+            return mark("v", V.tensor_scalar(out, in0, s1, None, op0), join)
+        return mark("v", V.tensor_scalar(out, in0, s1, s2, op0, op1), join)
 
-    def tt(out, in0, in1, op, to="v"):
-        sig(V.tensor_tensor(out, in0, in1, op), to)
+    def tt(out, in0, in1, op, join=None):
+        return mark("v", V.tensor_tensor(out, in0, in1, op), join)
 
-    def scan(out, d0, d1, init, op0, op1, to="v"):
-        sig(V.tensor_tensor_scan(out, d0, d1, init, op0, op1), to)
+    def scan(out, d0, d1, init, op0, op1, join=None):
+        return mark("v", V.tensor_tensor_scan(out, d0, d1, init, op0, op1), join)
 
-    def fill(ap, c, to="v"):
-        sig(V.memset(ap, c), to)
+    def copy(out, in_, join=None):
+        return mark("v", V.tensor_copy(out, in_), join)
 
-    def quant(q, s, tile, to="v"):
-        sig(V.quantize_mx(q, s, tile), to)
+    def fill(ap, c, join=None):
+        return mark("v", V.memset(ap, c), join)
 
-    def turn(out, in_, to="v"):
-        sig(V.transpose(out, in_), to)
+    def quant(q, a, e, tile):
+        return mark("v", V.quantize_mx(q[0][:, a:e], q[1][:, a:e], tile[:, 4 * a:4 * e]))
 
-    def act(out, in_, func, to, **kw):
-        sig(S.activation(out, in_, func, **kw), to)
+    def turn(out, in_):
+        return mark("v", V.transpose(out, in_))
 
-    def iota(out, pattern, base, to):
-        sig(g.iota(out, pattern, base, 0, allow_small_or_imprecise_dtypes=True), to)
+    def act(out, in_, func, join=None, **kw):
+        return mark("s", S.activation(out, in_, func, **kw), join)
 
-    def mx(out, a, b, to):
-        sig(PE.matmul_mx(out, a[0], a[1], b[0], b[1], True, True), to)
+    def iota(out, pattern, base, join=None, step=0):
+        if out.name in ("pi", "oi"):
+            return mark("g", g.iota(out, pattern, base, step), join)
+        return mark("g", g.iota(out, pattern, base, step, allow_small_or_imprecise_dtypes=True), join)
+
+    def mx(out, a, b):
+        return mark("p", PE.matmul_mx(out, a[0], a[1], b[0], b[1], True, True))
+
+    def dma(q, out, in_, name):
+        return mark(q, queue[q].dma_start(out, in_), None, name, 16)
 
     def cols(q, a, b):
         return (q[0][:, a:b], q[1][:, a:b])
 
-    def elem(tile, b, h):
-        return tile[:, 4 * H * h + b:4 * H * (h + 1):4]
+    def elem(tile, b, a, e):
+        return tile[:, 4 * a + b:4 * e:4]
 
-    r_col, x_col, r1_col, sc_col, sc8_col, scu_col = (T.pf[:, j:j + 1] for j in range(6))
-    win = [T["win%d" % b] for b in range(4)]
+    r_col, x_col, q_col, t_col, r1_col, q1_col, sc_col, sc4_col, zb_col = (T.pf[:, j:j + 1] for j in range(9))
     bank = [T[n] for n in BANKS]
-    pq, eq, wq = (T.pq, T.ps), (T.eq, T.es), (T.wq, T.wp)
+    eq, wq, zq = (T.eq, T.es), (T.wq, T.wp), (T.zq, T.zs)
+    rows16, even32, odd32, sign16 = (cols((T.pq, T.ps), 128 * j, 128 * j + 128) for j in range(4))
+    xqs = [(T["xq%d" % t], T["xs%d" % t]) for t in range(4)]
 
-    sig(SY.dma_start(T.x0[:], T.x[:]), "lx", 16)
-    sig(S.dma_start(T.ut[:], T.u[:]), "lu", 16)
-    wait("y", "lx")
-    sig(SY.dma_start(T.wq[:].bitcast(dt.uint8), T.wc[:]), "lw", 16)
-    sig(SY.dma_start(T.wp[:], T.ws[:]), "lw", 16)
-    sig(SY.dma_start(T.vt[:], T.v[:]), "lv", 16)
+    def thresholds(k, w):
+        wait("s", act(k[:, 0:NB], w, AF.Identity, bias=MAGIC, scale=1.0 / 512))
+        wait("s", act(k[:, NB:2 * NB], k[:, 0:NB], AF.Identity, bias=-512.0 * MAGIC, scale=512.0))
+        return act(k[:, 2 * NB:3 * NB], k[:, NB:2 * NB], AF.Identity, bias=257.5, scale=GROW)
 
-    sig(g.iota(T.pi[:, 0:1], [[0, 1]], 0, 1), "g0")
-    iota(T.c32[:], [[1, 34]], 0, "g0")
+    def picks(a, e):
+        return copy(T.pq[:, a:e].bitcast(dt.uint32), T.uq[:].bitcast(dt.uint32).indirect(T.off[:, a // 16:e // 16]))
+
+    def holds(cs):
+        m = None
+        for c in cs:
+            m = act(T.hold[:, AT[c + 1] - 32:AT[c + 1] + 1], T.p33[:, 0:33], AF.Identity, m, bias=1.0)
+        return m
+
+    lu = dma("s", T.ut[:], T.u[:], "lu")
+    lx = dma("y", T.x0[:], T.x[:], "lx")
+    wait("y", lx)
+    dma("y", T.wq[:].bitcast(dt.uint8), T.wc[:], "lw")
+    lw = dma("y", T.wp[:], T.ws[:], "lw")
+    lv = dma("y", T.vt[:], T.v[:], "lv")
+
+    g0 = iota(T.c32[:], [[1, 34]], 0, iota(T.pi[:, 0:1], [[0, 1]], 0, None, 1))
+    g1 = None
     for j, (pattern, base) in enumerate((([[16, 8]], 0), ([[32, 4], [0, 2]], 0), ([[32, 4], [0, 2]], 16), ([[16, 8]], 1))):
-        sig(g.iota(T.oi[:, 8 * j:8 * j + 8], pattern, base, 0), "g1")
-    iota(T.inc[:, 0:2 * B0], [[32, B0], [0, 2]], 33, "g2")
-    iota(T.jr[:], [[-32, NS // 2], [0, 2]], 1 + KAPPA0 - J[2 * B0], "g2")
-    fill(T.zb[:], 0.0)
-    fill(T.gr[:], GROW)
-    fill(T.ones[:], 1.0, "one")
-    fill(T.hold[:], 1.0, "hd")
-    wait("v", "v")
-    scan(T.wb[:], T.gr[:], T.zb[:, 0:STEPS], W0, OP.mult, OP.add, "wb")
-    wait("v", "g0")
-    ts(T.pi[:, 1:2], T.pi[:, 0:1], 15, OP.bitwise_and)
-    ts(T.pi[:, 2:3], T.pi[:, 0:1], 31, OP.bitwise_and)
-    fill(T.inc[:, 2 * B0:NB], float(LEN[NB - 1] + 1), "va")
-    fill(T.inc[:, NB:32], 0.0, "va")
-    wait("v", "v")
-    sig(V.tensor_copy(T.pf[:, 0:2], T.pi[:, 1:3]), "v")
-    wait("v", "g1")
-    sig(V.tensor_copy(T.off[:], T.oi[:]), "of")
-    wait("v", "v")
-    ts(T.p33[:, 0:32], T.c32[:, 0:32], x_col, OP.is_equal, 1.0 / TINY, OP.mult, "p33")
-    fill(T.p33[:, 32:34], -1.0, "p33")
-    ts(r1_col, r_col, 1.0, OP.add, to="vb")
-    ts(sc_col, r_col, 15.0, OP.is_equal, 2.0 ** -40, OP.max, "vb")
-    ts(T.rep[:], T.zb[:, 0:NB], r_col, OP.add, to="w16")
-    wait("v", "lu")
-    quant(T.uq[:], T.us[:], T.ut[:], "uq")
-    wait("v", "vb")
-    ts(T.w16[:, 16:32], T.c32[:, 0:16], r1_col, OP.is_gt, to="vc")
-    ts(T.w16[:, 32:48], T.c32[:, 0:16], r1_col, OP.is_equal, 2.0 ** 40, OP.mult, "vc")
-    wait("v", "uq", "of")
-    sig(V.tensor_copy(T.pq[:].bitcast(dt.uint32), T.uq[:].bitcast(dt.uint32).indirect(T.off[:])), "pk")
-    wait("v", "vc")
-    tt(T.w16[:, 0:16], T.w16[:, 16:32], T.w16[:, 32:48], OP.add, "w16")
-    magic = 1.5 * 2.0 ** 23
-    wait("s", "wb")
-    act(T.yb[:], T.wb[:], AF.Identity, "s", bias=magic, scale=1.0 / 512)
-    wait("s", "s")
-    act(T.nb[:], T.yb[:], AF.Identity, "s", bias=-512.0 * magic, scale=512.0)
-    wait("s", "s")
-    act(T.b1[:], T.nb[:], AF.Identity, "b1", bias=257.5, scale=GROW)
-    wait("s", "uq", "of")
-    act(T.ps[:], T.us[:].indirect(T.off[:]), AF.Copy, "pks")
-    wait("s", "w16")
-    act(T.wn[:], T.w16[:, 0:16].indirect(T.rep[:]), AF.Copy, "wn")
-    wait("s", "p33", "hd")
-    for c in reversed(range(NB)):
-        act(T.hold[:, AT[c + 1] - 32:AT[c + 1] + 1], T.p33[:, 0:33], AF.Identity, "hp", bias=1.0)
-    wait("g", "one")
-    for b in range(4):
-        if b == 2:
-            iota(T.cmod[:], [[0, NB], [1, 16]], 0, "g3")
-        sig(g.affine_select(T.et[:, 512 * b:512 * b + 512], T.ones[:], [[-1, 128], [1000, 4]], OP.is_equal, 0.0, -1000 * b, 1), "et")
-    wait("v", "b1", "va", "g2")
-    scan(T.kr[:], T.wb[:, 1:C + 1], T.b1[:, 0:C], 0.0, OP.max, OP.subtract, "va")
-    scan(T.ends[:], T.inc[:], T.zb[:, 0:32], -1.0, OP.add, OP.add, "vb")
-    wait("v", "va")
-    turn(T.krt[:], T.kr[:], "va")
-    wait("v", "lx")
-    quant(T.xq0[:], T.xs0[:], T.x0[:], "xq0")
-    wait("v", "va", "vb", "wn")
-    tt(T.st[:], T.jr[:], T.krt[:, 16 * 2 * B0:C:16], OP.subtract, "va")
-    scan(T.ew[:], T.wn[:, 0:32], T.ends[:], 0.0, OP.mult, OP.add, "vb")
-    ts(T.acc[:, 0:2 * B0], T.krt[:, 0:16 * 2 * B0:16], -UNIT, OP.mult, (1 + KAPPA0) * UNIT, OP.add)
-    wait("v", "va")
-    ts(T.sg[:, 0:NS * SW:SW], T.st[:], -8.0, OP.add, to="va")
-    fill(T.acc[:, NB:32], 0.0)
-    wait("v", "va", "vb")
-    tt(T.sg[:, 1:NS * SW:SW], T.st[:], T.sg[:, 0:NS * SW:SW], OP.subtract, "st")
-    ts(T.eo[:], T.ew[:, 15:32:16], sc_col, OP.mult)
-    fill(T.cmp[:, AT[NB - 1] - 1:AT[NB]:LEN[NB - 1] + 1], 0.0)
+        g1 = iota(T.oi[:, 8 * j:8 * j + 8], pattern, base, g1)
+    g2 = iota(T.c16[:], [[0, 2], [1, 16]], 0)
+    g2 = iota(T.inc[:, 0:2 * B0], [[32, B0], [0, 2]], 33, g2)
+    g2 = iota(T.inc[:, 2 * B0:32], [[0, 32 - 2 * B0]], LEN[NB - 1] + 1, g2)
+    g2 = iota(T.jr[:, 0:2 * B0], [[0, 2 * B0]], 1 + KAPPA0, g2)
+    g2 = iota(T.jr[:, 2 * B0:NB], [[-32, NS // 2], [0, 2]], 1 + KAPPA0 - J[2 * B0], g2)
+    g3 = iota(T.c4[:], [[0, 4], [1, 4]], 0)
+    gz = iota(T.zb[:], [[0, 512]], 0)
+
+    def unit_tile(b, join=None):
+        wait("g", gz)
+        return mark("g", g.affine_select(T.et[:, 512 * b:512 * b + 512], T.zb[:], [[-1, 128], [1000, 4]], OP.not_equal,
+                                         1.0, -1000 * b, 1), join)
+
+    et = unit_tile(0)
+    grow = fill(T.mul[:], GROW)
+    p33 = fill(T.p33[:, 32:34], -1.0)
+    wait("v", g0)
+    m = ts(T.pi[:, 1:2], T.pi[:, 0:1], 15, OP.bitwise_and)
+    m = ts(T.pi[:, 2:3], T.pi[:, 0:1], 31, OP.bitwise_and, join=m)
+    m = ts(T.pi[:, 3:4], T.pi[:, 0:1], 15, OP.bitwise_and, 2, OP.arith_shift_right, m)
+    m = ts(T.pi[:, 4:5], T.pi[:, 0:1], 3, OP.bitwise_and, join=m)
+    wait("v", grow)
+    wb = scan(T.wb[:], T.mul[:], T.mul[:], W0, OP.mult, OP.max)
+    wait("v", m)
+    pf = copy(T.pf[:, 0:4], T.pi[:, 1:5])
+    wait("v", wb)
+    wt = turn(T.wt[:], T.wb[:, 0:C])
+    wait("v", pf)
+    p33 = ts(T.p33[:, 0:32], T.c32[:, 0:32], x_col, OP.is_equal, 1.0 / TINY, OP.mult, p33)
+    pf = ts(T.pf[:, 4:6], T.pf[:, 0:3:2], 1.0, OP.add)
+    pf = ts(sc_col, r_col, 15.0, OP.is_equal, 2.0 ** -40, OP.max, pf)
+    ones = fill(T.hold[:], 1.0)
+    wait("s", wt)
+    ka = [act(T.ka[:, 3 * NB:4 * NB], T.wt[:, 0:C:16], AF.Copy, scale=GROW), thresholds(T.ka, T.wt[:, 0:C:16])]
+    wait("s", p33, ones)
+    hp_low = holds(range(CA))
+    wait("v", g1, g2, pf)
+    of = copy(T.off[:], T.oi[:])
+    m = ts(T.w32[:, 32:64], T.c16[:], r1_col, OP.is_gt)
+    m = ts(T.w32[:, 64:96], T.c16[:], r1_col, OP.is_equal, 2.0 ** 40, OP.mult, m)
+    ends = scan(T.ends[:], T.inc[:], T.c16[:], -1.0, OP.add, OP.max)
+    wait("v", ka)
+    kr = tt(T.kr[:], T.ka[:, 2 * NB:3 * NB], T.ka[:, 3 * NB:4 * NB], OP.subtract)
+    wait("v", lu)
+    uq = quant((T.uq, T.us), 0, 128, T.ut)
+    wait("v", m)
+    w16 = tt(T.w32[:, 0:32], T.w32[:, 32:64], T.w32[:, 64:96], OP.add)
+    wait("v", kr)
+    st = tt(T.st[:], T.jr[:], T.kr[:], OP.add)
+    once = fill(T.cmp[:, AT[NB - 1] - 1:AT[NB]:LEN[NB - 1] + 1], 0.0)
+    once = fill(T.cmp[:, AT[CA - 1] - 1:AT[CA]:LEN[CA - 1] + 1], 0.0, once)
+    once = fill(T.acc[:, NB:32], 0.0, once)
+    wait("v", uq, of)
+    pk0 = picks(0, 256)
+    wait("s", uq, of)
+    pks = None
+    for a, e in ((0, 256), (256, 384), (384, 512)):
+        pks = act(T.ps[:, a:e], T.us[:].indirect(T.off[:, a // 16:e // 16]), AF.Copy, pks)
+    hp_high = holds(range(CA, NB))
+    wait("v", w16, ends, st)
+    ew = scan(T.ew[:], T.w32[:, 0:32], T.ends[:], 0.0, OP.mult, OP.add)
+    m = ts(T.sg[:, 0:NS * SW:SW], T.st[:, 2 * B0:NB], -8.0, OP.add)
+    once = ts(T.acc[:, 0:2 * B0], T.st[:, 0:2 * B0], UNIT, OP.mult, join=once)
+    pk1 = picks(256, 384)
+    wait("v", m, ew)
+    sums = tt(T.sg[:, 1:NS * SW:SW], T.st[:, 2 * B0:NB], T.sg[:, 0:NS * SW:SW], OP.subtract)
+    once = ts(T.eo[:], T.ew[:, 15:32:16], sc_col, OP.mult, float(AT[NB] - 1), OP.min, once)
 
     def later_constants():
-        wait("v", "g3")
-        ts(T.ca[:], T.c32[:, 0:16], r_col, OP.is_gt, GROW - 1.0, OP.mult, "vb")
-        ts(T.cb[:], T.c32[:, 0:16], r_col, OP.not_equal, 2.0 ** -12, OP.max, "vb")
-        ts(sc8_col, sc_col, 2.0 ** 12 * UNIT, OP.mult, to="vb")
-        scan(T.kk[:], T.wn[:], T.b1[:, 0:C], 0.0, OP.mult, OP.add, "vb")
-        ts(T.rz[:], T.cmod[:], 0.0, OP.not_equal)
-        ts(T.rp[:], T.zb[:, 0:C], 0.0, OP.add)
-        ts(T.mul[:, 16:STEPS], T.zb[:, 16:STEPS], GROW, OP.add)
-        ts(T.mb[:, C:C + 1], T.zb[:, 0:1], LAST * UNIT, OP.add)
-        ts(T.stp[:, 0:1], T.zb[:, 0:1], 0.0, OP.add)
-        ts(T.stp[:, STEPS - 1:STEPS], T.zb[:, 0:1], LEAVE * UNIT, OP.add)
-        ts(scu_col, sc_col, 1.0 / UNIT, OP.mult)
-        wait("v", "vb")
-        tt(T.mul[:, 0:16], T.ca[:], T.cb[:], OP.add)
-        ts(T.k0[:], T.kk[:, 15:C:16], sc8_col, OP.mult, -2.0 ** 12 * UNIT, OP.add)
+        wait("v", g3, wn)
+        kk = scan(T.kk[:], T.wn[:], T.wb[:, 0:C], 0.0, OP.mult, OP.add)
+        a = ts(T.w4[:, 16:32], T.c4[:], q1_col, OP.is_gt)
+        a = ts(T.w4[:, 32:48], T.c4[:], q1_col, OP.is_equal, 2.0 ** 40, OP.mult, a)
+        a = ts(T.ca[:], T.c32[:, 0:16], r_col, OP.is_gt, GROW - 1.0, OP.mult, a)
+        a = ts(T.cb[:], T.c32[:, 0:16], r_col, OP.not_equal, 2.0 ** -12, OP.max, a)
+        a = ts(sc4_col, q_col, 3.0, OP.is_equal, 2.0 ** -40, OP.max, a)
+        b = ts(T.rp[:], T.zb[:, 0:C], 0.0, OP.add)
+        b = ts(T.mb[:, C:C + 1], T.zb[:, 0:1], LAST * UNIT, OP.add, join=b)
+        b = ts(T.stp[:, 0:STEPS:STEPS - 1], T.c32[:, 0:2], LEAVE * UNIT, OP.mult, join=b)
+        wait("v", a)
+        w4 = tt(T.w4[:, 0:16], T.w4[:, 16:32], T.w4[:, 32:48], OP.add)
+        b = tt(T.mul[:, 0:16], T.ca[:], T.cb[:], OP.add, b)
+        b = ts(sc4_col, sc4_col, 4.0 / UNIT, OP.mult, join=b)
+        b = ts(zb_col, t_col, -4.0 * NAME0, OP.add, join=b)
+        wait("s", kk)
+        wait("s", act(T.kb[:, 3 * NB:4 * NB], T.kk[:, 15:C:16], AF.Copy, scale=sc_col))
+        wait("s", thresholds(T.kb, T.kb[:, 3 * NB:4 * NB]))
+        k0 = act(T.k0[:], T.kb[:, 2 * NB:3 * NB], AF.Identity, bias=-2.0 ** 12 * UNIT, scale=2.0 ** 12 * UNIT)
+        wait("s", w4)
+        return b, k0, act(T.wn4[:], T.w4[:, 0:16].indirect(T.rep[:]), AF.Copy)
+
+    def own(c):
+        return T.tc[:, 16 * c:16 * c + 1]
+
+    def compare(c, rows, width, join=None):
+        n = min(LEN[c] + 1, width - J[c])
+        return ts(T.cmp[:, AT[c]:AT[c] + n], rows[:, J[c]:J[c] + n], own(c), OP.is_ge, TINY * UNIT, OP.mult, join)
+
+    def count(a, b, join=None):
+        return scan(T.cnt[:, AT[a]:AT[b]], T.hold[:, AT[a]:AT[b]], T.cmp[:, AT[a]:AT[b]], 0.0, OP.mult, OP.add, join)
+
+    def first_scores(xq, made):
+        wait("p", pk0, pk1, pks, made)
+        return [mx(bank[j][:, 0:A], side, cols(xq, 0, A)) for j, side in enumerate((rows16, even32, odd32))]
+
+    wait("v", lx)
+    xa = quant(xqs[0], 0, A, T.x0)
+    first = first_scores(xqs[0], xa)
+    xb = quant(xqs[0], A, C, T.x0)
+    pk2 = picks(384, 512)
+    wait("v", first[0])
+    tl = turn(T.tc[:, 0:A], bank[0][:, 0:A])
 
     for t, mask_t in enumerate(ROUNDS):
         peer = T.cores[rank ^ mask_t]
         rid, pid = topo.addr(peer)[0:2]
         mask, ne = topo.mask(core, peer), len(topo.engines(core, peer))
-        xq = (T["xq%d" % t], T["xs%d" % t])
+        xq, xn = xqs[t], xqs[t + 1]
         aq = (T["aq%d" % t], T["as%d" % t])
         snd, land = T["snd%d" % t], T["land%d" % t]
+        win, nxt = T["win%d" % (t % 2)], T["win%d" % ((t + 1) % 2)]
         last = t == len(ROUNDS) - 1
 
-        wait("g", "xq%d" % t)
-        g.remote_dma(aq[0][:].bitcast(dt.uint8), xq[0][:].bitcast(dt.uint8), T.sem["aq%d" % t], T.sem.left, pid, rid, mask)
-        g.remote_dma(aq[1][:], xq[1][:], T.sem["aq%d" % t], T.sem.left, pid, rid, mask)
-        cnt["aq%d" % t] += 2 * ne
-        cnt["left"] += 2 * ne
-        if t == 0:
-            iota(T.io1[:], [[1, C]], NAME0, "g3")
+        def send(out, in_, to):
+            g.remote_dma(out, in_, T.sem[to], T.sem.left, pid, rid, mask)
+            cnt[to] += ne
+            cnt["left"] += ne
+            return (to, cnt[to], {})
+
+        wait("g", xa, xb)
+        send(aq[0][:, 0:EARLY].bitcast(dt.uint8), xq[0][:, 0:EARLY].bitcast(dt.uint8), "aq%d" % t)
 
         ju = max(J)
-        wait("p", "pk", "pks", "xq%d" % t)
-        mx(bank[0][:, 0:C - UP], cols(pq, 0, 128), cols(xq, UP, C), "mu")
-        mx(bank[1][:, 0:ju], cols(pq, 128, 256), cols(xq, 0, ju), "mes")
-        mx(bank[3][:, 0:UP], cols(pq, 0, 128), cols(xq, 0, UP), "ml")
-        mx(bank[2][:, 0:C], cols(pq, 128, 256), cols(xq, 0, C), "mev")
-        mx(bank[4][:, 0:ju], cols(pq, 256, 384), cols(xq, 0, ju), "mos")
-        mx(bank[5][:, 0:C], cols(pq, 256, 384), cols(xq, 0, C), "mov")
-        mx(bank[6][:, 0:C], cols(pq, 384, 512), cols(xq, 0, C), "mw")
+        wait("p", xb)
+        mu = mx(bank[4][:, 0:C - A], rows16, cols(xq, A, C))
+        mes = mx(bank[5][:, 0:ju], even32, cols(xq, 0, ju))
+        mev = mx(bank[6][:, 0:C], even32, cols(xq, 0, C))
+        mos = mx(bank[7][:, 0:ju], odd32, cols(xq, 0, ju))
+        wait("p", tl, pk2)
+        mov = mx(bank[0][:, 0:C], odd32, cols(xq, 0, C))
+        mw = mx(bank[3][:, 0:C], sign16, cols(xq, 0, C))
 
-        wait("v", "mu", "v")
-        turn(T.tc[:, UP:C], bank[0][:, 0:C - UP], "tu")
-        wait("v", "ml")
-        turn(T.tc[:, 0:UP], bank[3][:, 0:UP], "tl")
-
-        def own(c):
-            return T.tc[:, 16 * c:16 * c + 1]
+        wait("v", tl, first[1], first[2])
+        low = None
+        for c in range(CA):
+            low = compare(c, bank[1 + c % 2], A, low)
+        wait("v", mu)
+        tu = turn(T.tc[:, A:C], bank[4][:, 0:C - A])
 
         order = [c for h in range(2) for c in reversed(range(2 * B0 + h, NB, 2))]
-        wait("s", "tu", "mes")
+        wait("s", tu, mes)
+        signs, summed = [], None
         for n in range(NS + 1):
             if n < NS:
                 c = order[n]
                 if c % 2:
-                    wait("s", "mos")
+                    wait("s", mos)
                 a = SW * (c - 2 * B0)
-                act(T.sg[:, a + 2:a + 2 + J[c]], bank[1 + 3 * (c % 2)][:, 0:J[c]], AF.Sign, "sa" if n % 2 else "sb",
-                    bias=own(c), scale=-1.0)
+                signs.append(act(T.sg[:, a + 2:a + 2 + J[c]], bank[5 + 2 * (c % 2)][:, 0:J[c]], AF.Sign, bias=own(c), scale=-1.0))
             if n > 0:
                 c = order[n - 1]
                 a = SW * (c - 2 * B0)
-                wait("s", "sb" if n % 2 else "sa", "st")
-                act(T.sr[:, a:a + 2 + J[c]], T.sg[:, a:a + 2 + J[c]], AF.Relu, "sr", scale=UNIT, accum_out=T.acc[:, c:c + 1])
+                wait("s", signs[n - 1], sums)
+                summed = act(T.sr[:, a:a + 2 + J[c]], T.sg[:, a:a + 2 + J[c]], AF.Relu, summed, scale=UNIT,
+                             accum_out=T.acc[:, c:c + 1])
 
-        def compare(c, to):
-            n = min(LEN[c] + 1, C - J[c])
-            ts(T.cmp[:, AT[c]:AT[c] + n], bank[2 + 3 * (c % 2)][:, J[c]:J[c] + n], own(c), OP.is_ge, TINY * UNIT, OP.mult, to)
-
-        def count(a, b, to):
-            scan(T.cnt[:, AT[a]:AT[b]], T.hold[:, AT[a]:AT[b]], T.cmp[:, AT[a]:AT[b]], 0.0, OP.mult, OP.add, to)
-
-        wait("v", "tu", "mev")
-        for c in range(2 * B0, NB, 2):
-            compare(c, "va")
-        wait("v", "tl")
-        for c in range(0, 2 * B0, 2):
-            compare(c, "vc" if c < 8 else "vb")
-        wait("v", "mov")
-        for c in range(2 * B0 + 1, NB, 2):
-            compare(c, "va")
-        for c in range(9, 2 * B0, 2):
-            compare(c, "vb")
-        wait("v", "va", "hp")
-        count(2 * B0, NB, "vd")
-        for c in range(1, 8, 2):
-            compare(c, "vc")
-        wait("v", "vb")
-        count(8, 2 * B0, "vd")
-        wait("v", "vc")
-        count(0, 8, "vd")
         if t == 0:
-            ts(T.cap[:], T.zb[:, 0:C], CAP * C * UNIT, OP.add, to="ve")
-            ts(T.cum[:, 0:1], T.zb[:, 0:1], 0.0, OP.add, to="ve")
-        wait("v", "mw")
-        ts(T.want[:], bank[6][:, 0:C], 0.0, OP.is_gt, C * UNIT, OP.mult, "ve")
-        wait("v", "vd", "sr", "v")
-        tt(snd[:], T.cnt[:, 0:AT[NB]].indirect(T.eo[:]), T.acc[:], OP.subtract, "sn%d" % t)
-        wait("g", "sn%d" % t)
-        g.remote_dma(land[:], snd[:, 0:NB], T.sem["at%d" % t], T.sem.left, pid, rid, mask)
-        cnt["at%d" % t] += ne
-        cnt["left"] += ne
+            w16 = [w16, ts(T.rep[:], T.c32[:, 0:NB], 0.0, OP.mult, r_col, OP.add)]
+        wait("v", low, once, hp_low)
+        counted = count(0, CA)
+        wait("v", tu, mev)
+        high = None
+        for c in range(CA, NB, 2):
+            high = compare(c, bank[6], C, high)
+        wait("v", mov)
+        cut = 2 * B0 - 2
+        for c in list(range(CA + 1, cut, 2)) + list(range(2 * B0 + 1, NB, 2)):
+            high = compare(c, bank[0], C, high)
+        final = compare(cut + 1, bank[0], C)
+        wait("v", high, hp_high)
+        counted = count(CA, cut, counted)
+        counted = count(2 * B0, NB, counted)
+        wait("v", final)
+        counted = count(cut, 2 * B0, counted)
+        wait("v", mw)
+        want = ts(T.want[:], bank[3][:, 0:C], 0.0, OP.is_gt, C * UNIT, OP.mult)
+        wait("v", counted, summed)
+        sn = tt(snd[:], T.cnt[:, 0:AT[NB]].indirect(T.eo[:]), T.acc[:], OP.subtract)
+        wait("g", sn)
+        at = send(land[:], snd[:, 0:NB], "at%d" % t)
+        send(aq[0][:, EARLY:C].bitcast(dt.uint8), xq[0][:, EARLY:C].bitcast(dt.uint8), "aq%d" % t)
+        arrived = send(aq[1][:], xq[1][:], "aq%d" % t)
 
-        wait("v", "ve")
-        scan(T.cum[:, 1:C + 1], T.want[:], T.cap[:], 0.0, OP.add, OP.min, "ve")
         if t == 0:
-            wait("s", "lx")
-            for b in range(4):
-                act(win[b][:, 0:C], T.x0[:, b:4 * C:4], AF.Copy, "dun", scale=32.0)
-            wait("v", "et", "g3")
-            quant(T.eq[:], T.es[:], T.et[:], "eq")
-            ts(T.iou[:], T.io1[:], UNIT, OP.mult, to="vc")
-        wait("v", "ve")
-        scan(T.take[:], T.cum[:, 1:C + 1], T.cum[:, 0:C], 0.0, OP.max, OP.subtract, "ve")
+            for b in range(1, 4):
+                et = unit_tile(b, et)
+            wait("s", w16, gz)
+            rz = act(T.rz16[:], T.c16[:, 0:16], AF.Sign)
+            wn = act(T.wn[:], T.w32[:, 0:16].indirect(T.rep[:]), AF.Copy)
+            wait("s", rz)
+            rz = act(T.rz[:], T.rz16[:].indirect(T.rep[:, 0:10]), AF.Copy)
+            wait("v", gz)
+            un = ts(T.un[:], T.zb[:, 0:C], UNIT, OP.add)
+            want = ts(T.cap[:], T.zb[:, 0:C], CAP * C * UNIT, OP.add, join=want)
+            want = ts(T.cum[:, 0:1], T.zb[:, 0:1], 0.0, OP.add, join=want)
+            wait("v", un)
+            iou = scan(T.iou[:], T.un[:], T.zb[:, 0:C], (NAME0 - 1) * UNIT, OP.add, OP.add)
+        wait("v", want)
+        cum = scan(T.cum[:, 1:C + 1], T.want[:], T.cap[:], 0.0, OP.add, OP.min)
         if t == 0:
-            later_constants()
-        wait("v", "ve", "vc")
-        turn(T.tkt[:], T.take[:], "va")
-        scan(T.val[:], T.take[:], T.iou[:], 2.0, OP.min, OP.add, "ve")
-        wait("v", "va", "sn%d" % t)
-        tt(T.hi[:], snd[:, 0:NB], T.tkt[:, 0:C:16], OP.add, "va")
-        tt(T.lo[:], snd[:, 0:NB], T.tkt[:, 0:C:16], OP.subtract, "va")
-        wait("p", "eq", "aq%d" % t, "tu", "tl")
-        for b, k in enumerate((7, 0, 3, 1)):
-            if k == 1:
-                wait("p", "sa", "sb")
-            mx(bank[k][:, 0:C], cols(eq, 128 * b, 128 * b + 128), cols(aq, 0, C), "md%d" % b)
-            wait("s", "md%d" % b)
-            act(win[b][:, C:2 * C], bank[k][:, 0:C], AF.Copy, "dun", scale=32.0)
+            made, k0, wn4 = later_constants()
+            wait("s", lx)
+            window = act(win[:, 0:4 * C], T.x0[:], AF.Copy, scale=32.0)
+        wait("v", cum)
+        take = scan(T.take[:], T.cum[:, 1:C + 1], T.cum[:, 0:C], 0.0, OP.max, OP.subtract)
+        wait("v", take)
+        wait("v", turn(T.tkt[:], T.take[:]), sn)
+        m = tt(T.hi[:], snd[:, 0:NB], T.tkt[:, 0:C:16], OP.add)
+        lo = tt(T.lo[:], snd[:, 0:NB], T.tkt[:, 0:C:16], OP.subtract)
 
-        wait("v", "at%d" % t, "va", "v")
-        tt(T.mid[:], land[:], T.hi[:], OP.min)
-        wait("v", "v")
-        tt(T.rp[:, H:C:16], T.mid[:, 10:NB], T.lo[:, 10:NB], OP.max, "va")
-        tt(T.rp[:, 0:H:16], T.mid[:, 0:10], T.lo[:, 0:10], OP.max, "vb")
-        for a, to in ((H, "va"), (0, "vb")):
-            wait("v", to)
-            scan(T.bc[:, a:a + H], T.rz[:, 0:H], T.rp[:, a:a + H], 0.0, OP.mult, OP.add, to)
-        for a, to in ((H, "va"), (0, "vb")):
-            wait("v", to)
-            turn(T.mb[:, a:a + H], T.bc[:, a:a + H], to)
-        for a, to in ((H, "va"), (0, "vb")):
-            wait("v", to)
-            scan(T.stp[:, a + 1:a + H + 1], T.mb[:, a:a + H], T.mb[:, a + 1:a + H + 1], 0.0, OP.min, OP.subtract, to)
+        wait("v", at, m)
+        m = tt(T.mid[:], land[:], T.hi[:], OP.min)
+        wait("v", iou)
+        val = scan(T.val[:], T.take[:], T.iou[:], 2.0, OP.min, OP.add)
+        wait("v", m, lo, made, rz)
+        halves = (H, 0)
+        m = [tt(T.rp[:, a:a + H:16], T.mid[:, a // 16:a // 16 + 10], T.lo[:, a // 16:a // 16 + 10], OP.max) for a in halves]
+        for j, a in enumerate(halves):
+            wait("v", m[j])
+            m[j] = scan(T.bc[:, a:a + H], T.rz[:], T.rp[:, a:a + H], 0.0, OP.mult, OP.add)
+        for j, a in enumerate(halves):
+            wait("v", m[j])
+            m[j] = turn(T.mb[:, a:a + H], T.bc[:, a:a + H])
+        if t == 0:
+            wait("v", lv)
+            vq = quant((T.vq, T.vs), 0, 128, T.vt)
+        for j, a in enumerate(halves):
+            wait("v", m[j])
+            m[j] = scan(T.stp[:, a + 1:a + H + 1], T.mb[:, a:a + H], T.mb[:, a + 1:a + H + 1], 0.0, OP.min, OP.subtract)
 
-        def order_scan(k, to):
-            scan(T.so[:, STEPS * k + 16 * k:STEPS * (k + 1)], T.stp[:, 16 * k:STEPS], T.mul[:, 0:STEPS - 16 * k],
-                 T.k0[:, k:k + 1], OP.add, OP.mult, to)
+        def order_scans(ks, join=None):
+            for k in ks:
+                join = scan(T.so[:, STEPS * k + 16 * k:STEPS * (k + 1)], T.stp[:, 16 * k:STEPS], T.mul[:, 0:STEPS - 16 * k],
+                            T.k0[:, k:k + 1], OP.add, OP.mult, join)
+            return join
 
         def places(a, b):
-            ts(T.po[:, a:b], T.so[:, STEPS * (a + 1) - 1:STEPS * b:STEPS], 1.0 / (UNIT * GROW), OP.mult, float(H), OP.add, "vc")
+            return ts(T.po[:, a:b], T.so[:, STEPS * (a + 1) - 1:STEPS * b:STEPS], 1.0 / (UNIT * GROW), OP.mult, float(H), OP.add)
 
-        wait("v", "va")
-        for k in range(11, NB):
-            order_scan(k, "va")
-        wait("v", "vb")
-        order_scan(10, "va")
-        for k in range(0, 5):
-            order_scan(k, "vb")
-        wait("v", "va")
-        places(10, NB)
-        for k in range(5, 10):
-            order_scan(k, "vb")
-        wait("v", "vc", "ve")
-        sig(V.tensor_copy(T.nm[:].indirect(T.po[:, 10:NB]), T.val[:, H:C]), "nm")
-        wait("v", "vb")
-        places(0, 10)
-        wait("v", "vc", "nm")
-        sig(V.tensor_copy(T.nm[:].indirect(T.po[:, 0:10]), T.val[:, 0:H]), "nm")
-        wait("v", "nm")
-        for a, to in ((0, "va"), (H, "vb")):
-            scan(T.ns[:, a:a + H], T.wn[:, 0:H], T.nm[:, a:a + H], 0.0, OP.mult, OP.add, to)
-        for h, to in ((0, "va"), (1, "vb")):
-            wait("v", to)
-            ts(T.zo[:, 10 * h:10 * h + 10], T.ns[:, H * h + 15:H * h + H:16], scu_col, OP.mult, -float(NAME0), OP.add, "zo%d" % h)
-        if last:
-            wait("s", "nm")
-            act(T.odb[:], T.nm[:], AF.Identity, "od", bias=-float(NAME0), scale=1.0 / UNIT)
-            wait("y", "od")
-            for k in range(8):
-                sig(SY.dma_start(T.od[k:k + 1, :], T.odb[16 * k:16 * k + 1, :]), "out", 16)
+        def scatter(a, b, join=None):
+            return copy(T.nm[:].indirect(T.po[:, a:b]), T.val[:, 16 * a:16 * b], join)
 
-        wait("v", "zo0", "dun")
-        wait("s", "zo1", "dun")
-        for b in range(4):
-            ts(elem(T.zt, b, 0), win[b][:].indirect(T.zo[:, 0:10]), 2.0 ** -5, OP.mult, to="zv")
-            act(elem(T.zt, b, 1), win[b][:].indirect(T.zo[:, 10:NB]), AF.Copy, "zg", scale=2.0 ** -5)
-        wait("p", "lw")
-        for h, made in enumerate(("zv", "zg")):
-            wait("v", made)
-            quant(T.zq[:, H * h:H * h + H], T.zs[:, H * h:H * h + H], T.zt[:, 4 * H * h:4 * H * (h + 1)], "zq%d" % h)
-            wait("s", made)
-            wait("p", "zq%d" % h)
-            for b in range(4):
-                j = 4 * h + b
-                act(T.z32[:, H * j:H * j + H], elem(T.zt, b, h), AF.Copy, "z%d" % j, scale=32.0)
-                mx(bank[j][:, 0:H], cols(wq, 128 * b, 128 * b + 128), cols((T.zq, T.zs), H * h, H * h + H), "r%d" % j)
+        wait("v", m[0], k0)
+        upper = order_scans(range(11, NB))
         if t == 0:
-            wait("v", "lv")
-            quant(T.vq[:], T.vs[:], T.vt[:], "vq")
-        for j in range(8):
-            h, b = divmod(j, 4)
-            wait("v", "r%d" % j, "z%d" % j)
-            tt(win[b][:, H * h:H * h + H], bank[j][:, 0:H], T.z32[:, H * j:H * j + H], OP.add, "e%d" % j)
-        for b in range(4):
-            wait("s", "e%d" % b)
-            act(elem(T.xn, b, 0), win[b][:, 0:H], AF.Copy, "xs", scale=2.0 ** -5)
-            wait("v", "e%d" % (4 + b))
-            ts(elem(T.xn, b, 1), win[b][:, H:C], 2.0 ** -5, OP.mult)
-        wait("v", "v", "xs")
-        quant(T["xq%d" % (t + 1)][:], T["xs%d" % (t + 1)][:], T.xn[:], "xq%d" % (t + 1))
+            wait("v", et)
+            eqm = quant(eq, 0, 512, T.et)
+        wait("p", eqm, arrived, sn, want, signs)
+        for b, k in enumerate((4, 5, 6, 7)):
+            wait("s", mx(bank[k][:, 0:C], cols(eq, 128 * b, 128 * b + 128), cols(aq, 0, C)))
+            window = act(elem(win, b, C, 2 * C), bank[k][:, 0:C], AF.Copy, window if b or t == 0 else None, scale=32.0)
+        wait("v", m[1])
+        upper = order_scans([10, 9, 8, 7, 6], upper)
+        m = order_scans([5, 4, 3])
+        wait("v", upper)
+        p = places(6, NB)
+        m = order_scans([2, 1, 0], m)
+        wait("v", p, val)
+        nm = scatter(6, NB)
+        wait("v", m)
+        wait("v", places(0, 6), nm)
+        nm = scatter(0, 6)
+        wait("v", nm, wn4)
+        parts = ((0, A), (A, C))
+        m = [scan(T.ns[:, a:e], T.wn4[:, a:e], T.nm[:, a:e], 0.0, OP.mult, OP.add) for a, e in parts]
+        zo = []
+        for j, (a, e) in enumerate(parts):
+            wait("v", m[j])
+            zo.append(ts(T.zo[:, a // 4:e // 4], T.ns[:, a + 3:e:4], sc4_col, OP.mult, zb_col, OP.add))
+        if last:
+            wait("s", nm)
+            wait("y", act(T.odb[:], T.nm[:], AF.Identity, bias=-float(NAME0), scale=1.0 / UNIT))
+            for k in range(8):
+                dma("y", T.od[k:k + 1, :], T.odb[16 * k:16 * k + 1, :], "out")
 
-    wait("p", "vq", "xq3")
-    mx(bank[0][:, 0:C], (T.vq[:], T.vs[:]), (T.xq3[:], T.xs3[:]), "my")
-    wait("y", "xq3")
-    wait("s", "xq3")
-    sig(SY.dma_start(T.oc[:], T.xq3[:].bitcast(dt.uint8)), "out", 16)
+        zv, zs = [], []
+        for j, (a, e) in enumerate(parts):
+            c = GATHER[j]
+            wait("s", zo[j], window)
+            zs.append(act(T.zt[:, 4 * c:4 * e], win[:].indirect(T.zo[:, c // 4:e // 4]), AF.Copy, scale=2.0 ** -5))
+            wait("v", zo[j], window)
+            zv.append(ts(T.zt[:, 4 * a:4 * c], win[:].indirect(T.zo[:, a // 4:c // 4]), 2.0 ** -5, OP.mult))
+
+        def products(j, made):
+            a, e = parts[j]
+            wait("p", made)
+            return [mx(bank[4 * j + b][:, 0:e - a], cols(wq, 128 * b, 128 * b + 128), cols(zq, a, e)) for b in range(4)]
+
+        def add(j, b):
+            a, e = parts[j]
+            wait("v", r[j][b], z32[j])
+            m = tt(elem(nxt, b, a, e), bank[4 * j + b][:, 0:e - a], elem(T.z32, b, a, e), OP.add)
+            wait("s", m)
+            return act(elem(T.xn, b, a, e), elem(nxt, b, a, e), AF.Copy, scale=2.0 ** -5)
+
+        wait("p", lw, window)
+        wait("v", zv[0], zs[0])
+        r = [products(0, quant(zq, 0, A, T.zt))]
+        z32 = [ts(T.z32[:, 0:4 * A], T.zt[:, 0:4 * A], 32.0, OP.mult)]
+        wait("s", zs[1])
+        c = GATHER[1]
+        m = act(T.z32[:, 4 * c:4 * C], T.zt[:, 4 * c:4 * C], AF.Copy, scale=32.0)
+        wait("v", zv[1])
+        z32.append([m, ts(T.z32[:, 4 * A:4 * c], T.zt[:, 4 * A:4 * c], 32.0, OP.mult)])
+        wait("v", zs[1])
+        r.append(products(1, quant(zq, A, C, T.zt)))
+        na = [add(0, b) for b in range(4)]
+        nb = [add(1, b) for b in range(3)]
+        wait("v", na)
+        xa = quant(xn, 0, A, T.xn)
+        if not last:
+            first = first_scores(xn, xa)
+        nb.append(add(1, 3))
+        if not last:
+            wait("v", first[0])
+            tl = turn(T.tc[:, 0:A], bank[0][:, 0:A])
+        wait("v", nb)
+        xb = quant(xn, A, C, T.xn)
+
+    wait("p", vq, xa)
+    my = mx(bank[0][:, 0:A], (T.vq[:], T.vs[:]), cols(xn, 0, A))
+    wait("y", xa)
+    dma("y", T.oc[:, 0:4 * A], T.xq3[:, 0:A].bitcast(dt.uint8), "out")
+    wait("s", my)
+    wait("y", act(T.ysb[:, 0:A], bank[0][:, 0:A], AF.Copy))
+    dma("y", T.y[:, 0:A], T.ysb[:, 0:A], "out")
+    wait("p", xb)
+    wait("v", mx(bank[1][:, 0:C - A], (T.vq[:], T.vs[:]), cols(xn, A, C)))
+    wait("y", copy(T.ysb[:, A:C], bank[1][:, 0:C - A]))
+    dma("y", T.y[:, A:C], T.ysb[:, A:C], "out")
+    wait("s", xa, xb)
+    dma("s", T.oc[:, 4 * A:4 * C], T.xq3[:, A:C].bitcast(dt.uint8), "out")
     for k in range(4):
-        sig(S.dma_start(T.osc[4 * k:4 * k + 4, :], T.xs3[32 * k:32 * k + 4, :]), "out", 16)
-    wait("v", "my")
-    sig(V.tensor_copy(T.ysb[:], bank[0][:, 0:C]), "ys")
-    wait("y", "ys")
-    sig(SY.dma_start(T.y[:], T.ysb[:]), "out", 16)
-    wait("g", *SEMAPHORES)
+        dma("s", T.osc[4 * k:4 * k + 4, :], T.xs3[32 * k:32 * k + 4, :], "out")
+    wait("g", [(n, cnt[n], {}) for n in SEMAPHORES])

@@ -31,23 +31,24 @@ def _ends():
 
 LAST, LEAVE = _ends()
 
-B0 = 7
-OVER = 48
-J = [0] * (2 * B0) + [32 * (c // 2) - OVER for c in range(2 * B0, NB)]
+U = 192
+CU = U // 16
+FS = CU + 1
+J = [0] * FS + [U] * (NB - FS)
 LEN = [32 * (c // 2) + 32 - J[c] for c in range(NB)]
 AT = [sum(LEN[:c]) + c for c in range(NB + 1)]
-SW = max(J) + 2
-NS = NB - 2 * B0
-A = 128
-CA = A // 16
-GATHER = (64, 208)
+SW = U + 2
+NS = NB - FS
+LAG = 2
+PARTS = ((U, C), (0, U))
+GATHER = (256, 80)
 EARLY = 160
 
 X4 = "float8_e4m3fn_x4"
 SCRATCH = {}
 for _dt, _list in (
         ("bfloat16", (("x0", 4 * C), ("xn", 4 * C), ("ut", 512), ("vt", 512), ("et", 2048), ("zt", 4 * C), ("z32", 4 * C),
-                      ("zb", 512), ("rz16", 16), ("rz", H), ("c32", 34), ("c16", 32), ("c4", 16), ("p33", 34),
+                      ("zb", 512), ("rz16", 16), ("rz", C), ("c32", 34), ("c16", 32), ("c4", 16), ("p33", 34),
                       ("w32", 96), ("w4", 48), ("wn", C), ("wn4", C), ("cmp", AT[NB] + 1), ("hold", AT[NB] + 1),
                       ("cnt", AT[NB] + 1), ("sg", NS * SW), ("sr", NS * SW), ("so", NB * STEPS),
                       ("win0", 8 * C), ("win1", 8 * C))),
@@ -72,7 +73,7 @@ for _n in BANKS:
     SCRATCH[_n] = ("psum", [128, 512], "float32")
 
 POOL = ["c%d" % _b for _b in range(130)]
-SEMAPHORES = (POOL + ["lx", "lu", "lv", "lw", "out", "left"]
+SEMAPHORES = (POOL + ["la", "lx", "lu", "lv", "lw", "out", "left"]
               + ["%s%d" % (n, t) for n in ("aq", "at") for t in range(3)])
 
 
@@ -85,43 +86,48 @@ def rank_program(g, core, T, topo):
 
     cnt = {n: 0 for n in SEMAPHORES}
     known = {q: {} for q in queue}
+    calls = {q: 0 for q in queue}
     free = list(POOL)
+    user = {}
 
     def wait(q, *marks):
+        flat = []
         for m in marks:
-            if isinstance(m, list):
-                wait(q, *m)
-            elif known[q].get(m[0], 0) < m[1]:
-                queue[q].wait_ge(T.sem[m[0]], m[1])
-                known[q][m[0]] = m[1]
-                for n, c in m[2].items():
+            flat += [x for y in m for x in (y if isinstance(y, list) else [y])] if isinstance(m, list) else [m]
+        for name, count, done, key in sorted(flat, key=lambda m: -m[2][m[3]]):
+            if known[q].get(key, 0) < done[key]:
+                queue[q].wait_ge(T.sem[name], count)
+                for n, c in done.items():
                     known[q][n] = max(known[q].get(n, 0), c)
 
-    def mark(q, ins, join=None, name=None, n=1):
+    def mark(q, ins, name=None, n=1):
+        key = name or q
         if name is None:
-            name = join[0] if join else [s for s in free if known[q].get(s, 0) == cnt[s]][0]
+            calls[q] += 1
+            name = [s for s in free if s not in user or known[q].get(user[s][0], 0) >= user[s][1]][0]
             free.remove(name)
             free.append(name)
+            user[name] = (q, calls[q])
         ins.then_inc(T.sem[name], n)
         cnt[name] += n
-        return (name, cnt[name], dict(known[q]))
+        return (name, cnt[name], dict(known[q], **{key: calls[q] if key == q else cnt[name]}), key)
 
-    def ts(out, in0, s1, op0, s2=None, op1=None, join=None):
+    def ts(out, in0, s1, op0, s2=None, op1=None):
         if op1 is None:
-            return mark("v", V.tensor_scalar(out, in0, s1, None, op0), join)
-        return mark("v", V.tensor_scalar(out, in0, s1, s2, op0, op1), join)
+            return mark("v", V.tensor_scalar(out, in0, s1, None, op0))
+        return mark("v", V.tensor_scalar(out, in0, s1, s2, op0, op1))
 
-    def tt(out, in0, in1, op, join=None):
-        return mark("v", V.tensor_tensor(out, in0, in1, op), join)
+    def tt(out, in0, in1, op):
+        return mark("v", V.tensor_tensor(out, in0, in1, op))
 
-    def scan(out, d0, d1, init, op0, op1, join=None):
-        return mark("v", V.tensor_tensor_scan(out, d0, d1, init, op0, op1), join)
+    def scan(out, d0, d1, init, op0, op1):
+        return mark("v", V.tensor_tensor_scan(out, d0, d1, init, op0, op1))
 
-    def copy(out, in_, join=None):
-        return mark("v", V.tensor_copy(out, in_), join)
+    def copy(out, in_):
+        return mark("v", V.tensor_copy(out, in_))
 
-    def fill(ap, c, join=None):
-        return mark("v", V.memset(ap, c), join)
+    def fill(ap, c):
+        return mark("v", V.memset(ap, c))
 
     def quant(q, a, e, tile):
         return mark("v", V.quantize_mx(q[0][:, a:e], q[1][:, a:e], tile[:, 4 * a:4 * e]))
@@ -129,169 +135,153 @@ def rank_program(g, core, T, topo):
     def turn(out, in_):
         return mark("v", V.transpose(out, in_))
 
-    def act(out, in_, func, join=None, **kw):
-        return mark("s", S.activation(out, in_, func, **kw), join)
+    def act(out, in_, func, **kw):
+        return mark("s", S.activation(out, in_, func, **kw))
 
-    def iota(out, pattern, base, join=None, step=0):
-        if out.name in ("pi", "oi"):
-            return mark("g", g.iota(out, pattern, base, step), join)
-        return mark("g", g.iota(out, pattern, base, step, allow_small_or_imprecise_dtypes=True), join)
+    def iota(out, pattern, base):
+        return mark("g", g.iota(out, pattern, base, 0, allow_small_or_imprecise_dtypes=True))
 
     def mx(out, a, b):
         return mark("p", PE.matmul_mx(out, a[0], a[1], b[0], b[1], True, True))
 
     def dma(q, out, in_, name):
-        return mark(q, queue[q].dma_start(out, in_), None, name, 16)
+        return mark(q, queue[q].dma_start(out, in_), name, 16)
 
     def cols(q, a, b):
         return (q[0][:, a:b], q[1][:, a:b])
+
+    def run(tile, a, e):
+        return tile[:, 4 * a:4 * e]
 
     def elem(tile, b, a, e):
         return tile[:, 4 * a + b:4 * e:4]
 
     r_col, x_col, q_col, t_col, r1_col, q1_col, sc_col, sc4_col, zb_col = (T.pf[:, j:j + 1] for j in range(9))
     bank = [T[n] for n in BANKS]
-    eq, wq, zq = (T.eq, T.es), (T.wq, T.wp), (T.zq, T.zs)
+    eq, wq, zq, vq = (T.eq, T.es), (T.wq, T.wp), (T.zq, T.zs), (T.vq, T.vs)
     rows16, even32, odd32, sign16 = (cols((T.pq, T.ps), 128 * j, 128 * j + 128) for j in range(4))
     xqs = [(T["xq%d" % t], T["xs%d" % t]) for t in range(4)]
 
-    def thresholds(k, w):
-        wait("s", act(k[:, 0:NB], w, AF.Identity, bias=MAGIC, scale=1.0 / 512))
-        wait("s", act(k[:, NB:2 * NB], k[:, 0:NB], AF.Identity, bias=-512.0 * MAGIC, scale=512.0))
+    def thresholds(k, w, between):
+        m = act(k[:, 0:NB], w, AF.Identity, bias=MAGIC, scale=1.0 / 512)
+        between(0)
+        wait("s", m)
+        m = act(k[:, NB:2 * NB], k[:, 0:NB], AF.Identity, bias=-512.0 * MAGIC, scale=512.0)
+        between(1)
+        wait("s", m)
         return act(k[:, 2 * NB:3 * NB], k[:, NB:2 * NB], AF.Identity, bias=257.5, scale=GROW)
 
     def picks(a, e):
         return copy(T.pq[:, a:e].bitcast(dt.uint32), T.uq[:].bitcast(dt.uint32).indirect(T.off[:, a // 16:e // 16]))
 
+    def scales(a, e):
+        wait("s", uq, of)
+        pks.append(act(T.ps[:, a:e], T.us[:].indirect(T.off[:, a // 16:e // 16]), AF.Copy))
+
     def holds(cs):
-        m = None
-        for c in cs:
-            m = act(T.hold[:, AT[c + 1] - 32:AT[c + 1] + 1], T.p33[:, 0:33], AF.Identity, m, bias=1.0)
-        return m
+        return [act(T.hold[:, AT[c + 1] - 32:AT[c + 1] + 1], T.p33[:, 0:33], AF.Identity, bias=1.0) for c in cs]
+
+    def unit_tile(b):
+        wait("g", gz)
+        return mark("g", g.affine_select(T.et[:, 512 * b:512 * b + 512], T.zb[:], [[-1, 128], [1000, 4]], OP.not_equal,
+                                         1.0, -1000 * b, 1))
 
     lu = dma("s", T.ut[:], T.u[:], "lu")
-    lx = dma("y", T.x0[:], T.x[:], "lx")
+    lx = [dma("y", run(T.x0, a, e), run(T.x, a, e), name) for (a, e), name in zip(PARTS, ("la", "lx"))]
     wait("y", lx)
     dma("y", T.wq[:].bitcast(dt.uint8), T.wc[:], "lw")
     lw = dma("y", T.wp[:], T.ws[:], "lw")
     lv = dma("y", T.vt[:], T.v[:], "lv")
 
-    g0 = iota(T.c32[:], [[1, 34]], 0, iota(T.pi[:, 0:1], [[0, 1]], 0, None, 1))
-    g1 = None
+    mark("g", g.iota(T.pi[:, 0:1], [[0, 1]], 0, 1))
+    g0 = iota(T.c32[:], [[1, 34]], 0)
     for j, (pattern, base) in enumerate((([[16, 8]], 0), ([[32, 4], [0, 2]], 0), ([[32, 4], [0, 2]], 16), ([[16, 8]], 1))):
-        g1 = iota(T.oi[:, 8 * j:8 * j + 8], pattern, base, g1)
-    g2 = iota(T.c16[:], [[0, 2], [1, 16]], 0)
-    g2 = iota(T.inc[:, 0:2 * B0], [[32, B0], [0, 2]], 33, g2)
-    g2 = iota(T.inc[:, 2 * B0:32], [[0, 32 - 2 * B0]], LEN[NB - 1] + 1, g2)
-    g2 = iota(T.jr[:, 0:2 * B0], [[0, 2 * B0]], 1 + KAPPA0, g2)
-    g2 = iota(T.jr[:, 2 * B0:NB], [[-32, NS // 2], [0, 2]], 1 + KAPPA0 - J[2 * B0], g2)
+        g1 = mark("g", g.iota(T.oi[:, 8 * j:8 * j + 8], pattern, base, 0))
+    iota(T.c16[:], [[0, 2], [1, 16]], 0)
+    iota(T.inc[:, 0:CU], [[32, CU // 2], [0, 2]], LEN[0] + 1)
+    iota(T.inc[:, CU:CU + 2], [[LEN[CU + 1] - LEN[CU], 2]], LEN[CU] + 1)
+    iota(T.inc[:, CU + 2:32], [[32, 15 - CU // 2], [0, 2]], LEN[CU + 2] + 1)
+    iota(T.jr[:, 0:FS], [[0, FS]], 1 + KAPPA0)
+    g2 = iota(T.jr[:, FS:NB], [[0, NS]], 1 + KAPPA0 - U)
     g3 = iota(T.c4[:], [[0, 4], [1, 4]], 0)
     gz = iota(T.zb[:], [[0, 512]], 0)
-
-    def unit_tile(b, join=None):
-        wait("g", gz)
-        return mark("g", g.affine_select(T.et[:, 512 * b:512 * b + 512], T.zb[:], [[-1, 128], [1000, 4]], OP.not_equal,
-                                         1.0, -1000 * b, 1), join)
-
-    et = unit_tile(0)
+    unit_tile(0)
+    unit_tile(1)
     grow = fill(T.mul[:], GROW)
-    p33 = fill(T.p33[:, 32:34], -1.0)
-    wait("v", g0)
-    m = ts(T.pi[:, 1:2], T.pi[:, 0:1], 15, OP.bitwise_and)
-    m = ts(T.pi[:, 2:3], T.pi[:, 0:1], 31, OP.bitwise_and, join=m)
-    m = ts(T.pi[:, 3:4], T.pi[:, 0:1], 15, OP.bitwise_and, 2, OP.arith_shift_right, m)
-    m = ts(T.pi[:, 4:5], T.pi[:, 0:1], 3, OP.bitwise_and, join=m)
-    wait("v", grow)
+    fill(T.hold[:], 1.0)
+    wait("v", g0, grow)
+    ts(T.pi[:, 1:2], T.pi[:, 0:1], 15, OP.bitwise_and)
+    ts(T.pi[:, 2:3], T.pi[:, 0:1], 31, OP.bitwise_and)
+    ts(T.pi[:, 3:4], T.pi[:, 0:1], 15, OP.bitwise_and, 2, OP.arith_shift_right)
+    m = ts(T.pi[:, 4:5], T.pi[:, 0:1], 3, OP.bitwise_and)
     wb = scan(T.wb[:], T.mul[:], T.mul[:], W0, OP.mult, OP.max)
-    wait("v", m)
+    wait("v", m, g1)
     pf = copy(T.pf[:, 0:4], T.pi[:, 1:5])
-    wait("v", wb)
-    wt = turn(T.wt[:], T.wb[:, 0:C])
-    wait("v", pf)
-    p33 = ts(T.p33[:, 0:32], T.c32[:, 0:32], x_col, OP.is_equal, 1.0 / TINY, OP.mult, p33)
-    pf = ts(T.pf[:, 4:6], T.pf[:, 0:3:2], 1.0, OP.add)
-    pf = ts(sc_col, r_col, 15.0, OP.is_equal, 2.0 ** -40, OP.max, pf)
-    ones = fill(T.hold[:], 1.0)
-    wait("s", wt)
-    ka = [act(T.ka[:, 3 * NB:4 * NB], T.wt[:, 0:C:16], AF.Copy, scale=GROW), thresholds(T.ka, T.wt[:, 0:C:16])]
-    wait("s", p33, ones)
-    hp_low = holds(range(CA))
-    wait("v", g1, g2, pf)
     of = copy(T.off[:], T.oi[:])
-    m = ts(T.w32[:, 32:64], T.c16[:], r1_col, OP.is_gt)
-    m = ts(T.w32[:, 64:96], T.c16[:], r1_col, OP.is_equal, 2.0 ** 40, OP.mult, m)
-    ends = scan(T.ends[:], T.inc[:], T.c16[:], -1.0, OP.add, OP.max)
-    wait("v", ka)
-    kr = tt(T.kr[:], T.ka[:, 2 * NB:3 * NB], T.ka[:, 3 * NB:4 * NB], OP.subtract)
+    fill(T.p33[:, 32:34], -1.0)
+    fill(T.cmp[:, AT[NB - 1] - 1:AT[NB]:LEN[NB - 1] + 1], 0.0)
+    wait("v", wb, pf)
+    p33 = ts(T.p33[:, 0:32], T.c32[:, 0:32], x_col, OP.is_equal, 1.0 / TINY, OP.mult)
+    pf = ts(T.pf[:, 4:6], T.pf[:, 0:3:2], 1.0, OP.add)
+    wt = turn(T.wt[:], T.wb[:, 0:C])
+    wait("s", p33)
+    hp_first = holds(range(FS - 1, NB))
+    wait("s", wt)
+    act(T.ka[:, 3 * NB:4 * NB], T.wt[:, 0:C:16], AF.Copy, scale=GROW)
+    wait("v", g2, pf)
+    ts(T.w32[:, 32:64], T.c16[:], r1_col, OP.is_gt)
+    ts(T.w32[:, 64:96], T.c16[:], r1_col, OP.is_equal, 2.0 ** 40, OP.mult)
+    m = scan(T.ends[:], T.inc[:], T.c16[:], -1.0, OP.add, OP.max)
+    ts(sc_col, r_col, 15.0, OP.is_equal, 2.0 ** -40, OP.max)
+    fill(T.acc[:, NB:32], 0.0)
     wait("v", lu)
     uq = quant((T.uq, T.us), 0, 128, T.ut)
     wait("v", m)
-    w16 = tt(T.w32[:, 0:32], T.w32[:, 32:64], T.w32[:, 64:96], OP.add)
-    wait("v", kr)
-    st = tt(T.st[:], T.jr[:], T.kr[:], OP.add)
-    once = fill(T.cmp[:, AT[NB - 1] - 1:AT[NB]:LEN[NB - 1] + 1], 0.0)
-    once = fill(T.cmp[:, AT[CA - 1] - 1:AT[CA]:LEN[CA - 1] + 1], 0.0, once)
-    once = fill(T.acc[:, NB:32], 0.0, once)
+    tt(T.w32[:, 0:32], T.w32[:, 32:64], T.w32[:, 64:96], OP.add)
+    w16 = ts(T.rep[:], T.c32[:, 0:NB], 0.0, OP.mult, r_col, OP.add)
+    pks = []
+    ka = thresholds(T.ka, T.wt[:, 0:C:16], lambda j: scales(0, 128) if j else holds(range(4)))
+    scales(128, 384)
+    scales(384, 512)
+    hp_second = holds(range(4, FS - 1))
     wait("v", uq, of)
-    pk0 = picks(0, 256)
-    wait("s", uq, of)
-    pks = None
-    for a, e in ((0, 256), (256, 384), (384, 512)):
-        pks = act(T.ps[:, a:e], T.us[:].indirect(T.off[:, a // 16:e // 16]), AF.Copy, pks)
-    hp_high = holds(range(CA, NB))
-    wait("v", w16, ends, st)
-    ew = scan(T.ew[:], T.w32[:, 0:32], T.ends[:], 0.0, OP.mult, OP.add)
-    m = ts(T.sg[:, 0:NS * SW:SW], T.st[:, 2 * B0:NB], -8.0, OP.add)
-    once = ts(T.acc[:, 0:2 * B0], T.st[:, 0:2 * B0], UNIT, OP.mult, join=once)
-    pk1 = picks(256, 384)
-    wait("v", m, ew)
-    sums = tt(T.sg[:, 1:NS * SW:SW], T.st[:, 2 * B0:NB], T.sg[:, 0:NS * SW:SW], OP.subtract)
-    once = ts(T.eo[:], T.ew[:, 15:32:16], sc_col, OP.mult, float(AT[NB] - 1), OP.min, once)
-
-    def later_constants():
-        wait("v", g3, wn)
-        kk = scan(T.kk[:], T.wn[:], T.wb[:, 0:C], 0.0, OP.mult, OP.add)
-        a = ts(T.w4[:, 16:32], T.c4[:], q1_col, OP.is_gt)
-        a = ts(T.w4[:, 32:48], T.c4[:], q1_col, OP.is_equal, 2.0 ** 40, OP.mult, a)
-        a = ts(T.ca[:], T.c32[:, 0:16], r_col, OP.is_gt, GROW - 1.0, OP.mult, a)
-        a = ts(T.cb[:], T.c32[:, 0:16], r_col, OP.not_equal, 2.0 ** -12, OP.max, a)
-        a = ts(sc4_col, q_col, 3.0, OP.is_equal, 2.0 ** -40, OP.max, a)
-        b = ts(T.rp[:], T.zb[:, 0:C], 0.0, OP.add)
-        b = ts(T.mb[:, C:C + 1], T.zb[:, 0:1], LAST * UNIT, OP.add, join=b)
-        b = ts(T.stp[:, 0:STEPS:STEPS - 1], T.c32[:, 0:2], LEAVE * UNIT, OP.mult, join=b)
-        wait("v", a)
-        w4 = tt(T.w4[:, 0:16], T.w4[:, 16:32], T.w4[:, 32:48], OP.add)
-        b = tt(T.mul[:, 0:16], T.ca[:], T.cb[:], OP.add, b)
-        b = ts(sc4_col, sc4_col, 4.0 / UNIT, OP.mult, join=b)
-        b = ts(zb_col, t_col, -4.0 * NAME0, OP.add, join=b)
-        wait("s", kk)
-        wait("s", act(T.kb[:, 3 * NB:4 * NB], T.kk[:, 15:C:16], AF.Copy, scale=sc_col))
-        wait("s", thresholds(T.kb, T.kb[:, 3 * NB:4 * NB]))
-        k0 = act(T.k0[:], T.kb[:, 2 * NB:3 * NB], AF.Identity, bias=-2.0 ** 12 * UNIT, scale=2.0 ** 12 * UNIT)
-        wait("s", w4)
-        return b, k0, act(T.wn4[:], T.w4[:, 0:16].indirect(T.rep[:]), AF.Copy)
+    pk = [picks(0, 128)]
 
     def own(c):
         return T.tc[:, 16 * c:16 * c + 1]
 
-    def compare(c, rows, width, join=None):
-        n = min(LEN[c] + 1, width - J[c])
-        return ts(T.cmp[:, AT[c]:AT[c] + n], rows[:, J[c]:J[c] + n], own(c), OP.is_ge, TINY * UNIT, OP.mult, join)
+    def compare(c, rows):
+        n = min(LEN[c] + 1, C - J[c])
+        return ts(T.cmp[:, AT[c]:AT[c] + n], rows[:, 0:n], own(c), OP.is_ge, TINY * UNIT, OP.mult)
 
-    def count(a, b, join=None):
-        return scan(T.cnt[:, AT[a]:AT[b]], T.hold[:, AT[a]:AT[b]], T.cmp[:, AT[a]:AT[b]], 0.0, OP.mult, OP.add, join)
+    def count(a, b):
+        return scan(T.cnt[:, AT[a]:AT[b]], T.hold[:, AT[a]:AT[b]], T.cmp[:, AT[a]:AT[b]], 0.0, OP.mult, OP.add)
 
     def first_scores(xq, made):
-        wait("p", pk0, pk1, pks, made)
-        return [mx(bank[j][:, 0:A], side, cols(xq, 0, A)) for j, side in enumerate((rows16, even32, odd32))]
+        m = []
+        for j, side in enumerate((rows16, even32, odd32)):
+            wait("p", pk[min(j, 1)], pks[min(j, 1)], made)
+            m.append(mx(bank[j][:, 0:C - U], side, cols(xq, U, C)))
+        return m
 
-    wait("v", lx)
-    xa = quant(xqs[0], 0, A, T.x0)
+    wait("v", lx[0])
+    xa = quant(xqs[0], U, C, T.x0)
+    pk.append(picks(128, 384))
     first = first_scores(xqs[0], xa)
-    xb = quant(xqs[0], A, C, T.x0)
-    pk2 = picks(384, 512)
+    wait("v", w16, ka)
+    scan(T.ew[:], T.w32[:, 0:32], T.ends[:], 0.0, OP.mult, OP.add)
+    m = tt(T.kr[:], T.ka[:, 2 * NB:3 * NB], T.ka[:, 3 * NB:4 * NB], OP.subtract)
     wait("v", first[0])
-    tl = turn(T.tc[:, 0:A], bank[0][:, 0:A])
+    tu = turn(T.tc[:, U:C], bank[0][:, 0:C - U])
+    wait("v", lx[1])
+    xb = quant(xqs[0], 0, U, T.x0)
+    wait("v", m)
+    m = tt(T.st[:], T.jr[:], T.kr[:], OP.add)
+    ts(T.eo[:], T.ew[:, 15:32:16], sc_col, OP.mult, float(AT[NB] - 1), OP.min)
+    pk.append(picks(384, 512))
+    wait("v", m)
+    sums = ts(T.sg[:, 0:NS * SW:SW], T.st[:, FS:NB], -8.0, OP.add)
+    ts(T.acc[:, 0:FS], T.st[:, 0:FS], UNIT, OP.mult)
 
     for t, mask_t in enumerate(ROUNDS):
         peer = T.cores[rank ^ mask_t]
@@ -307,63 +297,63 @@ def rank_program(g, core, T, topo):
             g.remote_dma(out, in_, T.sem[to], T.sem.left, pid, rid, mask)
             cnt[to] += ne
             cnt["left"] += ne
-            return (to, cnt[to], {})
+            return (to, cnt[to], {to: cnt[to]}, to)
 
-        wait("g", xa, xb)
+        wait("g", xb)
         send(aq[0][:, 0:EARLY].bitcast(dt.uint8), xq[0][:, 0:EARLY].bitcast(dt.uint8), "aq%d" % t)
+        if t == 0:
+            unit_tile(2)
+            et = unit_tile(3)
 
-        ju = max(J)
+        wide = [max(LEN[h:FS:2]) + 2 for h in range(2)]
         wait("p", xb)
-        mu = mx(bank[4][:, 0:C - A], rows16, cols(xq, A, C))
-        mes = mx(bank[5][:, 0:ju], even32, cols(xq, 0, ju))
-        mev = mx(bank[6][:, 0:C], even32, cols(xq, 0, C))
-        mos = mx(bank[7][:, 0:ju], odd32, cols(xq, 0, ju))
-        wait("p", tl, pk2)
-        mov = mx(bank[0][:, 0:C], odd32, cols(xq, 0, C))
+        ml = mx(bank[5][:, 0:U], rows16, cols(xq, 0, U))
+        mes = mx(bank[4][:, 0:U], even32, cols(xq, 0, U))
+        mev = mx(bank[6][:, 0:wide[0]], even32, cols(xq, 0, wide[0]))
+        mos = mx(bank[7][:, 0:U], odd32, cols(xq, 0, U))
+        wait("p", tu, pk, pks)
+        mov = mx(bank[0][:, 0:wide[1]], odd32, cols(xq, 0, wide[1]))
         mw = mx(bank[3][:, 0:C], sign16, cols(xq, 0, C))
 
-        wait("v", tl, first[1], first[2])
-        low = None
-        for c in range(CA):
-            low = compare(c, bank[1 + c % 2], A, low)
-        wait("v", mu)
-        tu = turn(T.tc[:, A:C], bank[4][:, 0:C - A])
+        wait("v", tu, first)
+        early = [compare(c, bank[1 + c % 2]) for c in range(FS, NB)]
+        if t == 0:
+            wait("v", sums)
+            sums = tt(T.sg[:, 1:NS * SW:SW], T.st[:, FS:NB], T.sg[:, 0:NS * SW:SW], OP.subtract)
+        wait("v", ml)
+        tl = turn(T.tc[:, 0:U], bank[5][:, 0:U])
 
-        order = [c for h in range(2) for c in reversed(range(2 * B0 + h, NB, 2))]
+        order = [c for h in range(2) for c in range(FS, NB) if c % 2 == h]
         wait("s", tu, mes)
-        signs, summed = [], None
-        for n in range(NS + 1):
+        signs = []
+        for n in range(NS + LAG):
             if n < NS:
                 c = order[n]
                 if c % 2:
                     wait("s", mos)
-                a = SW * (c - 2 * B0)
-                signs.append(act(T.sg[:, a + 2:a + 2 + J[c]], bank[5 + 2 * (c % 2)][:, 0:J[c]], AF.Sign, bias=own(c), scale=-1.0))
-            if n > 0:
-                c = order[n - 1]
-                a = SW * (c - 2 * B0)
-                wait("s", signs[n - 1], sums)
-                summed = act(T.sr[:, a:a + 2 + J[c]], T.sg[:, a:a + 2 + J[c]], AF.Relu, summed, scale=UNIT,
-                             accum_out=T.acc[:, c:c + 1])
+                a = SW * (c - FS)
+                signs.append(act(T.sg[:, a + 2:a + SW], bank[4 + 3 * (c % 2)][:, 0:U], AF.Sign, bias=own(c), scale=-1.0))
+            if n >= LAG:
+                c = order[n - LAG]
+                a = SW * (c - FS)
+                wait("s", signs[n - LAG], sums)
+                summed = act(T.sr[:, a:a + SW], T.sg[:, a:a + SW], AF.Relu, scale=UNIT, accum_out=T.acc[:, c:c + 1])
 
         if t == 0:
-            w16 = [w16, ts(T.rep[:], T.c32[:, 0:NB], 0.0, OP.mult, r_col, OP.add)]
-        wait("v", low, once, hp_low)
-        counted = count(0, CA)
-        wait("v", tu, mev)
-        high = None
-        for c in range(CA, NB, 2):
-            high = compare(c, bank[6], C, high)
+            wait("v", gz)
+            ts(T.cap[:], T.zb[:, 0:C], CAP * C * UNIT, OP.add)
+            ts(T.cum[:, 0:1], T.zb[:, 0:1], 0.0, OP.add)
+        wait("v", early, hp_first)
+        count(FS, NB)
+        wait("v", tl, mev)
+        for c in range(0, FS, 2):
+            compare(c, bank[6])
         wait("v", mov)
-        cut = 2 * B0 - 2
-        for c in list(range(CA + 1, cut, 2)) + list(range(2 * B0 + 1, NB, 2)):
-            high = compare(c, bank[0], C, high)
-        final = compare(cut + 1, bank[0], C)
-        wait("v", high, hp_high)
-        counted = count(CA, cut, counted)
-        counted = count(2 * B0, NB, counted)
-        wait("v", final)
-        counted = count(cut, 2 * B0, counted)
+        m = [compare(c, bank[0]) for c in range(1, CU, 2)]
+        wait("v", m[-2], hp_second)
+        count(0, CU - 1)
+        wait("v", m[-1])
+        counted = count(CU - 1, FS)
         wait("v", mw)
         want = ts(T.want[:], bank[3][:, 0:C], 0.0, OP.is_gt, C * UNIT, OP.mult)
         wait("v", counted, summed)
@@ -373,90 +363,104 @@ def rank_program(g, core, T, topo):
         send(aq[0][:, EARLY:C].bitcast(dt.uint8), xq[0][:, EARLY:C].bitcast(dt.uint8), "aq%d" % t)
         arrived = send(aq[1][:], xq[1][:], "aq%d" % t)
 
-        if t == 0:
-            for b in range(1, 4):
-                et = unit_tile(b, et)
-            wait("s", w16, gz)
-            rz = act(T.rz16[:], T.c16[:, 0:16], AF.Sign)
-            wn = act(T.wn[:], T.w32[:, 0:16].indirect(T.rep[:]), AF.Copy)
-            wait("s", rz)
-            rz = act(T.rz[:], T.rz16[:].indirect(T.rep[:, 0:10]), AF.Copy)
-            wait("v", gz)
-            un = ts(T.un[:], T.zb[:, 0:C], UNIT, OP.add)
-            want = ts(T.cap[:], T.zb[:, 0:C], CAP * C * UNIT, OP.add, join=want)
-            want = ts(T.cum[:, 0:1], T.zb[:, 0:1], 0.0, OP.add, join=want)
-            wait("v", un)
-            iou = scan(T.iou[:], T.un[:], T.zb[:, 0:C], (NAME0 - 1) * UNIT, OP.add, OP.add)
         wait("v", want)
         cum = scan(T.cum[:, 1:C + 1], T.want[:], T.cap[:], 0.0, OP.add, OP.min)
         if t == 0:
-            made, k0, wn4 = later_constants()
-            wait("s", lx)
-            window = act(win[:, 0:4 * C], T.x0[:], AF.Copy, scale=32.0)
+            wait("s", w16)
+            wn = act(T.wn[:], T.w32[:, 0:16].indirect(T.rep[:]), AF.Copy)
+            wait("s", act(T.rz16[:], T.c16[:, 0:16], AF.Sign))
+            rz = act(T.rz[:], T.rz16[:].indirect(T.rep[:]), AF.Copy)
+            ts(T.un[:], T.zb[:, 0:C], UNIT, OP.add)
+            ts(T.rp[:], T.zb[:, 0:C], 0.0, OP.add)
         wait("v", cum)
         take = scan(T.take[:], T.cum[:, 1:C + 1], T.cum[:, 0:C], 0.0, OP.max, OP.subtract)
+        if t == 0:
+            wait("v", wn)
+            wait("s", scan(T.kk[:], T.wn[:], T.wb[:, 0:C], 0.0, OP.mult, OP.add))
+            wait("s", act(T.kb[:, 3 * NB:4 * NB], T.kk[:, 15:C:16], AF.Copy, scale=sc_col))
+            wait("s", lx, thresholds(T.kb, T.kb[:, 3 * NB:4 * NB], lambda j: act(
+                run(win, 80 * j, 80 * j + 80), run(T.x0, 80 * j, 80 * j + 80), AF.Copy, scale=32.0)))
+            k0 = act(T.k0[:], T.kb[:, 2 * NB:3 * NB], AF.Identity, bias=-2.0 ** 12 * UNIT, scale=2.0 ** 12 * UNIT)
+            act(run(win, H, C), run(T.x0, H, C), AF.Copy, scale=32.0)
         wait("v", take)
-        wait("v", turn(T.tkt[:], T.take[:]), sn)
+        m = turn(T.tkt[:], T.take[:])
+        if t == 0:
+            wait("v", g3)
+            ts(T.w4[:, 16:32], T.c4[:], q1_col, OP.is_gt)
+            ts(T.w4[:, 32:48], T.c4[:], q1_col, OP.is_equal, 2.0 ** 40, OP.mult)
+            ts(T.ca[:], T.c32[:, 0:16], r_col, OP.is_gt, GROW - 1.0, OP.mult)
+            ts(T.cb[:], T.c32[:, 0:16], r_col, OP.not_equal, 2.0 ** -12, OP.max)
+            made = ts(sc4_col, q_col, 3.0, OP.is_equal, 2.0 ** -40, OP.max)
+        wait("v", m, sn)
         m = tt(T.hi[:], snd[:, 0:NB], T.tkt[:, 0:C:16], OP.add)
         lo = tt(T.lo[:], snd[:, 0:NB], T.tkt[:, 0:C:16], OP.subtract)
+        if t == 0:
+            iou = scan(T.iou[:], T.un[:], T.zb[:, 0:C], (NAME0 - 1) * UNIT, OP.add, OP.add)
+            wait("v", made)
+            wait("s", tt(T.w4[:, 0:16], T.w4[:, 16:32], T.w4[:, 32:48], OP.add))
+            wn4 = act(T.wn4[:], T.w4[:, 0:16].indirect(T.rep[:]), AF.Copy)
 
         wait("v", at, m)
         m = tt(T.mid[:], land[:], T.hi[:], OP.min)
         wait("v", iou)
         val = scan(T.val[:], T.take[:], T.iou[:], 2.0, OP.min, OP.add)
-        wait("v", m, lo, made, rz)
-        halves = (H, 0)
-        m = [tt(T.rp[:, a:a + H:16], T.mid[:, a // 16:a // 16 + 10], T.lo[:, a // 16:a // 16 + 10], OP.max) for a in halves]
-        for j, a in enumerate(halves):
+        wait("v", m, lo, rz)
+        m = [tt(T.rp[:, a:e:16], T.mid[:, a // 16:e // 16], T.lo[:, a // 16:e // 16], OP.max) for a, e in PARTS]
+        if t == 0:
+            ts(T.mb[:, C:C + 1], T.zb[:, 0:1], LAST * UNIT, OP.add)
+            ts(T.stp[:, 0:STEPS:STEPS - 1], T.c32[:, 0:2], LEAVE * UNIT, OP.mult)
+            tt(T.mul[:, 0:16], T.ca[:], T.cb[:], OP.add)
+            ts(sc4_col, sc4_col, 4.0 / UNIT, OP.mult)
+        for j, (a, e) in enumerate(PARTS):
             wait("v", m[j])
-            m[j] = scan(T.bc[:, a:a + H], T.rz[:], T.rp[:, a:a + H], 0.0, OP.mult, OP.add)
-        for j, a in enumerate(halves):
+            m[j] = scan(T.bc[:, a:e], T.rz[:, a:e], T.rp[:, a:e], 0.0, OP.mult, OP.add)
+        if t == 0:
+            wait("v", et)
+            quant(eq, 0, 256, T.et)
+        for j, (a, e) in enumerate(PARTS):
             wait("v", m[j])
-            m[j] = turn(T.mb[:, a:a + H], T.bc[:, a:a + H])
+            m[j] = turn(T.mb[:, a:e], T.bc[:, a:e])
+        if t == 0:
+            eqm = quant(eq, 256, 512, T.et)
+        for j, (a, e) in enumerate(PARTS):
+            wait("v", m[j])
+            m[j] = scan(T.stp[:, a + 1:e + 1], T.mb[:, a:e], T.mb[:, a + 1:e + 1], 0.0, OP.min, OP.subtract)
         if t == 0:
             wait("v", lv)
-            vq = quant((T.vq, T.vs), 0, 128, T.vt)
-        for j, a in enumerate(halves):
-            wait("v", m[j])
-            m[j] = scan(T.stp[:, a + 1:a + H + 1], T.mb[:, a:a + H], T.mb[:, a + 1:a + H + 1], 0.0, OP.min, OP.subtract)
+            vqm = quant(vq, 0, 128, T.vt)
+            ts(zb_col, t_col, -4.0 * NAME0, OP.add)
 
-        def order_scans(ks, join=None):
-            for k in ks:
-                join = scan(T.so[:, STEPS * k + 16 * k:STEPS * (k + 1)], T.stp[:, 16 * k:STEPS], T.mul[:, 0:STEPS - 16 * k],
-                            T.k0[:, k:k + 1], OP.add, OP.mult, join)
-            return join
+        def order_scans(ks):
+            return [scan(T.so[:, STEPS * k + 16 * k:STEPS * (k + 1)], T.stp[:, 16 * k:STEPS], T.mul[:, 0:STEPS - 16 * k],
+                         T.k0[:, k:k + 1], OP.add, OP.mult) for k in ks]
 
         def places(a, b):
             return ts(T.po[:, a:b], T.so[:, STEPS * (a + 1) - 1:STEPS * b:STEPS], 1.0 / (UNIT * GROW), OP.mult, float(H), OP.add)
 
-        def scatter(a, b, join=None):
-            return copy(T.nm[:].indirect(T.po[:, a:b]), T.val[:, 16 * a:16 * b], join)
+        def scatter(a, b):
+            return copy(T.nm[:].indirect(T.po[:, a:b]), T.val[:, 16 * a:16 * b])
 
+        wait("p", eqm, arrived, sn, signs)
+        for b in range(4):
+            wait("s", mx(bank[4 + b][:, 0:C], cols(eq, 128 * b, 128 * b + 128), cols(aq, 0, C)))
+            window = act(elem(win, b, C, 2 * C), bank[4 + b][:, 0:C], AF.Copy, scale=32.0)
         wait("v", m[0], k0)
-        upper = order_scans(range(11, NB))
-        if t == 0:
-            wait("v", et)
-            eqm = quant(eq, 0, 512, T.et)
-        wait("p", eqm, arrived, sn, want, signs)
-        for b, k in enumerate((4, 5, 6, 7)):
-            wait("s", mx(bank[k][:, 0:C], cols(eq, 128 * b, 128 * b + 128), cols(aq, 0, C)))
-            window = act(elem(win, b, C, 2 * C), bank[k][:, 0:C], AF.Copy, window if b or t == 0 else None, scale=32.0)
-        wait("v", m[1])
-        upper = order_scans([10, 9, 8, 7, 6], upper)
-        m = order_scans([5, 4, 3])
+        order_scans(range(NB - 1, CU, -1))
+        wait("v", m)
+        upper = order_scans(range(CU, 5, -1))
+        order_scans([5, 4, 3])
         wait("v", upper)
         p = places(6, NB)
-        m = order_scans([2, 1, 0], m)
+        m = order_scans([2, 1, 0])
         wait("v", p, val)
         nm = scatter(6, NB)
         wait("v", m)
         wait("v", places(0, 6), nm)
         nm = scatter(0, 6)
         wait("v", nm, wn4)
-        parts = ((0, A), (A, C))
-        m = [scan(T.ns[:, a:e], T.wn4[:, a:e], T.nm[:, a:e], 0.0, OP.mult, OP.add) for a, e in parts]
+        m = [scan(T.ns[:, a:e], T.wn4[:, a:e], T.nm[:, a:e], 0.0, OP.mult, OP.add) for a, e in PARTS]
         zo = []
-        for j, (a, e) in enumerate(parts):
+        for j, (a, e) in enumerate(PARTS):
             wait("v", m[j])
             zo.append(ts(T.zo[:, a // 4:e // 4], T.ns[:, a + 3:e:4], sc4_col, OP.mult, zb_col, OP.add))
         if last:
@@ -466,62 +470,67 @@ def rank_program(g, core, T, topo):
                 dma("y", T.od[k:k + 1, :], T.odb[16 * k:16 * k + 1, :], "out")
 
         zv, zs = [], []
-        for j, (a, e) in enumerate(parts):
+        for j, (a, e) in enumerate(PARTS):
             c = GATHER[j]
             wait("s", zo[j], window)
-            zs.append(act(T.zt[:, 4 * c:4 * e], win[:].indirect(T.zo[:, c // 4:e // 4]), AF.Copy, scale=2.0 ** -5))
+            zs.append(act(run(T.zt, c, e), win[:].indirect(T.zo[:, c // 4:e // 4]), AF.Copy, scale=2.0 ** -5))
             wait("v", zo[j], window)
-            zv.append(ts(T.zt[:, 4 * a:4 * c], win[:].indirect(T.zo[:, a // 4:c // 4]), 2.0 ** -5, OP.mult))
+            zv.append(ts(run(T.zt, a, c), win[:].indirect(T.zo[:, a // 4:c // 4]), 2.0 ** -5, OP.mult))
 
         def products(j, made):
-            a, e = parts[j]
+            a, e = PARTS[j]
             wait("p", made)
             return [mx(bank[4 * j + b][:, 0:e - a], cols(wq, 128 * b, 128 * b + 128), cols(zq, a, e)) for b in range(4)]
 
+        def scaled(j):
+            (a, e), c = PARTS[j], GATHER[j]
+            wait("s", zs[j])
+            wait("v", zv[j])
+            return [act(run(T.z32, c, e), run(T.zt, c, e), AF.Copy, scale=32.0),
+                    ts(run(T.z32, a, c), run(T.zt, a, c), 32.0, OP.mult)]
+
         def add(j, b):
-            a, e = parts[j]
+            a, e = PARTS[j]
             wait("v", r[j][b], z32[j])
             m = tt(elem(nxt, b, a, e), bank[4 * j + b][:, 0:e - a], elem(T.z32, b, a, e), OP.add)
+            if (j, b) == (1, 3):
+                wait("v", m)
+                return ts(elem(T.xn, b, a, e), elem(nxt, b, a, e), 2.0 ** -5, OP.mult)
             wait("s", m)
             return act(elem(T.xn, b, a, e), elem(nxt, b, a, e), AF.Copy, scale=2.0 ** -5)
 
         wait("p", lw, window)
         wait("v", zv[0], zs[0])
-        r = [products(0, quant(zq, 0, A, T.zt))]
-        z32 = [ts(T.z32[:, 0:4 * A], T.zt[:, 0:4 * A], 32.0, OP.mult)]
-        wait("s", zs[1])
-        c = GATHER[1]
-        m = act(T.z32[:, 4 * c:4 * C], T.zt[:, 4 * c:4 * C], AF.Copy, scale=32.0)
-        wait("v", zv[1])
-        z32.append([m, ts(T.z32[:, 4 * A:4 * c], T.zt[:, 4 * A:4 * c], 32.0, OP.mult)])
+        r = [products(0, quant(zq, U, C, T.zt))]
+        z32 = [scaled(0), scaled(1)]
         wait("v", zs[1])
-        r.append(products(1, quant(zq, A, C, T.zt)))
+        r.append(products(1, quant(zq, 0, U, T.zt)))
         na = [add(0, b) for b in range(4)]
         nb = [add(1, b) for b in range(3)]
         wait("v", na)
-        xa = quant(xn, 0, A, T.xn)
+        xa = quant(xn, U, C, T.xn)
         if not last:
             first = first_scores(xn, xa)
         nb.append(add(1, 3))
         if not last:
             wait("v", first[0])
-            tl = turn(T.tc[:, 0:A], bank[0][:, 0:A])
+            tu = turn(T.tc[:, U:C], bank[0][:, 0:C - U])
         wait("v", nb)
-        xb = quant(xn, A, C, T.xn)
+        xb = quant(xn, 0, U, T.xn)
 
-    wait("p", vq, xa)
-    my = mx(bank[0][:, 0:A], (T.vq[:], T.vs[:]), cols(xn, 0, A))
+    wait("p", vqm, xa)
+    my = mx(bank[0][:, 0:C - U], cols(vq, 0, 128), cols(xn, U, C))
     wait("y", xa)
-    dma("y", T.oc[:, 0:4 * A], T.xq3[:, 0:A].bitcast(dt.uint8), "out")
+    dma("y", run(T.oc, U, C), T.xq3[:, U:C].bitcast(dt.uint8), "out")
     wait("s", my)
-    wait("y", act(T.ysb[:, 0:A], bank[0][:, 0:A], AF.Copy))
-    dma("y", T.y[:, 0:A], T.ysb[:, 0:A], "out")
+    wait("y", act(T.ysb[:, U:C], bank[0][:, 0:C - U], AF.Copy))
+    dma("y", T.y[:, U:C], T.ysb[:, U:C], "out")
     wait("p", xb)
-    wait("v", mx(bank[1][:, 0:C - A], (T.vq[:], T.vs[:]), cols(xn, A, C)))
-    wait("y", copy(T.ysb[:, A:C], bank[1][:, 0:C - A]))
-    dma("y", T.y[:, A:C], T.ysb[:, A:C], "out")
-    wait("s", xa, xb)
-    dma("s", T.oc[:, 4 * A:4 * C], T.xq3[:, A:C].bitcast(dt.uint8), "out")
+    wait("v", mx(bank[1][:, 0:U], cols(vq, 0, 128), cols(xn, 0, U)))
+    wait("y", copy(T.ysb[:, 0:U], bank[1][:, 0:U]))
+    dma("y", T.y[:, 0:U], T.ysb[:, 0:U], "out")
+    wait("s", xb)
+    dma("s", run(T.oc, 0, U), T.xq3[:, 0:U].bitcast(dt.uint8), "out")
     for k in range(4):
         dma("s", T.osc[4 * k:4 * k + 4, :], T.xs3[32 * k:32 * k + 4, :], "out")
-    wait("g", [(n, cnt[n], {}) for n in SEMAPHORES])
+    wait("g", [(n, cnt[n], {n: cnt[n]}, n) for n in SEMAPHORES])

@@ -6,13 +6,15 @@ H = C // 2
 NB = C // 16
 ROUNDS = [1, 2, 3]
 CAP = 128
-NAME0 = C + 1
+NAME0 = 1
 HALF = "float16"
 
 GROW = 513.0 / 512.0
 UNIT = 2.0 ** -9
+FAR = C * UNIT
 W0 = 8522306.0
 KAPPA0 = 1152
+UNDER = KAPPA0 + 514
 STEPS = C + 2
 TINY = 2.0 ** -30
 MAGIC = 1.5 * 2.0 ** 23
@@ -33,8 +35,9 @@ LAST, LEAVE = _ends()
 
 U = 192
 CU = U // 16
-FS = CU + 1
-J = [0] * FS + [U] * (NB - FS)
+FS = CU
+J = [0] * FS + [32] + [U] * (NB - FS - 1)
+PW = U + 32
 LEN = [32 * (c // 2) + 32 - J[c] for c in range(NB)]
 AT = [sum(LEN[:c]) + c for c in range(NB + 1)]
 SW = U + 2
@@ -42,24 +45,22 @@ NS = NB - FS
 LAG = 2
 PARTS = ((U, C), (0, U))
 GATHER = (256, 80)
-EARLY = 160
 
 X4 = "float8_e4m3fn_x4"
 SCRATCH = {}
 for _dt, _list in (
         ("bfloat16", (("x0", 4 * C), ("xn", 4 * C), ("ut", 512), ("vt", 512), ("et", 2048), ("zt", 4 * C), ("z32", 4 * C),
-                      ("zb", 512), ("rz16", 16), ("rz", C), ("c32", 34), ("c16", 32), ("c4", 16), ("p33", 34),
+                      ("zb", 512), ("un", C), ("c32", 34), ("c16", 32), ("c4", 16), ("p33", PW + 34),
                       ("w32", 96), ("w4", 48), ("wn", C), ("wn4", C), ("cmp", AT[NB] + 1), ("hold", AT[NB] + 1),
-                      ("cnt", AT[NB] + 1), ("sg", NS * SW), ("sr", NS * SW), ("so", NB * STEPS),
-                      ("win0", 8 * C), ("win1", 8 * C))),
+                      ("cnt", AT[NB] + 1), ("sg", NS * SW), ("sr", NS * SW), ("so", NB * STEPS), ("win", 8 * C))),
         ("float32", (("pf", 12), ("wb", STEPS), ("wt", C), ("ka", 4 * NB), ("kb", 4 * NB), ("kr", NB), ("kk", C),
-                     ("k0", NB), ("ca", 16), ("cb", 16), ("inc", 32), ("ends", 32), ("ew", 32), ("jr", NB),
-                     ("st", NB), ("acc", 32), ("tc", C), ("lo", NB), ("hi", NB), ("mid", NB), ("nm", C), ("ns", C),
+                     ("k0", NB), ("ca", 16), ("cb", 16), ("inc", 32), ("ends", 32), ("ew", 32),
+                     ("acc", 32), ("tc", C), ("lo", NB), ("hi", NB), ("nm", C), ("ns", C),
                      ("odb", C), ("ysb", C), ("snd0", 32), ("snd1", 32), ("snd2", 32),
                      ("land0", NB), ("land1", NB), ("land2", NB))),
-        (HALF, (("mul", STEPS), ("rp", C), ("un", C), ("bc", C), ("mb", C + 2), ("stp", STEPS),
+        (HALF, (("mul", STEPS), ("rp", C), ("rz", C), ("bc", C), ("mb", C + 2), ("stp", STEPS),
                 ("cap", C), ("want", C), ("cum", C + 2), ("take", C), ("tkt", C), ("val", C), ("iou", C))),
-        ("int32", (("pi", 6), ("oi", 32))),
+        ("int32", (("pi", 4), ("dj", 32), ("oi", 32))),
         ("uint16", (("off", 32), ("rep", NB), ("eo", 2), ("po", NB), ("zo", C // 4)))):
     for _n, _w in _list:
         SCRATCH[_n] = ("sbuf", [128, _w], _dt)
@@ -156,30 +157,32 @@ def rank_program(g, core, T, topo):
     def elem(tile, b, a, e):
         return tile[:, 4 * a + b:4 * e:4]
 
-    r_col, x_col, q_col, t_col, r1_col, q1_col, sc_col, sc4_col, zb_col = (T.pf[:, j:j + 1] for j in range(9))
+    r_col, t_col, q_col, sc9_col, r1_col, q1_col, sc_col, sc4_col, zb_col = (T.pf[:, j:j + 1] for j in range(9))
     bank = [T[n] for n in BANKS]
+    win = T.win
     eq, wq, zq, vq = (T.eq, T.es), (T.wq, T.wp), (T.zq, T.zs), (T.vq, T.vs)
     rows16, even32, odd32, sign16 = (cols((T.pq, T.ps), 128 * j, 128 * j + 128) for j in range(4))
     xqs = [(T["xq%d" % t], T["xs%d" % t]) for t in range(4)]
 
-    def thresholds(k, w, between):
-        m = act(k[:, 0:NB], w, AF.Identity, bias=MAGIC, scale=1.0 / 512)
+    def thresholds(k, w, scale, less, unit, between):
+        m = act(k[:, 0:NB], w, AF.Identity, bias=MAGIC, scale=scale)
         between(0)
         wait("s", m)
         m = act(k[:, NB:2 * NB], k[:, 0:NB], AF.Identity, bias=-512.0 * MAGIC, scale=512.0)
         between(1)
         wait("s", m)
-        return act(k[:, 2 * NB:3 * NB], k[:, NB:2 * NB], AF.Identity, bias=257.5, scale=GROW)
+        return act(k[:, 2 * NB:3 * NB], k[:, NB:2 * NB], AF.Identity, bias=(257.5 - less) * unit, scale=GROW * unit)
 
     def picks(a, e):
         return copy(T.pq[:, a:e].bitcast(dt.uint32), T.uq[:].bitcast(dt.uint32).indirect(T.off[:, a // 16:e // 16]))
 
     def scales(a, e):
         wait("s", uq, of)
-        pks.append(act(T.ps[:, a:e], T.us[:].indirect(T.off[:, a // 16:e // 16]), AF.Copy))
+        return act(T.ps[:, a:e], T.us[:].indirect(T.off[:, a // 16:e // 16]), AF.Copy)
 
     def holds(cs):
-        return [act(T.hold[:, AT[c + 1] - 32:AT[c + 1] + 1], T.p33[:, 0:33], AF.Identity, bias=1.0) for c in cs]
+        return [act(T.hold[:, AT[c] + min(c, 1):AT[c + 1] + 1], T.p33[:, PW + 31 - LEN[c] + min(c, 1):PW + 33], AF.Identity,
+                    bias=1.0) for c in cs]
 
     def unit_tile(b):
         wait("g", gz)
@@ -193,6 +196,7 @@ def rank_program(g, core, T, topo):
     lw = dma("y", T.wp[:], T.ws[:], "lw")
     lv = dma("y", T.vt[:], T.v[:], "lv")
 
+    gd = mark("g", g.iota(T.dj[:], [[1, 32]], 128, -1))
     mark("g", g.iota(T.pi[:, 0:1], [[0, 1]], 0, 1))
     g0 = iota(T.c32[:], [[1, 34]], 0)
     for j, (pattern, base) in enumerate((([[16, 8]], 0), ([[32, 4], [0, 2]], 0), ([[32, 4], [0, 2]], 16), ([[16, 8]], 1))):
@@ -200,59 +204,67 @@ def rank_program(g, core, T, topo):
     iota(T.c16[:], [[0, 2], [1, 16]], 0)
     iota(T.inc[:, 0:CU], [[32, CU // 2], [0, 2]], LEN[0] + 1)
     iota(T.inc[:, CU:CU + 2], [[LEN[CU + 1] - LEN[CU], 2]], LEN[CU] + 1)
-    iota(T.inc[:, CU + 2:32], [[32, 15 - CU // 2], [0, 2]], LEN[CU + 2] + 1)
-    iota(T.jr[:, 0:FS], [[0, FS]], 1 + KAPPA0)
-    g2 = iota(T.jr[:, FS:NB], [[0, NS]], 1 + KAPPA0 - U)
+    g2 = iota(T.inc[:, CU + 2:32], [[32, 15 - CU // 2], [0, 2]], LEN[CU + 2] + 1)
     g3 = iota(T.c4[:], [[0, 4], [1, 4]], 0)
     gz = iota(T.zb[:], [[0, 512]], 0)
-    unit_tile(0)
-    unit_tile(1)
-    grow = fill(T.mul[:], GROW)
-    fill(T.hold[:], 1.0)
-    wait("v", g0, grow)
+    wait("s", fill(T.p33[:, 0:PW], 0.0))
+    fill(T.mul[:], GROW)
+    fill(T.rp[:], 0.0)
+    un = []
+    for out, n, c in ((T.p33[:, PW + 32:PW + 34], 2, -1), (T.cmp[:, AT[NB - 1] - 1:AT[NB]:LEN[NB - 1] + 1], 2, 0),
+                      (T.un[:, 0:H], H, FAR), (T.un[:, H:C], H, FAR), (T.acc[:, 0:FS], FS, (UNDER + 1) * UNIT),
+                      (T.acc[:, NB:32], 32 - NB, 0), (T.sg[:, 0:1], 1, UNDER - 2 - J[FS]),
+                      (T.sg[:, SW:NS * SW:SW], NS - 1, UNDER - 2 - U), (T.sg[:, 1:NS * SW:SW], NS, 3)):
+        un.append(act(out, T.p33[:, 0:n], AF.Identity, bias=float(c)))
+    wait("v", gd)
+    m = ts(T.dj[:], T.dj[:], 31, OP.bitwise_and)
+    fill(T.rz[:], -100.0)
+    wait("v", m, g0)
+    p33 = ts(T.p33[:, PW:PW + 32], T.dj[:], 0.0, OP.is_equal, 1.0 / TINY, OP.mult)
     ts(T.pi[:, 1:2], T.pi[:, 0:1], 15, OP.bitwise_and)
-    ts(T.pi[:, 2:3], T.pi[:, 0:1], 31, OP.bitwise_and)
-    ts(T.pi[:, 3:4], T.pi[:, 0:1], 15, OP.bitwise_and, 2, OP.arith_shift_right)
-    m = ts(T.pi[:, 4:5], T.pi[:, 0:1], 3, OP.bitwise_and)
+    ts(T.pi[:, 2:3], T.pi[:, 0:1], 3, OP.bitwise_and)
+    m = ts(T.pi[:, 3:4], T.pi[:, 0:1], 15, OP.bitwise_and, 2, OP.arith_shift_right)
     wb = scan(T.wb[:], T.mul[:], T.mul[:], W0, OP.mult, OP.max)
-    wait("v", m, g1)
-    pf = copy(T.pf[:, 0:4], T.pi[:, 1:5])
-    of = copy(T.off[:], T.oi[:])
-    fill(T.p33[:, 32:34], -1.0)
-    fill(T.cmp[:, AT[NB - 1] - 1:AT[NB]:LEN[NB - 1] + 1], 0.0)
-    wait("v", wb, pf)
-    p33 = ts(T.p33[:, 0:32], T.c32[:, 0:32], x_col, OP.is_equal, 1.0 / TINY, OP.mult)
-    pf = ts(T.pf[:, 4:6], T.pf[:, 0:3:2], 1.0, OP.add)
+    wait("v", m, un[3])
+    copy(T.pf[:, 0:3], T.pi[:, 1:4])
+    cap = scan(T.cap[:], T.un[:], T.rz[:], -CAP * FAR, OP.add, OP.max)
+    wait("v", wb)
     wt = turn(T.wt[:], T.wb[:, 0:C])
-    wait("s", p33)
-    hp_first = holds(range(FS - 1, NB))
-    wait("s", wt)
-    act(T.ka[:, 3 * NB:4 * NB], T.wt[:, 0:C:16], AF.Copy, scale=GROW)
-    wait("v", g2, pf)
+    wait("v", cap)
+    pf = ts(T.pf[:, 4:6], T.pf[:, 0:3:2], 1.0, OP.add)
+    ts(T.ca[:], T.c32[:, 0:16], r_col, OP.is_gt, GROW - 1.0, OP.mult)
+    ts(T.cb[:], T.c32[:, 0:16], r_col, OP.not_equal, 2.0 ** -12, OP.max)
+    ts(T.iou[:], T.cap[:], 1.0 / C, OP.mult, (CAP + C + NAME0 - 1) * UNIT, OP.add)
+    wait("v", g1, g2)
+    of = copy(T.off[:], T.oi[:])
+    wait("v", pf)
     ts(T.w32[:, 32:64], T.c16[:], r1_col, OP.is_gt)
     ts(T.w32[:, 64:96], T.c16[:], r1_col, OP.is_equal, 2.0 ** 40, OP.mult)
     m = scan(T.ends[:], T.inc[:], T.c16[:], -1.0, OP.add, OP.max)
     ts(sc_col, r_col, 15.0, OP.is_equal, 2.0 ** -40, OP.max)
-    fill(T.acc[:, NB:32], 0.0)
+    ts(T.rep[:], T.c32[:, 0:NB], 0.0, OP.mult, r_col, OP.add)
     wait("v", lu)
     uq = quant((T.uq, T.us), 0, 128, T.ut)
     wait("v", m)
-    tt(T.w32[:, 0:32], T.w32[:, 32:64], T.w32[:, 64:96], OP.add)
-    w16 = ts(T.rep[:], T.c32[:, 0:NB], 0.0, OP.mult, r_col, OP.add)
-    pks = []
-    ka = thresholds(T.ka, T.wt[:, 0:C:16], lambda j: scales(0, 128) if j else holds(range(4)))
-    scales(128, 384)
-    scales(384, 512)
-    hp_second = holds(range(4, FS - 1))
+    w16 = tt(T.w32[:, 0:32], T.w32[:, 32:64], T.w32[:, 64:96], OP.add)
+    ts(T.cum[:, 0:1], T.c32[:, 0:1], 0.0, OP.add)
+    ts(T.mb[:, C:C + 1], T.c32[:, 0:1], LAST * UNIT, OP.add)
+    ts(T.stp[:, 0:STEPS:STEPS - 1], T.c32[:, 0:2], LEAVE * UNIT, OP.mult)
+    wait("s", p33, un[0])
+    hp_first = holds(range(CU, NB))
+    holds(range(CU - 1, CU - 6, -1))
+    pks = [scales(a, e) for a, e in ((0, 128), (128, 384), (384, 512))]
+    hp_second = holds(range(CU - 6, -1, -1))
     wait("v", uq, of)
     pk = [picks(0, 128)]
+    et = [unit_tile(0)]
 
     def own(c):
         return T.tc[:, 16 * c:16 * c + 1]
 
-    def compare(c, rows):
+    def compare(c, rows, a=0):
         n = min(LEN[c] + 1, C - J[c])
-        return ts(T.cmp[:, AT[c]:AT[c] + n], rows[:, 0:n], own(c), OP.is_ge, TINY * UNIT, OP.mult)
+        return ts(T.cmp[:, AT[c]:AT[c] + n], rows[:, a:a + n], own(c), OP.is_ge, TINY * UNIT, OP.mult)
 
     def count(a, b):
         return scan(T.cnt[:, AT[a]:AT[b]], T.hold[:, AT[a]:AT[b]], T.cmp[:, AT[a]:AT[b]], 0.0, OP.mult, OP.add)
@@ -268,20 +280,13 @@ def rank_program(g, core, T, topo):
     xa = quant(xqs[0], U, C, T.x0)
     pk.append(picks(128, 384))
     first = first_scores(xqs[0], xa)
-    wait("v", w16, ka)
+    wait("v", w16)
     scan(T.ew[:], T.w32[:, 0:32], T.ends[:], 0.0, OP.mult, OP.add)
-    m = tt(T.kr[:], T.ka[:, 2 * NB:3 * NB], T.ka[:, 3 * NB:4 * NB], OP.subtract)
-    wait("v", first[0])
-    tu = turn(T.tc[:, U:C], bank[0][:, 0:C - U])
     wait("v", lx[1])
     xb = quant(xqs[0], 0, U, T.x0)
-    wait("v", m)
-    m = tt(T.st[:], T.jr[:], T.kr[:], OP.add)
-    ts(T.eo[:], T.ew[:, 15:32:16], sc_col, OP.mult, float(AT[NB] - 1), OP.min)
+    wait("v", first[0])
+    tu = turn(T.tc[:, U:C], bank[0][:, 0:C - U])
     pk.append(picks(384, 512))
-    wait("v", m)
-    sums = ts(T.sg[:, 0:NS * SW:SW], T.st[:, FS:NB], -8.0, OP.add)
-    ts(T.acc[:, 0:FS], T.st[:, 0:FS], UNIT, OP.mult)
 
     for t, mask_t in enumerate(ROUNDS):
         peer = T.cores[rank ^ mask_t]
@@ -290,7 +295,6 @@ def rank_program(g, core, T, topo):
         xq, xn = xqs[t], xqs[t + 1]
         aq = (T["aq%d" % t], T["as%d" % t])
         snd, land = T["snd%d" % t], T["land%d" % t]
-        win, nxt = T["win%d" % (t % 2)], T["win%d" % ((t + 1) % 2)]
         last = t == len(ROUNDS) - 1
 
         def send(out, in_, to):
@@ -299,31 +303,33 @@ def rank_program(g, core, T, topo):
             cnt["left"] += ne
             return (to, cnt[to], {to: cnt[to]}, to)
 
+        wait("g", xa)
+        send(aq[0][:, U:C].bitcast(dt.uint8), xq[0][:, U:C].bitcast(dt.uint8), "aq%d" % t)
         wait("g", xb)
-        send(aq[0][:, 0:EARLY].bitcast(dt.uint8), xq[0][:, 0:EARLY].bitcast(dt.uint8), "aq%d" % t)
+        send(aq[1][:], xq[1][:], "aq%d" % t)
         if t == 0:
-            unit_tile(2)
-            et = unit_tile(3)
+            et += [unit_tile(b) for b in range(1, 4)]
 
-        wide = [max(LEN[h:FS:2]) + 2 for h in range(2)]
         wait("p", xb)
-        ml = mx(bank[5][:, 0:U], rows16, cols(xq, 0, U))
         mes = mx(bank[4][:, 0:U], even32, cols(xq, 0, U))
-        mev = mx(bank[6][:, 0:wide[0]], even32, cols(xq, 0, wide[0]))
+        ml = mx(bank[5][:, 0:U], rows16, cols(xq, 0, U))
+        mev = mx(bank[6][:, 0:U + 34], even32, cols(xq, 0, U + 34))
+        wait("p", tu)
+        mov = mx(bank[0][:, 0:U + 2], odd32, cols(xq, 0, U + 2))
         mos = mx(bank[7][:, 0:U], odd32, cols(xq, 0, U))
-        wait("p", tu, pk, pks)
-        mov = mx(bank[0][:, 0:wide[1]], odd32, cols(xq, 0, wide[1]))
+        wait("p", pk, pks)
         mw = mx(bank[3][:, 0:C], sign16, cols(xq, 0, C))
 
         wait("v", tu, first)
-        early = [compare(c, bank[1 + c % 2]) for c in range(FS, NB)]
-        if t == 0:
-            wait("v", sums)
-            sums = tt(T.sg[:, 1:NS * SW:SW], T.st[:, FS:NB], T.sg[:, 0:NS * SW:SW], OP.subtract)
+        early = [compare(c, bank[1 + c % 2]) for c in range(FS + 1, NB)]
+        wait("v", early[2], hp_first)
+        count(FS + 1, FS + 4)
         wait("v", ml)
         tl = turn(T.tc[:, 0:U], bank[5][:, 0:U])
+        if t == 0:
+            ts(T.eo[:], T.ew[:, 15:32:16], sc_col, OP.mult, float(AT[NB] - 1), OP.min)
 
-        order = [c for h in range(2) for c in range(FS, NB) if c % 2 == h]
+        order = [c for h in range(2) for c in range(NB - 1, FS - 1, -1) if c % 2 == h]
         wait("s", tu, mes)
         signs = []
         for n in range(NS + LAG):
@@ -332,103 +338,97 @@ def rank_program(g, core, T, topo):
                 if c % 2:
                     wait("s", mos)
                 a = SW * (c - FS)
-                signs.append(act(T.sg[:, a + 2:a + SW], bank[4 + 3 * (c % 2)][:, 0:U], AF.Sign, bias=own(c), scale=-1.0))
+                signs.append(act(T.sg[:, a + 2:a + 2 + J[c]], bank[4 + 3 * (c % 2)][:, 0:J[c]], AF.Sign, bias=own(c),
+                                 scale=-1.0))
             if n >= LAG:
                 c = order[n - LAG]
                 a = SW * (c - FS)
-                wait("s", signs[n - LAG], sums)
-                summed = act(T.sr[:, a:a + SW], T.sg[:, a:a + SW], AF.Relu, scale=UNIT, accum_out=T.acc[:, c:c + 1])
+                wait("s", signs[n - LAG])
+                summed = act(T.sr[:, a:a + 2 + J[c]], T.sg[:, a:a + 2 + J[c]], AF.Relu, scale=UNIT,
+                             accum_out=T.acc[:, c:c + 1])
 
-        if t == 0:
-            wait("v", gz)
-            ts(T.cap[:], T.zb[:, 0:C], CAP * C * UNIT, OP.add)
-            ts(T.cum[:, 0:1], T.zb[:, 0:1], 0.0, OP.add)
-        wait("v", early, hp_first)
-        count(FS, NB)
+        wait("v", early)
+        count(FS + 4, NB)
         wait("v", tl, mev)
-        for c in range(0, FS, 2):
+        for c in range(0, CU, 2):
             compare(c, bank[6])
         wait("v", mov)
-        m = [compare(c, bank[0]) for c in range(1, CU, 2)]
-        wait("v", m[-2], hp_second)
+        m = [compare(c, bank[6 * (1 - c % 2)], J[c]) for c in list(range(1, CU - 1, 2)) + [CU, CU - 1]]
+        wait("v", m[-3], hp_second)
         count(0, CU - 1)
         wait("v", m[-1])
-        counted = count(CU - 1, FS)
+        counted = count(CU - 1, FS + 1)
         wait("v", mw)
-        want = ts(T.want[:], bank[3][:, 0:C], 0.0, OP.is_gt, C * UNIT, OP.mult)
+        want = ts(T.want[:], bank[3][:, 0:C], 0.0, OP.is_le, FAR, OP.mult)
         wait("v", counted, summed)
         sn = tt(snd[:], T.cnt[:, 0:AT[NB]].indirect(T.eo[:]), T.acc[:], OP.subtract)
         wait("g", sn)
         at = send(land[:], snd[:, 0:NB], "at%d" % t)
-        send(aq[0][:, EARLY:C].bitcast(dt.uint8), xq[0][:, EARLY:C].bitcast(dt.uint8), "aq%d" % t)
-        arrived = send(aq[1][:], xq[1][:], "aq%d" % t)
+        arrived = send(aq[0][:, 0:U].bitcast(dt.uint8), xq[0][:, 0:U].bitcast(dt.uint8), "aq%d" % t)
 
-        wait("v", want)
-        cum = scan(T.cum[:, 1:C + 1], T.want[:], T.cap[:], 0.0, OP.add, OP.min)
+        def unit_codes(b):
+            if t == 0:
+                wait("v", et[b])
+                eqm.append(quant(eq, 128 * b, 128 * b + 128, T.et))
+
         if t == 0:
-            wait("s", w16)
-            wn = act(T.wn[:], T.w32[:, 0:16].indirect(T.rep[:]), AF.Copy)
-            wait("s", act(T.rz16[:], T.c16[:, 0:16], AF.Sign))
-            rz = act(T.rz[:], T.rz16[:].indirect(T.rep[:]), AF.Copy)
-            ts(T.un[:], T.zb[:, 0:C], UNIT, OP.add)
-            ts(T.rp[:], T.zb[:, 0:C], 0.0, OP.add)
+            eqm = []
+            wait("s", w16, wt)
+            act(T.ka[:, 3 * NB:4 * NB], T.wt[:, 0:C:16], AF.Copy, scale=GROW * UNIT)
+            wn = []
+            ka = thresholds(T.ka, T.wt[:, 0:C:16], 1.0 / 512, UNDER - KAPPA0, UNIT, lambda j: wn.append(act(
+                T.wn[:, H * j:H * j + H], T.w32[:, 0:16].indirect(T.rep[:, 0:10]), AF.Copy)))
+        unit_codes(0)
+        wait("v", want)
+        cum = scan(T.cum[:, 1:C + 1], T.want[:], T.cap[:], 0.0, OP.add, OP.max)
+        wait("v", sn)
+        ts(T.lo[:], snd[:, 0:NB], -FAR, OP.add, 1.0 / FAR, OP.mult)
+        if t == 0:
+            ts(sc9_col, sc_col, 1.0 / 512, OP.mult)
+            tt(T.mul[:, 0:16], T.ca[:], T.cb[:], OP.add)
         wait("v", cum)
-        take = scan(T.take[:], T.cum[:, 1:C + 1], T.cum[:, 0:C], 0.0, OP.max, OP.subtract)
+        take = [scan(T.take[:, a:e], T.cum[:, a + 1:e + 1], T.cum[:, a:e], 0.0, OP.max, OP.subtract) for a, e in PARTS]
+        if t == 0:
+            wait("v", ka)
+            tt(T.kr[:], T.ka[:, 3 * NB:4 * NB], T.ka[:, 2 * NB:3 * NB], OP.subtract)
+        m = []
+        for j, (a, e) in enumerate(PARTS):
+            wait("v", take[j])
+            m.append(turn(T.tkt[:, a:e], T.take[:, a:e]))
+
+        def names():
+            return scan(T.val[:], T.iou[:], T.take[:], 0.0, OP.max, OP.subtract)
+
+        if t > 0:
+            val = names()
         if t == 0:
             wait("v", wn)
-            wait("s", scan(T.kk[:], T.wn[:], T.wb[:, 0:C], 0.0, OP.mult, OP.add))
-            wait("s", act(T.kb[:, 3 * NB:4 * NB], T.kk[:, 15:C:16], AF.Copy, scale=sc_col))
-            wait("s", lx, thresholds(T.kb, T.kb[:, 3 * NB:4 * NB], lambda j: act(
-                run(win, 80 * j, 80 * j + 80), run(T.x0, 80 * j, 80 * j + 80), AF.Copy, scale=32.0)))
+            wait("s", lx, scan(T.kk[:], T.wn[:], T.wb[:, 0:C], 0.0, OP.mult, OP.add))
+            wait("s", thresholds(T.kb, T.kk[:, 15:C:16], sc9_col, 0, 1.0, lambda j: act(
+                run(win, 64 * j, 64 * j + 64), run(T.x0, 64 * j, 64 * j + 64), AF.Copy, scale=32.0)))
             k0 = act(T.k0[:], T.kb[:, 2 * NB:3 * NB], AF.Identity, bias=-2.0 ** 12 * UNIT, scale=2.0 ** 12 * UNIT)
-            act(run(win, H, C), run(T.x0, H, C), AF.Copy, scale=32.0)
-        wait("v", take)
-        m = turn(T.tkt[:], T.take[:])
-        if t == 0:
-            wait("v", g3)
-            ts(T.w4[:, 16:32], T.c4[:], q1_col, OP.is_gt)
-            ts(T.w4[:, 32:48], T.c4[:], q1_col, OP.is_equal, 2.0 ** 40, OP.mult)
-            ts(T.ca[:], T.c32[:, 0:16], r_col, OP.is_gt, GROW - 1.0, OP.mult)
-            ts(T.cb[:], T.c32[:, 0:16], r_col, OP.not_equal, 2.0 ** -12, OP.max)
-            made = ts(sc4_col, q_col, 3.0, OP.is_equal, 2.0 ** -40, OP.max)
-        wait("v", m, sn)
-        m = tt(T.hi[:], snd[:, 0:NB], T.tkt[:, 0:C:16], OP.add)
-        lo = tt(T.lo[:], snd[:, 0:NB], T.tkt[:, 0:C:16], OP.subtract)
-        if t == 0:
-            iou = scan(T.iou[:], T.un[:], T.zb[:, 0:C], (NAME0 - 1) * UNIT, OP.add, OP.add)
-            wait("v", made)
-            wait("s", tt(T.w4[:, 0:16], T.w4[:, 16:32], T.w4[:, 32:48], OP.add))
-            wn4 = act(T.wn4[:], T.w4[:, 0:16].indirect(T.rep[:]), AF.Copy)
-
-        wait("v", at, m)
-        m = tt(T.mid[:], land[:], T.hi[:], OP.min)
-        wait("v", iou)
-        val = scan(T.val[:], T.take[:], T.iou[:], 2.0, OP.min, OP.add)
-        wait("v", m, lo, rz)
-        m = [tt(T.rp[:, a:e:16], T.mid[:, a // 16:e // 16], T.lo[:, a // 16:e // 16], OP.max) for a, e in PARTS]
-        if t == 0:
-            ts(T.mb[:, C:C + 1], T.zb[:, 0:1], LAST * UNIT, OP.add)
-            ts(T.stp[:, 0:STEPS:STEPS - 1], T.c32[:, 0:2], LEAVE * UNIT, OP.mult)
-            tt(T.mul[:, 0:16], T.ca[:], T.cb[:], OP.add)
-            ts(sc4_col, sc4_col, 4.0 / UNIT, OP.mult)
+            act(run(win, 128, C), run(T.x0, 128, C), AF.Copy, scale=32.0)
         for j, (a, e) in enumerate(PARTS):
             wait("v", m[j])
-            m[j] = scan(T.bc[:, a:e], T.rz[:, a:e], T.rp[:, a:e], 0.0, OP.mult, OP.add)
+            m[j] = tt(T.hi[:, a // 16:e // 16], T.lo[:, a // 16:e // 16], T.tkt[:, a:e:16], OP.mult)
+        tt(T.rz[:, 0:C:16], T.tkt[:, 0:C:16], T.kr[:], OP.add)
+
+        for j, (a, e) in enumerate(PARTS):
+            wait("v", at, m[j])
+            m[j] = tt(T.rp[:, a:e:16], land[:, a // 16:e // 16], T.hi[:, a // 16:e // 16], OP.min)
         if t == 0:
-            wait("v", et)
-            quant(eq, 0, 256, T.et)
+            val = names()
+        for j, (a, e) in enumerate(PARTS):
+            wait("v", m[j])
+            m[j] = scan(T.bc[:, a:e], T.rz[:, a:e], T.rp[:, a:e], -4.0, OP.max, OP.add)
+        unit_codes(1)
         for j, (a, e) in enumerate(PARTS):
             wait("v", m[j])
             m[j] = turn(T.mb[:, a:e], T.bc[:, a:e])
-        if t == 0:
-            eqm = quant(eq, 256, 512, T.et)
+        unit_codes(2)
         for j, (a, e) in enumerate(PARTS):
             wait("v", m[j])
             m[j] = scan(T.stp[:, a + 1:e + 1], T.mb[:, a:e], T.mb[:, a + 1:e + 1], 0.0, OP.min, OP.subtract)
-        if t == 0:
-            wait("v", lv)
-            vqm = quant(vq, 0, 128, T.vt)
-            ts(zb_col, t_col, -4.0 * NAME0, OP.add)
 
         def order_scans(ks):
             return [scan(T.so[:, STEPS * k + 16 * k:STEPS * (k + 1)], T.stp[:, 16 * k:STEPS], T.mul[:, 0:STEPS - 16 * k],
@@ -440,10 +440,16 @@ def rank_program(g, core, T, topo):
         def scatter(a, b):
             return copy(T.nm[:].indirect(T.po[:, a:b]), T.val[:, 16 * a:16 * b])
 
-        wait("p", eqm, arrived, sn, signs)
-        for b in range(4):
+        def unpack(b):
+            wait("p", eqm[b], arrived, sn, signs)
             wait("s", mx(bank[4 + b][:, 0:C], cols(eq, 128 * b, 128 * b + 128), cols(aq, 0, C)))
-            window = act(elem(win, b, C, 2 * C), bank[4 + b][:, 0:C], AF.Copy, scale=32.0)
+            return act(elem(win, b, C, 2 * C), bank[4 + b][:, 0:C], AF.Copy, scale=32.0)
+
+        if t == 0:
+            wait("v", g3)
+            ts(T.w4[:, 16:32], T.c4[:], q1_col, OP.is_gt)
+            ts(T.w4[:, 32:48], T.c4[:], q1_col, OP.is_equal, 2.0 ** 40, OP.mult)
+        window = [unpack(b) for b in range(3 if t == 0 else 4)]
         wait("v", m[0], k0)
         order_scans(range(NB - 1, CU, -1))
         wait("v", m)
@@ -451,16 +457,32 @@ def rank_program(g, core, T, topo):
         order_scans([5, 4, 3])
         wait("v", upper)
         p = places(6, NB)
+        if t == 0:
+            wait("s", tt(T.w4[:, 0:16], T.w4[:, 16:32], T.w4[:, 32:48], OP.add))
+            wn4 = act(T.wn4[:], T.w4[:, 0:16].indirect(T.rep[:]), AF.Copy)
         m = order_scans([2, 1, 0])
         wait("v", p, val)
         nm = scatter(6, NB)
         wait("v", m)
-        wait("v", places(0, 6), nm)
+        p = places(0, 6)
+        if t == 0:
+            unit_codes(3)
+            window = unpack(3)
+            m = ts(sc4_col, q_col, 3.0, OP.is_equal, 2.0 ** -40, OP.max)
+        if t == 1:
+            wait("v", lv)
+            vqm = quant(vq, 0, 128, T.vt)
+        wait("v", p, nm)
         nm = scatter(0, 6)
+        if t == 0:
+            wait("v", m)
+            ts(sc4_col, sc4_col, 4.0 / UNIT, OP.mult)
+            ts(zb_col, t_col, -4.0 * NAME0, OP.add)
         wait("v", nm, wn4)
-        m = [scan(T.ns[:, a:e], T.wn4[:, a:e], T.nm[:, a:e], 0.0, OP.mult, OP.add) for a, e in PARTS]
+        pieces = ((GATHER[0], C), (U, GATHER[0]), (0, U))
+        m = [scan(T.ns[:, a:e], T.wn4[:, a:e], T.nm[:, a:e], 0.0, OP.mult, OP.add) for a, e in pieces]
         zo = []
-        for j, (a, e) in enumerate(PARTS):
+        for j, (a, e) in enumerate(pieces):
             wait("v", m[j])
             zo.append(ts(T.zo[:, a // 4:e // 4], T.ns[:, a + 3:e:4], sc4_col, OP.mult, zb_col, OP.add))
         if last:
@@ -472,9 +494,9 @@ def rank_program(g, core, T, topo):
         zv, zs = [], []
         for j, (a, e) in enumerate(PARTS):
             c = GATHER[j]
-            wait("s", zo[j], window)
+            wait("s", zo[2 * j], window)
             zs.append(act(run(T.zt, c, e), win[:].indirect(T.zo[:, c // 4:e // 4]), AF.Copy, scale=2.0 ** -5))
-            wait("v", zo[j], window)
+            wait("v", zo[j + 1], window)
             zv.append(ts(run(T.zt, a, c), win[:].indirect(T.zo[:, a // 4:c // 4]), 2.0 ** -5, OP.mult))
 
         def products(j, made):
@@ -492,12 +514,16 @@ def rank_program(g, core, T, topo):
         def add(j, b):
             a, e = PARTS[j]
             wait("v", r[j][b], z32[j])
-            m = tt(elem(nxt, b, a, e), bank[4 * j + b][:, 0:e - a], elem(T.z32, b, a, e), OP.add)
-            if (j, b) == (1, 3):
-                wait("v", m)
-                return ts(elem(T.xn, b, a, e), elem(nxt, b, a, e), 2.0 ** -5, OP.mult)
+            m = tt(elem(win, b, a, e), bank[4 * j + b][:, 0:e - a], elem(T.z32, b, a, e), OP.add)
+            if b == 3:
+                return m
             wait("s", m)
-            return act(elem(T.xn, b, a, e), elem(nxt, b, a, e), AF.Copy, scale=2.0 ** -5)
+            return act(elem(T.xn, b, a, e), elem(win, b, a, e), AF.Copy, scale=2.0 ** -5)
+
+        def last_element(j, m):
+            a, e = PARTS[j]
+            wait("v", m)
+            return ts(elem(T.xn, 3, a, e), elem(win, 3, a, e), 2.0 ** -5, OP.mult)
 
         wait("p", lw, window)
         wait("v", zv[0], zs[0])
@@ -506,12 +532,14 @@ def rank_program(g, core, T, topo):
         wait("v", zs[1])
         r.append(products(1, quant(zq, 0, U, T.zt)))
         na = [add(0, b) for b in range(4)]
-        nb = [add(1, b) for b in range(3)]
+        nb = [add(1, 0)]
+        na[3] = last_element(0, na[3])
+        nb += [add(1, 1), add(1, 2)]
         wait("v", na)
         xa = quant(xn, U, C, T.xn)
         if not last:
             first = first_scores(xn, xa)
-        nb.append(add(1, 3))
+        nb.append(last_element(1, add(1, 3)))
         if not last:
             wait("v", first[0])
             tu = turn(T.tc[:, U:C], bank[0][:, 0:C - U])
@@ -526,11 +554,18 @@ def rank_program(g, core, T, topo):
     wait("y", act(T.ysb[:, U:C], bank[0][:, 0:C - U], AF.Copy))
     dma("y", T.y[:, U:C], T.ysb[:, U:C], "out")
     wait("p", xb)
-    wait("v", mx(bank[1][:, 0:U], cols(vq, 0, 128), cols(xn, 0, U)))
-    wait("y", copy(T.ysb[:, 0:U], bank[1][:, 0:U]))
-    dma("y", T.y[:, 0:U], T.ysb[:, 0:U], "out")
+    my = [mx(bank[k][:, 0:128], cols(vq, 0, 128), cols(xn, a, a + 128)) for k, a in ((1, 0), (2, U - 128))]
+    wait("v", my[0])
+    m = copy(T.ysb[:, 0:112], bank[1][:, 0:112])
     wait("s", xb)
+    wait("y", xb)
     dma("s", run(T.oc, 0, U), T.xq3[:, 0:U].bitcast(dt.uint8), "out")
     for k in range(4):
-        dma("s", T.osc[4 * k:4 * k + 4, :], T.xs3[32 * k:32 * k + 4, :], "out")
-    wait("g", [(n, cnt[n], {n: cnt[n]}, n) for n in SEMAPHORES])
+        dma("sy"[k % 2], T.osc[4 * k:4 * k + 4, :], T.xs3[32 * k:32 * k + 4, :], "out")
+    wait("y", m)
+    dma("y", T.y[:, 0:112], T.ysb[:, 0:112], "out")
+    wait("s", my[1])
+    wait("s", act(T.ysb[:, 112:U], bank[2][:, 240 - U:128], AF.Copy))
+    dma("s", T.y[:, 112:U], T.ysb[:, 112:U], "out")
+    for n in sorted(SEMAPHORES, key=lambda n: n == "out"):
+        wait("g", (n, cnt[n], {n: cnt[n]}, n))

@@ -16,7 +16,7 @@ W0 = 8522306.0
 KAPPA0 = 1152
 UNDER = KAPPA0 + 514
 STEPS = C + 2
-TINY = 2.0 ** -30
+BIG = 2.0 ** 36
 MAGIC = 1.5 * 2.0 ** 23
 
 
@@ -35,36 +35,41 @@ LAST, LEAVE = _ends()
 
 U = 192
 CU = U // 16
-FS = CU
-J = [0] * FS + [32] + [U] * (NB - FS - 1)
-PW = U + 32
-LEN = [32 * (c // 2) + 32 - J[c] for c in range(NB)]
-AT = [sum(LEN[:c]) + c for c in range(NB + 1)]
-SW = U + 2
-NS = NB - FS
-LAG = 2
+NR = C // 32
+TOP, LOW = NR - 1, CU // 2 - 1
+HIGH, BASE, OVER, STEP, MID = 2.0 ** 26, 3 * 2.0 ** 22, 2.0 ** 34, -1.5, 256.0
+NT = TOP - LOW
+LEN = [min(32 * b + 32, U) for b in range(NR)]
+LEAD = [2] * LOW + [0] + [1] * NT
+RUN = [LEAD[b] + LEN[b] + 1 for b in range(NR)]
+TOPS = sum(RUN[:NT]) - 2
+SU, SL = sum(RUN[LOW + 1:]) + TOPS, sum(RUN[:LOW + 1])
+END = [[2 * SU + SL * h + sum(RUN[b:LOW + 1]) - 1 if b <= LOW else SU * h + sum(RUN[b:]) - 1 for h in range(2)]
+       for b in range(NR)]
+HOLD = RUN[TOP] + SL
+VE = 2
 PARTS = ((U, C), (0, U))
-GATHER = (256, 80)
+GATHER = (256, 72)
 
 X4 = "float8_e4m3fn_x4"
 SCRATCH = {}
 for _dt, _list in (
-        ("bfloat16", (("x0", 4 * C), ("xn", 4 * C), ("ut", 512), ("vt", 512), ("et", 2048), ("zt", 4 * C), ("z32", 4 * C),
-                      ("zb", 512), ("un", C), ("c32", 34), ("c16", 32), ("c4", 16), ("p33", PW + 34),
-                      ("w32", 96), ("w4", 48), ("wn", C), ("wn4", C), ("cmp", AT[NB] + 1), ("hold", AT[NB] + 1),
-                      ("cnt", AT[NB] + 1), ("sg", NS * SW), ("sr", NS * SW), ("so", NB * STEPS), ("win", 8 * C))),
-        ("float32", (("pf", 12), ("wb", STEPS), ("wt", C), ("ka", 4 * NB), ("kb", 4 * NB), ("kr", NB), ("kk", C),
-                     ("k0", NB), ("ca", 16), ("cb", 16), ("inc", 32), ("ends", 32), ("ew", 32),
-                     ("acc", 32), ("tc", C), ("lo", NB), ("hi", NB), ("nm", C), ("ns", C),
+        ("bfloat16", (("x0", 4 * C), ("xn", 4 * C), ("ut", 512), ("vt", 512), ("et", 516), ("zt", 4 * C), ("z32", 4 * C),
+                      ("zb", 516), ("un", C), ("rows", 160), ("cols", 160), ("lead", U + 3), ("mid", 32),
+                      ("w32", 96), ("w4", 4), ("n4", C), ("s4", C), ("wn4", C), ("hold", HOLD),
+                      ("cnu", 2 * SU), ("cnl", 2 * SL), ("sg", 2 * (SU + SL)), ("so", NB * STEPS), ("win", 8 * C))),
+        ("float32", (("pf", 9), ("wb", C), ("ka", 6 * NB), ("kr", NB),
+                     ("k0", NB), ("ca", 16), ("cb", 16), ("cc", 16), ("inc", 32), ("ends", 32), ("ew", 32),
+                     ("tc", C), ("lo", NB), ("hi", NB), ("nm", C), ("ns", C),
                      ("odb", C), ("ysb", C), ("snd0", 32), ("snd1", 32), ("snd2", 32),
                      ("land0", NB), ("land1", NB), ("land2", NB))),
         (HALF, (("mul", STEPS), ("rp", C), ("rz", C), ("bc", C), ("mb", C + 2), ("stp", STEPS),
                 ("cap", C), ("want", C), ("cum", C + 2), ("take", C), ("tkt", C), ("val", C), ("iou", C))),
-        ("int32", (("pi", 4), ("dj", 32), ("oi", 32))),
-        ("uint16", (("off", 32), ("rep", NB), ("eo", 2), ("po", NB), ("zo", C // 4)))):
+        ("int32", (("oi", 24),)),
+        ("uint16", (("off", 24), ("eo", 2), ("ep", 2), ("po", NB), ("zo", C // 4)))):
     for _n, _w in _list:
         SCRATCH[_n] = ("sbuf", [128, _w], _dt)
-for _q, _s, _w in (("uq", "us", 128), ("pq", "ps", 512), ("vq", "vs", 128), ("wq", "wp", 512), ("eq", "es", 512),
+for _q, _s, _w in (("uq", "us", 128), ("pq", "ps", 384), ("vq", "vs", 128), ("wq", "wp", 512), ("eq", "es", 512),
                    ("zq", "zs", C), ("xq0", "xs0", C), ("xq1", "xs1", C),
                    ("xq2", "xs2", C), ("xq3", "xs3", C), ("aq0", "as0", C), ("aq1", "as1", C), ("aq2", "as2", C)):
     SCRATCH[_q] = ("sbuf", [128, _w], X4)
@@ -75,7 +80,7 @@ for _n in BANKS:
 
 POOL = ["c%d" % _b for _b in range(130)]
 SEMAPHORES = (POOL + ["la", "lx", "lu", "lv", "lw", "out", "left"]
-              + ["%s%d" % (n, t) for n in ("aq", "at") for t in range(3)])
+              + ["%s%d" % (n, t) for n in ("aq", "au", "al") for t in range(3)])
 
 
 def rank_program(g, core, T, topo):
@@ -157,21 +162,25 @@ def rank_program(g, core, T, topo):
     def elem(tile, b, a, e):
         return tile[:, 4 * a + b:4 * e:4]
 
-    r_col, t_col, q_col, sc9_col, r1_col, q1_col, sc_col, sc4_col, zb_col = (T.pf[:, j:j + 1] for j in range(9))
+    sc_col, nq_col, zb_col, sc4_col = (T.pf[:, j:j + 1] for j in (0, 1, 2, 8))
+    half_col = [T.pf[:, j:j + 1] for j in (3, 4)]
+    c16, c16_1, c32, c4 = (T.rows[:, 32 * j:32 * j + 32] for j in range(4))
+    r1_col, x_col, t_col, q1_col = (T.cols[:, 32 * j:32 * j + 1] for j in range(1, 5))
     bank = [T[n] for n in BANKS]
     win = T.win
     eq, wq, zq, vq = (T.eq, T.es), (T.wq, T.wp), (T.zq, T.zs), (T.vq, T.vs)
-    rows16, even32, odd32, sign16 = (cols((T.pq, T.ps), 128 * j, 128 * j + 128) for j in range(4))
+    even32, odd32, sign16 = (cols((T.pq, T.ps), 128 * j, 128 * j + 128) for j in range(3))
+    plain = cols((T.uq, T.us), 0, 128)
     xqs = [(T["xq%d" % t], T["xs%d" % t]) for t in range(4)]
 
-    def thresholds(k, w, scale, less, unit, between):
-        m = act(k[:, 0:NB], w, AF.Identity, bias=MAGIC, scale=scale)
-        between(0)
-        wait("s", m)
-        m = act(k[:, NB:2 * NB], k[:, 0:NB], AF.Identity, bias=-512.0 * MAGIC, scale=512.0)
-        between(1)
-        wait("s", m)
-        return act(k[:, 2 * NB:3 * NB], k[:, NB:2 * NB], AF.Identity, bias=(257.5 - less) * unit, scale=GROW * unit)
+    ka, members, steps = [T.ka[:, NB * j:NB * j + NB] for j in range(6)], T.wb[:, 15:C:16], []
+
+    def thresholds(j):
+        wait("s", wb, steps)
+        if j == 0:
+            act(ka[4], members, AF.Identity, bias=(UNDER - KAPPA0) * UNIT, scale=GROW * UNIT)
+        bias, scale = ((MAGIC, 1.0 / 512), (-512.0 * MAGIC, 512.0), (257.5 * UNIT, GROW * UNIT))[j]
+        steps.append(act(ka[j], ka[j - 1] if j else members, AF.Identity, bias=bias, scale=scale))
 
     def picks(a, e):
         return copy(T.pq[:, a:e].bitcast(dt.uint32), T.uq[:].bitcast(dt.uint32).indirect(T.off[:, a // 16:e // 16]))
@@ -180,14 +189,9 @@ def rank_program(g, core, T, topo):
         wait("s", uq, of)
         return act(T.ps[:, a:e], T.us[:].indirect(T.off[:, a // 16:e // 16]), AF.Copy)
 
-    def holds(cs):
-        return [act(T.hold[:, AT[c] + min(c, 1):AT[c + 1] + 1], T.p33[:, PW + 31 - LEN[c] + min(c, 1):PW + 33], AF.Identity,
-                    bias=1.0) for c in cs]
-
-    def unit_tile(b):
-        wait("g", gz)
-        return mark("g", g.affine_select(T.et[:, 512 * b:512 * b + 512], T.zb[:], [[-1, 128], [1000, 4]], OP.not_equal,
-                                         1.0, -1000 * b, 1))
+    def holds(bs):
+        return [act(T.hold[:, e - LEN[b] - n:e], T.lead[:, 3 - n:3 + LEN[b]], AF.Identity, bias=STEP)
+                for b in bs for n, e in [(3 * (b < LOW), HOLD - sum(RUN[:b]) - 1)]]
 
     lu = dma("s", T.ut[:], T.u[:], "lu")
     lx = [dma("y", run(T.x0, a, e), run(T.x, a, e), name) for (a, e), name in zip(PARTS, ("la", "lx"))]
@@ -196,97 +200,116 @@ def rank_program(g, core, T, topo):
     lw = dma("y", T.wp[:], T.ws[:], "lw")
     lv = dma("y", T.vt[:], T.v[:], "lv")
 
-    gd = mark("g", g.iota(T.dj[:], [[1, 32]], 128, -1))
-    mark("g", g.iota(T.pi[:, 0:1], [[0, 1]], 0, 1))
-    g0 = iota(T.c32[:], [[1, 34]], 0)
-    for j, (pattern, base) in enumerate((([[16, 8]], 0), ([[32, 4], [0, 2]], 0), ([[32, 4], [0, 2]], 16), ([[16, 8]], 1))):
-        g1 = mark("g", g.iota(T.oi[:, 8 * j:8 * j + 8], pattern, base, 0))
-    iota(T.c16[:], [[0, 2], [1, 16]], 0)
-    iota(T.inc[:, 0:CU], [[32, CU // 2], [0, 2]], LEN[0] + 1)
-    iota(T.inc[:, CU:CU + 2], [[LEN[CU + 1] - LEN[CU], 2]], LEN[CU] + 1)
-    g2 = iota(T.inc[:, CU + 2:32], [[32, 15 - CU // 2], [0, 2]], LEN[CU + 2] + 1)
-    g3 = iota(T.c4[:], [[0, 4], [1, 4]], 0)
-    gz = iota(T.zb[:], [[0, 512]], 0)
-    wait("s", fill(T.p33[:, 0:PW], 0.0))
+    mark("g", g.iota(T.oi[:, 0:16], [[16, 2], [32, 4], [0, 2]], 0, 0))
+    g1 = mark("g", g.iota(T.oi[:, 16:24], [[16, 8]], 1, 0))
+    iota(T.rows[:, 0:64], [[1, 2], [0, 2], [1, 16]], 0)
+    g0 = iota(c32, [[1, 32]], 0)
+    iota(T.inc[:, 1:32:2], [[SL - SU, 2], [0, 8]], SU)
+    iota(T.inc[:, 0:8:2], [[0, NT]], -RUN[TOP] - SU)
+    iota(T.inc[:, 8:9], [[0, 1]], SU - 1 - END[TOP][1])
+    iota(T.inc[:, 10:16:2], [[-32, NT - 1]], -RUN[0] - SU)
+    iota(T.inc[:, 16:17], [[0, 1]], END[0][0] - 2 * SU + TOPS - LEN[NT - 1])
+    g2 = iota(T.inc[:, 18:32:2], [[-32, 7]], -RUN[0] - SL)
+    iota(c4, [[0, 8], [1, 4]], 0)
+    g3 = iota(T.rows[:, 128:160], [[0, 2], [1, 4], [0, 4]], 1)
+    gz = iota(T.zb[:], [[0, 516]], 0)
+    wait("s", fill(T.lead[:, 35:U + 3], 0.0))
     fill(T.mul[:], GROW)
     fill(T.rp[:], 0.0)
+    rz = fill(T.rz[:], -100.0)
     un = []
-    for out, n, c in ((T.p33[:, PW + 32:PW + 34], 2, -1), (T.cmp[:, AT[NB - 1] - 1:AT[NB]:LEN[NB - 1] + 1], 2, 0),
-                      (T.un[:, 0:H], H, FAR), (T.un[:, H:C], H, FAR), (T.acc[:, 0:FS], FS, (UNDER + 1) * UNIT),
-                      (T.acc[:, NB:32], 32 - NB, 0), (T.sg[:, 0:1], 1, UNDER - 2 - J[FS]),
-                      (T.sg[:, SW:NS * SW:SW], NS - 1, UNDER - 2 - U), (T.sg[:, 1:NS * SW:SW], NS, 3)):
-        un.append(act(out, T.p33[:, 0:n], AF.Identity, bias=float(c)))
-    wait("v", gd)
-    m = ts(T.dj[:], T.dj[:], 31, OP.bitwise_and)
-    fill(T.rz[:], -100.0)
-    wait("v", m, g0)
-    p33 = ts(T.p33[:, PW:PW + 32], T.dj[:], 0.0, OP.is_equal, 1.0 / TINY, OP.mult)
-    ts(T.pi[:, 1:2], T.pi[:, 0:1], 15, OP.bitwise_and)
-    ts(T.pi[:, 2:3], T.pi[:, 0:1], 3, OP.bitwise_and)
-    m = ts(T.pi[:, 3:4], T.pi[:, 0:1], 15, OP.bitwise_and, 2, OP.arith_shift_right)
-    wb = scan(T.wb[:], T.mul[:], T.mul[:], W0, OP.mult, OP.max)
-    wait("v", m, un[3])
-    copy(T.pf[:, 0:3], T.pi[:, 1:4])
-    cap = scan(T.cap[:], T.un[:], T.rz[:], -CAP * FAR, OP.add, OP.max)
-    wait("v", wb)
-    wt = turn(T.wt[:], T.wb[:, 0:C])
-    wait("v", cap)
-    pf = ts(T.pf[:, 4:6], T.pf[:, 0:3:2], 1.0, OP.add)
-    ts(T.ca[:], T.c32[:, 0:16], r_col, OP.is_gt, GROW - 1.0, OP.mult)
-    ts(T.cb[:], T.c32[:, 0:16], r_col, OP.not_equal, 2.0 ** -12, OP.max)
-    ts(T.iou[:], T.cap[:], 1.0 / C, OP.mult, (CAP + C + NAME0 - 1) * UNIT, OP.add)
-    wait("v", g1, g2)
+    for out, n, c in ((T.un[:, 0:H], H, FAR), (T.un[:, H:C], H, FAR), (T.mid[:], 32, MID),
+                      (T.lead[:, 0:1], 1, -BASE), (T.lead[:, 1:2], 1, OVER), (T.lead[:, 2:3], 1, HIGH - OVER),
+                      (T.hold[:, U + 1:HOLD:SL], 2, -BASE), (T.hold[:, 0:1], 1, BASE),
+                      (T.hold[:, 1:U // 2], U // 2 - 1, STEP), (T.hold[:, U // 2:U + 1], U // 2 + 1, STEP)):
+        un.append(act(out, T.lead[:, 35:35 + n], AF.Identity, bias=float(c)))
+    wait("v", g1)
     of = copy(T.off[:], T.oi[:])
-    wait("v", pf)
-    ts(T.w32[:, 32:64], T.c16[:], r1_col, OP.is_gt)
-    ts(T.w32[:, 64:96], T.c16[:], r1_col, OP.is_equal, 2.0 ** 40, OP.mult)
-    m = scan(T.ends[:], T.inc[:], T.c16[:], -1.0, OP.add, OP.max)
-    ts(sc_col, r_col, 15.0, OP.is_equal, 2.0 ** -40, OP.max)
-    ts(T.rep[:], T.c32[:, 0:NB], 0.0, OP.mult, r_col, OP.add)
+    wait("v", g0)
+    m = turn(T.cols[:, 32:96], T.rows[:, 32:96])
+    wait("v", un[1], rz)
+    scan(T.cap[:], T.un[:], T.rz[:], -CAP * FAR, OP.add, OP.max)
+    wait("v", m)
+    lead = ts(T.lead[:, 3:35], c32[:, ::-1], x_col, OP.is_equal, BASE - HIGH, OP.mult)
+    ts(T.w32[:, 32:64], c16, r1_col, OP.is_gt)
+    ts(T.w32[:, 64:96], c16, r1_col, OP.is_equal, 2.0 ** 40, OP.mult)
+    m = ts(T.cc[:], c16_1[:, 15::-1], r1_col, OP.is_gt, 1.0 - GROW, OP.mult)
+    ts(sc_col, r1_col, 16.0, OP.is_equal, 2.0 ** -40, OP.max)
     wait("v", lu)
     uq = quant((T.uq, T.us), 0, 128, T.ut)
-    wait("v", m)
-    w16 = tt(T.w32[:, 0:32], T.w32[:, 32:64], T.w32[:, 64:96], OP.add)
-    ts(T.cum[:, 0:1], T.c32[:, 0:1], 0.0, OP.add)
-    ts(T.mb[:, C:C + 1], T.c32[:, 0:1], LAST * UNIT, OP.add)
-    ts(T.stp[:, 0:STEPS:STEPS - 1], T.c32[:, 0:2], LEAVE * UNIT, OP.mult)
-    wait("s", p33, un[0])
-    hp_first = holds(range(CU, NB))
-    holds(range(CU - 1, CU - 6, -1))
-    pks = [scales(a, e) for a, e in ((0, 128), (128, 384), (384, 512))]
-    hp_second = holds(range(CU - 6, -1, -1))
+    wait("v", m, g2)
+    tt(T.w32[:, 0:32], T.w32[:, 32:64], T.w32[:, 64:96], OP.add)
+    m = scan(T.ends[:], T.inc[:], c16, float(END[LOW + 1][0] + RUN[TOP] + SU), OP.add, OP.max)
+    ts(T.mul[:, 0:16], T.cc[:], GROW, OP.add)
+    wait("s", lead, un[5])
+    holds([LOW, LOW - 1])
+    pks = [scales(a, e) for a, e in ((0, 256), (256, 384))]
+    held = holds(range(LOW - 2, -1, -1))
     wait("v", uq, of)
-    pk = [picks(0, 128)]
-    et = [unit_tile(0)]
+    pk = [picks(0, 256)]
+    wait("v", m)
+    m = scan(T.ew[:], T.w32[:, 0:32], T.ends[:], 0.0, OP.mult, OP.add)
 
-    def own(c):
-        return T.tc[:, 16 * c:16 * c + 1]
+    def own(b, h):
+        return T.tc[:, 32 * b + 16 * h:32 * b + 16 * h + 1]
 
-    def compare(c, rows, a=0):
-        n = min(LEN[c] + 1, C - J[c])
-        return ts(T.cmp[:, AT[c]:AT[c] + n], rows[:, a:a + n], own(c), OP.is_ge, TINY * UNIT, OP.mult)
+    def top_end(b, h):
+        return SU * (h + 1) - 1 - sum(RUN[:b - LOW - 1])
 
-    def count(a, b):
-        return scan(T.cnt[:, AT[a]:AT[b]], T.hold[:, AT[a]:AT[b]], T.cmp[:, AT[a]:AT[b]], 0.0, OP.mult, OP.add)
+    def sides(b, h, top):
+        if top:
+            n, e = LEN[b - LOW - 1] + 2 * (b < TOP), top_end(b, h)
+            return T.sg[:, e - n:e], bank[1 + h][:, n - 1::-1]
+        n, e = LEN[b] + 2 * (b < LOW), END[b][h]
+        return T.sg[:, e - n:e], bank[5 + h][:, n - 1::-1]
+
+    def compare(bs, h, top=0):
+        return [ts(*sides(b, h, top), own(b, h), OP.is_lt) for b in bs]
+
+    def sign(bs, h, top=0):
+        return [act(*sides(b, h, top), AF.Sign, bias=own(b, h), scale=-1.0) for b in bs]
+
+    def count_tops(h):
+        e = SU * (h + 1)
+        return scan(T.cnu[:, e - TOPS:e], T.sg[:, e - TOPS:e], T.hold[:, HOLD - TOPS:HOLD], HIGH, OP.add, OP.add)
+
+    def count_upper(b, h):
+        a, e = END[b][h] + 1 - RUN[b], END[b][h] + 1
+        return scan(T.cnu[:, a:e], T.sg[:, a:e], T.hold[:, 0:RUN[b]], T.cnu[:, top_end(b, h):top_end(b, h) + 1],
+                    OP.add, OP.add)
+
+    def count_lower(a, b, h):
+        s, e = sum(RUN[a + 1:LOW + 1]), sum(RUN[b:LOW + 1])
+        o = 2 * SU + SL * h
+        return scan(T.cnl[:, SL * h + s:SL * h + e], T.sg[:, o + s:o + e], T.hold[:, RUN[TOP] + s:RUN[TOP] + e],
+                    HIGH * (a == LOW), OP.add, OP.add)
 
     def first_scores(xq, made):
-        m = []
-        for j, side in enumerate((rows16, even32, odd32)):
-            wait("p", pk[min(j, 1)], pks[min(j, 1)], made)
-            m.append(mx(bank[j][:, 0:C - U], side, cols(xq, U, C)))
+        wait("p", uq, made)
+        m = [mx(bank[0][:, 0:C - U], plain, cols(xq, U, C))]
+        for j, side in enumerate((even32, odd32, sign16)):
+            wait("p", pk[j // 2], pks[j // 2])
+            m.append(mx(bank[1 + j][:, 0:C - U], side, cols(xq, U, C)))
         return m
+
+    lower, upper = range(LOW, -1, -1), range(TOP, LOW, -1)
 
     wait("v", lx[0])
     xa = quant(xqs[0], U, C, T.x0)
-    pk.append(picks(128, 384))
+    pk.append(picks(256, 384))
     first = first_scores(xqs[0], xa)
-    wait("v", w16)
-    scan(T.ew[:], T.w32[:, 0:32], T.ends[:], 0.0, OP.mult, OP.add)
+    wait("v", m)
+    eo = ts(T.eo[:], T.ew[:, 15:32:16], sc_col, OP.mult)
+    ts(T.ep[:, 0:1], T.ew[:, 31:32], sc_col, OP.mult, -2.0 * SU, OP.add)
     wait("v", lx[1])
     xb = quant(xqs[0], 0, U, T.x0)
+    wait("v", eo, un)
+    slots = copy(T.sg[:].indirect(T.eo[:]), T.mid[:])
     wait("v", first[0])
     tu = turn(T.tc[:, U:C], bank[0][:, 0:C - U])
-    pk.append(picks(384, 512))
+    wb = scan(T.wb[:], T.mul[:, 0:C], T.mul[:, 0:C], W0, OP.mult, OP.max)
+    wait("s", slots)
+    slots = [act(T.sg[:, SU * h:SU * h + NT * RUN[TOP]:RUN[TOP]], T.mid[:, 0:NT], AF.Copy, scale=-1.0) for h in range(2)]
 
     for t, mask_t in enumerate(ROUNDS):
         peer = T.cores[rank ^ mask_t]
@@ -308,127 +331,139 @@ def rank_program(g, core, T, topo):
         wait("g", xb)
         send(aq[1][:], xq[1][:], "aq%d" % t)
         if t == 0:
-            et += [unit_tile(b) for b in range(1, 4)]
+            wait("g", gz)
+            et = mark("g", g.affine_select(T.et[:], T.zb[:], [[-1, 516]], OP.not_equal, 1.0, 3, 4))
+            g4 = iota(T.n4[:], [[0, C // 4], [1, 4]], 1)
 
         wait("p", xb)
-        mes = mx(bank[4][:, 0:U], even32, cols(xq, 0, U))
-        ml = mx(bank[5][:, 0:U], rows16, cols(xq, 0, U))
-        mev = mx(bank[6][:, 0:U + 34], even32, cols(xq, 0, U + 34))
-        wait("p", tu)
-        mov = mx(bank[0][:, 0:U + 2], odd32, cols(xq, 0, U + 2))
-        mos = mx(bank[7][:, 0:U], odd32, cols(xq, 0, U))
-        wait("p", pk, pks)
-        mw = mx(bank[3][:, 0:C], sign16, cols(xq, 0, C))
+        second = {k: mx(bank[k][:, 0:U], side, cols(xq, 0, U)) for k, side in ((5, even32), (4, plain), (6, odd32), (7, sign16))}
 
-        wait("v", tu, first)
-        early = [compare(c, bank[1 + c % 2]) for c in range(FS + 1, NB)]
-        wait("v", early[2], hp_first)
-        count(FS + 1, FS + 4)
-        wait("v", ml)
-        tl = turn(T.tc[:, 0:U], bank[5][:, 0:U])
+        wait("s", tu, first[1])
+        s_top = sign(upper, 0, 1)
+        wait("v", tu, first[2])
+        v_top = compare(upper, 1, 1)
+        wait("v", first[3])
+        ts(T.want[:, U:C], bank[3][:, 0:C - U], 0.0, OP.is_le, FAR, OP.mult)
         if t == 0:
-            ts(T.eo[:], T.ew[:, 15:32:16], sc_col, OP.mult, float(AT[NB] - 1), OP.min)
+            ts(half_col[0], x_col, 16.0, OP.is_lt)
+            ts(half_col[1], x_col, 16.0, OP.is_ge)
+        wait("v", s_top, held)
+        tops = [count_tops(0)]
+        wait("v", v_top)
+        tops.append(count_tops(1))
+        wait("v", second[4])
+        tl = turn(T.tc[:, 0:U], bank[4][:, 0:U])
+        wait("s", second[5], slots)
+        s_even = sign(upper, 0)
+        wait("s", second[6])
+        s_odd = sign(upper, 1)
+        wait("s", tl)
+        s_low = []
+        for j, b in enumerate(lower):
+            if t == 0 and j % 2 == 0:
+                thresholds(j // 2)
+            s_low += sign([b], 1)
 
-        order = [c for h in range(2) for c in range(NB - 1, FS - 1, -1) if c % 2 == h]
-        wait("s", tu, mes)
-        signs = []
-        for n in range(NS + LAG):
-            if n < NS:
-                c = order[n]
-                if c % 2:
-                    wait("s", mos)
-                a = SW * (c - FS)
-                signs.append(act(T.sg[:, a + 2:a + 2 + J[c]], bank[4 + 3 * (c % 2)][:, 0:J[c]], AF.Sign, bias=own(c),
-                                 scale=-1.0))
-            if n >= LAG:
-                c = order[n - LAG]
-                a = SW * (c - FS)
-                wait("s", signs[n - LAG])
-                summed = act(T.sr[:, a:a + 2 + J[c]], T.sg[:, a:a + 2 + J[c]], AF.Relu, scale=UNIT,
-                             accum_out=T.acc[:, c:c + 1])
+        def counts(js, h, made):
+            for j in js:
+                wait("v", made[j], tops[h])
+                m = count_upper(upper[j], h)
+            return m
 
-        wait("v", early)
-        count(FS + 4, NB)
-        wait("v", tl, mev)
-        for c in range(0, CU, 2):
-            compare(c, bank[6])
-        wait("v", mov)
-        m = [compare(c, bank[6 * (1 - c % 2)], J[c]) for c in list(range(1, CU - 1, 2)) + [CU, CU - 1]]
-        wait("v", m[-3], hp_second)
-        count(0, CU - 1)
-        wait("v", m[-1])
-        counted = count(CU - 1, FS + 1)
-        wait("v", mw)
-        want = ts(T.want[:], bank[3][:, 0:C], 0.0, OP.is_le, FAR, OP.mult)
-        wait("v", counted, summed)
-        sn = tt(snd[:], T.cnt[:, 0:AT[NB]].indirect(T.eo[:]), T.acc[:], OP.subtract)
-        wait("g", sn)
-        at = send(land[:], snd[:, 0:NB], "at%d" % t)
+        def part(j):
+            a, e = PARTS[j]
+            return snd[:, 16 * j:16 * j + (e - a) // 16]
+
+        def table(j, to):
+            a, e = PARTS[j]
+            sn.append(ts(snd[:, 16 * j:16 * j + 16], (T.cnu, T.cnl)[j][:].indirect((T.eo, T.ep)[j][:, 0:1]),
+                         -0.5 * UNIT, OP.mult, (MID / 2 - UNDER) * UNIT, OP.add))
+            wait("g", sn)
+            at.append(send(land[:, a // 16:e // 16], part(j), to))
+
+        def entries(j):
+            a, e = PARTS[j]
+            return ts(T.lo[:, a // 16:e // 16], part(j), -FAR, OP.add, 1.0 / FAR, OP.mult)
+
+        sn, at = [], []
+        if t == 0:
+            ts(T.cum[:, 0:1], c16[:, 0:1], 0.0, OP.add)
+        counts(range(2), 0, s_even)
+        wait("v", second[7])
+        want = ts(T.want[:, 0:U], bank[7][:, 0:U], 0.0, OP.is_le, FAR, OP.mult)
+        counts(range(2, NT), 0, s_even)
+        wait("v", tl)
+        v_low = compare(lower[:1], 0)
+        counts(range(2), 1, s_odd)
+        v_low += compare(lower[1:VE], 0)
+        wait("s", v_low)
+        signs = sign(lower[VE:], 0)
+        counted = counts(range(2, NT), 1, s_odd)
+        wait("v", want)
+        cum = scan(T.cum[:, 1:C + 1], T.want[:], T.cap[:], 0.0, OP.add, OP.max)
+        wait("v", counted)
+        table(0, "au%d" % t)
+        count_lower(LOW, LOW + 1 - VE, 0)
+        if t == 0:
+            wait("v", steps)
+            wait("s", tt(ka[5], ka[4], ka[2], OP.subtract), lx)
+            half = [act(ka[h][:, 0:NR], ka[5][:, h:NB:2], AF.Copy, scale=half_col[h]) for h in range(2)]
+            k0 = act(T.k0[:], ka[2], AF.Identity, bias=-2.0 ** 12 * UNIT, scale=2.0 ** 12)
+            act(run(win, 0, C), run(T.x0, 0, C), AF.Copy, scale=32.0)
+        wait("v", cum)
+        take = [scan(T.take[:, a:e], T.cum[:, a + 1:e + 1], T.cum[:, a:e], 0.0, OP.max, OP.subtract) for a, e in PARTS]
+        wait("v", s_low)
+        count_lower(LOW, 0, 1)
+        wait("v", signs)
+        counted = count_lower(LOW - VE, 0, 0)
+        wait("v", take)
+        tkt = [turn(T.tkt[:, a:e], T.take[:, a:e]) for a, e in PARTS]
+        lo = entries(0)
+        wait("v", counted)
+        table(1, "al%d" % t)
         arrived = send(aq[0][:, 0:U].bitcast(dt.uint8), xq[0][:, 0:U].bitcast(dt.uint8), "aq%d" % t)
 
         def unit_codes(b):
             if t == 0:
-                wait("v", et[b])
-                eqm.append(quant(eq, 128 * b, 128 * b + 128, T.et))
+                wait("v", et)
+                eqm.append(mark("v", V.quantize_mx(*cols(eq, 128 * b, 128 * b + 128), T.et[:, 3 - b:515 - b])))
 
-        if t == 0:
-            eqm = []
-            wait("s", w16, wt)
-            act(T.ka[:, 3 * NB:4 * NB], T.wt[:, 0:C:16], AF.Copy, scale=GROW * UNIT)
-            wn = []
-            ka = thresholds(T.ka, T.wt[:, 0:C:16], 1.0 / 512, UNDER - KAPPA0, UNIT, lambda j: wn.append(act(
-                T.wn[:, H * j:H * j + H], T.w32[:, 0:16].indirect(T.rep[:, 0:10]), AF.Copy)))
-        unit_codes(0)
-        wait("v", want)
-        cum = scan(T.cum[:, 1:C + 1], T.want[:], T.cap[:], 0.0, OP.add, OP.max)
-        wait("v", sn)
-        ts(T.lo[:], snd[:, 0:NB], -FAR, OP.add, 1.0 / FAR, OP.mult)
-        if t == 0:
-            ts(sc9_col, sc_col, 1.0 / 512, OP.mult)
-            tt(T.mul[:, 0:16], T.ca[:], T.cb[:], OP.add)
-        wait("v", cum)
-        take = [scan(T.take[:, a:e], T.cum[:, a + 1:e + 1], T.cum[:, a:e], 0.0, OP.max, OP.subtract) for a, e in PARTS]
-        if t == 0:
-            wait("v", ka)
-            tt(T.kr[:], T.ka[:, 3 * NB:4 * NB], T.ka[:, 2 * NB:3 * NB], OP.subtract)
-        m = []
-        for j, (a, e) in enumerate(PARTS):
-            wait("v", take[j])
-            m.append(turn(T.tkt[:, a:e], T.take[:, a:e]))
+        def bound(j):
+            a, e = PARTS[j]
+            return tt(T.hi[:, a // 16:e // 16], T.lo[:, a // 16:e // 16], T.tkt[:, a:e:16], OP.mult)
+
+        def back(j):
+            a, e = PARTS[j]
+            return tt(T.rz[:, a:e:16], T.tkt[:, a:e:16], T.kr[:, a // 16:e // 16], OP.add)
 
         def names():
             return scan(T.val[:], T.iou[:], T.take[:], 0.0, OP.max, OP.subtract)
 
-        if t > 0:
-            val = names()
         if t == 0:
-            wait("v", wn)
-            wait("s", lx, scan(T.kk[:], T.wn[:], T.wb[:, 0:C], 0.0, OP.mult, OP.add))
-            wait("s", thresholds(T.kb, T.kk[:, 15:C:16], sc9_col, 0, 1.0, lambda j: act(
-                run(win, 64 * j, 64 * j + 64), run(T.x0, 64 * j, 64 * j + 64), AF.Copy, scale=32.0)))
-            k0 = act(T.k0[:], T.kb[:, 2 * NB:3 * NB], AF.Identity, bias=-2.0 ** 12 * UNIT, scale=2.0 ** 12 * UNIT)
-            act(run(win, 128, C), run(T.x0, 128, C), AF.Copy, scale=32.0)
-        for j, (a, e) in enumerate(PARTS):
-            wait("v", m[j])
-            m[j] = tt(T.hi[:, a // 16:e // 16], T.lo[:, a // 16:e // 16], T.tkt[:, a:e:16], OP.mult)
-        tt(T.rz[:, 0:C:16], T.tkt[:, 0:C:16], T.kr[:], OP.add)
+            eqm = []
+            wait("v", half)
+            kr = [tt(T.kr[:, h:NB:2], ka[0][:, 0:NR], ka[1][:, 0:NR], OP.add) for h in range(2)]
+        else:
+            val = names()
+        wait("v", tkt[0], lo)
+        m = [bound(0)]
+        if t == 0:
+            wait("v", g3)
+            turned = turn(T.cols[:, 96:160], T.rows[:, 96:160])
+            ts(T.ca[:], c16[:, 0:16], r1_col, OP.is_ge, GROW - 1.0, OP.mult)
+        wait("v", kr)
+        back(0)
+        wait("v", sn, tkt)
+        lo = entries(1)
+        back(1)
 
-        for j, (a, e) in enumerate(PARTS):
-            wait("v", at, m[j])
-            m[j] = tt(T.rp[:, a:e:16], land[:, a // 16:e // 16], T.hi[:, a // 16:e // 16], OP.min)
-        if t == 0:
-            val = names()
-        for j, (a, e) in enumerate(PARTS):
-            wait("v", m[j])
-            m[j] = scan(T.bc[:, a:e], T.rz[:, a:e], T.rp[:, a:e], -4.0, OP.max, OP.add)
-        unit_codes(1)
-        for j, (a, e) in enumerate(PARTS):
-            wait("v", m[j])
-            m[j] = turn(T.mb[:, a:e], T.bc[:, a:e])
-        unit_codes(2)
-        for j, (a, e) in enumerate(PARTS):
-            wait("v", m[j])
-            m[j] = scan(T.stp[:, a + 1:e + 1], T.mb[:, a:e], T.mb[:, a + 1:e + 1], 0.0, OP.min, OP.subtract)
+        def mix(j, step):
+            a, e = PARTS[j]
+            wait("v", m[j], at[j])
+            m[j] = (lambda: tt(T.rp[:, a:e:16], land[:, a // 16:e // 16], T.hi[:, a // 16:e // 16], OP.min),
+                    lambda: scan(T.bc[:, a:e], T.rz[:, a:e], T.rp[:, a:e], -4.0, OP.max, OP.add),
+                    lambda: turn(T.mb[:, a:e], T.bc[:, a:e]),
+                    lambda: scan(T.stp[:, a + 1:e + 1], T.mb[:, a:e], T.mb[:, a + 1:e + 1], 0.0, OP.min, OP.subtract))[step]()
 
         def order_scans(ks):
             return [scan(T.so[:, STEPS * k + 16 * k:STEPS * (k + 1)], T.stp[:, 16 * k:STEPS], T.mul[:, 0:STEPS - 16 * k],
@@ -445,30 +480,57 @@ def rank_program(g, core, T, topo):
             wait("s", mx(bank[4 + b][:, 0:C], cols(eq, 128 * b, 128 * b + 128), cols(aq, 0, C)))
             return act(elem(win, b, C, 2 * C), bank[4 + b][:, 0:C], AF.Copy, scale=32.0)
 
+        mix(0, 0)
         if t == 0:
-            wait("v", g3)
-            ts(T.w4[:, 16:32], T.c4[:], q1_col, OP.is_gt)
-            ts(T.w4[:, 32:48], T.c4[:], q1_col, OP.is_equal, 2.0 ** 40, OP.mult)
-        window = [unpack(b) for b in range(3 if t == 0 else 4)]
+            ts(T.mb[:, C:C + 1], c16[:, 0:1], LAST * UNIT, OP.add)
+        wait("v", lo)
+        m.append(bound(1))
+        if t == 0:
+            ts(T.cb[:], c16_1[:, 0:16], r1_col, OP.not_equal, 2.0 ** -12, OP.max)
+        mix(0, 1)
+        if t == 0:
+            ts(T.iou[:], T.cap[:], 1.0 / C, OP.mult, (CAP + C + NAME0 - 1) * UNIT, OP.add)
+        unit_codes(0)
+        mix(0, 2)
+        if t == 0:
+            tt(T.mul[:, 0:16], T.ca[:], T.cb[:], OP.add)
+            ts(T.stp[:, 0:STEPS:STEPS - 1], c16[:, 0:2], LEAVE * UNIT, OP.mult)
+            wait("s", turned, g4)
+            wait("s", act(nq_col, q1_col, AF.Copy, scale=-1.0))
+            wait("s", act(T.s4[:], T.n4[:], AF.Sign, bias=nq_col))
+            act(zb_col, t_col, AF.Identity, bias=-4.0 * NAME0)
+            wn4 = act(T.wn4[:], T.s4[:], AF.Relu, scale=BIG)
+        unit_codes(1)
+        mix(0, 3)
+        mix(1, 0)
+        if t == 0:
+            val = names()
         wait("v", m[0], k0)
-        order_scans(range(NB - 1, CU, -1))
-        wait("v", m)
-        upper = order_scans(range(CU, 5, -1))
-        order_scans([5, 4, 3])
-        wait("v", upper)
-        p = places(6, NB)
-        if t == 0:
-            wait("s", tt(T.w4[:, 0:16], T.w4[:, 16:32], T.w4[:, 32:48], OP.add))
-            wn4 = act(T.wn4[:], T.w4[:, 0:16].indirect(T.rep[:]), AF.Copy)
-        m = order_scans([2, 1, 0])
+        order_scans(range(NB - 1, NB - 5, -1))
+        mix(1, 1)
+        done = order_scans(range(NB - 5, CU, -1))
+        mix(1, 2)
+        unit_codes(2)
+        wait("v", done[1])
+        p = places(CU + 2, NB)
+        unit_codes(3)
+        window = [unpack(b) for b in range(4)]
+        mix(1, 3)
         wait("v", p, val)
-        nm = scatter(6, NB)
+        nm = scatter(CU + 2, NB)
+        wait("v", m)
+        done = order_scans(range(CU, 5, -1))
+        order_scans([5, 4])
+        wait("v", done)
+        p = places(6, CU + 2)
+        m = order_scans([3, 2, 1, 0])
+        wait("v", p, nm)
+        nm = scatter(6, CU + 2)
         wait("v", m)
         p = places(0, 6)
         if t == 0:
-            unit_codes(3)
-            window = unpack(3)
-            m = ts(sc4_col, q_col, 3.0, OP.is_equal, 2.0 ** -40, OP.max)
+            wait("v", wn4)
+            m = ts(T.w4[:], T.n4[:, 0:4], q1_col, OP.is_le, 1.0 / BIG, OP.max)
         if t == 1:
             wait("v", lv)
             vqm = quant(vq, 0, 128, T.vt)
@@ -476,9 +538,8 @@ def rank_program(g, core, T, topo):
         nm = scatter(0, 6)
         if t == 0:
             wait("v", m)
-            ts(sc4_col, sc4_col, 4.0 / UNIT, OP.mult)
-            ts(zb_col, t_col, -4.0 * NAME0, OP.add)
-        wait("v", nm, wn4)
+            scan(T.pf[:, 5:9], T.w4[:], T.rz[:, 1:5], 4.0 / UNIT, OP.mult, OP.max)
+        wait("v", nm)
         pieces = ((GATHER[0], C), (U, GATHER[0]), (0, U))
         m = [scan(T.ns[:, a:e], T.wn4[:, a:e], T.nm[:, a:e], 0.0, OP.mult, OP.add) for a, e in pieces]
         zo = []
@@ -535,11 +596,14 @@ def rank_program(g, core, T, topo):
         nb = [add(1, 0)]
         na[3] = last_element(0, na[3])
         nb += [add(1, 1), add(1, 2)]
+        if last:
+            m = add(1, 3)
         wait("v", na)
         xa = quant(xn, U, C, T.xn)
         if not last:
             first = first_scores(xn, xa)
-        nb.append(last_element(1, add(1, 3)))
+            m = add(1, 3)
+        nb.append(last_element(1, m))
         if not last:
             wait("v", first[0])
             tu = turn(T.tc[:, U:C], bank[0][:, 0:C - U])

@@ -2,12 +2,20 @@ import numpy as np
 from concourse.mybir import dt, AluOpType as OP, ActivationFunctionType as AF
 
 C = 320
+U = 192
 H = C // 2
 NB = C // 16
+CU = U // 16
+NR = C // 32
+LOW = U // 32
 ROUNDS = [1, 2, 3]
 CAP = 128
 NAME0 = 1
 HALF = "float16"
+PARTS = ((U, C), (U // 2, U), (0, U // 2))
+SIDES = ((U, C), (0, U))
+A = 160
+LAY = ((A, C), (0, A))
 
 GROW = 513.0 / 512.0
 UNIT = 2.0 ** -9
@@ -20,53 +28,40 @@ BIG = 2.0 ** 36
 MAGIC = 1.5 * 2.0 ** 23
 
 
-def _ends():
+def _behind(j, middle):
     f = np.float32
     x, w = f(W0), []
     for _ in range(STEPS):
         x = f(f(GROW) * x)
         w.append(int(x))
-    b1 = int(f(f(513 * int(np.rint(w[C] / 512.0))) + f(257.5)))
-    behind = (b1 - 1 + H) % 8192
-    return behind + w[C + 1] - b1 - KAPPA0, -(b1 - 1 - behind + H)
+    b1 = int(f(f(513 * int(np.rint(w[j] / 512.0))) + f(257.5)))
+    behind = (b1 - 1 + middle) % 8192
+    return (behind + w[j + 1] - b1 - KAPPA0) * UNIT, (b1 - 1 - behind + middle) * UNIT
 
 
-LAST, LEAVE = _ends()
+LAST, LAST_BASE = _behind(C, H)
 
-U = 192
-CU = U // 16
-NR = C // 32
-TOP, LOW = NR - 1, CU // 2 - 1
-HIGH, BASE, OVER, STEP, MID = 2.0 ** 26, 3 * 2.0 ** 22, 2.0 ** 34, -1.5, 256.0
-NT = TOP - LOW
-LEN = [min(32 * b + 32, U) for b in range(NR)]
-LEAD = [2] * LOW + [0] + [1] * NT
-RUN = [LEAD[b] + LEN[b] + 1 for b in range(NR)]
-TOPS = sum(RUN[:NT]) - 2
-SU, SL = sum(RUN[LOW + 1:]) + TOPS, sum(RUN[:LOW + 1])
-END = [[2 * SU + SL * h + sum(RUN[b:LOW + 1]) - 1 if b <= LOW else SU * h + sum(RUN[b:]) - 1 for h in range(2)]
-       for b in range(NR)]
-HOLD = RUN[TOP] + SL
-VE = 2
-PARTS = ((U, C), (0, U))
-GATHER = (256, 72)
+HIGH, BASE, STEP, MID = 2.0 ** 26, 3 * 2.0 ** 22, -1.5, 252
+WIDE = C + 4
+ROW = NB * (C + 1)
+VE = 1
+GATHER = (248, 48)
 
 X4 = "float8_e4m3fn_x4"
 SCRATCH = {}
 for _dt, _list in (
         ("bfloat16", (("x0", 4 * C), ("xn", 4 * C), ("ut", 512), ("vt", 512), ("et", 516), ("zt", 4 * C), ("z32", 4 * C),
-                      ("zb", 516), ("un", C), ("rows", 160), ("cols", 160), ("lead", U + 3), ("mid", 32),
-                      ("w32", 96), ("w4", 4), ("n4", C), ("s4", C), ("wn4", C), ("hold", HOLD),
-                      ("cnu", 2 * SU), ("cnl", 2 * SL), ("sg", 2 * (SU + SL)), ("so", NB * STEPS), ("win", 8 * C))),
+                      ("zb", 516), ("rows", 160), ("cols", 160), ("lead", C + 2),
+                      ("w4", 4), ("un", C), ("n4", C), ("s4", C), ("wn4", C), ("hold", C + 2), ("sg", WIDE * NB + 1),
+                      ("cn", ROW + NB), ("so", NB * STEPS), ("win", 8 * C))),
         ("float32", (("pf", 9), ("wb", C), ("ka", 6 * NB), ("kr", NB),
-                     ("k0", NB), ("ca", 16), ("cb", 16), ("cc", 16), ("inc", 32), ("ends", 32), ("ew", 32),
-                     ("tc", C), ("lo", NB), ("hi", NB), ("nm", C), ("ns", C),
-                     ("odb", C), ("ysb", C), ("snd0", 32), ("snd1", 32), ("snd2", 32),
-                     ("land0", NB), ("land1", NB), ("land2", NB))),
-        (HALF, (("mul", STEPS), ("rp", C), ("rz", C), ("bc", C), ("mb", C + 2), ("stp", STEPS),
-                ("cap", C), ("want", C), ("cum", C + 2), ("take", C), ("tkt", C), ("val", C), ("iou", C))),
+                     ("k0", NB), ("ca", 16), ("cb", 16), ("cc", 16),
+                     ("tc", C), ("lo", NB), ("hi", NB), ("nm", C), ("ns", C), ("odb", C), ("ysb", C),
+                     ("snd0", NB), ("snd1", NB), ("snd2", NB), ("land0", NB), ("land1", NB), ("land2", NB))),
+        (HALF, (("mul", STEPS), ("bc", C), ("mb", C + 2), ("stp", STEPS), ("rp", C), ("rz", C), ("val", C), ("iou", C),
+                ("cap", C), ("want", C), ("cum", C + 2), ("take", C), ("tkt", C))),
         ("int32", (("oi", 24),)),
-        ("uint16", (("off", 24), ("eo", 2), ("ep", 2), ("po", NB), ("zo", C // 4)))):
+        ("uint16", (("off", 24), ("po", NB), ("zo", C // 4)))):
     for _n, _w in _list:
         SCRATCH[_n] = ("sbuf", [128, _w], _dt)
 for _q, _s, _w in (("uq", "us", 128), ("pq", "ps", 384), ("vq", "vs", 128), ("wq", "wp", 512), ("eq", "es", 512),
@@ -78,9 +73,9 @@ BANKS = ["p%d" % _b for _b in range(8)]
 for _n in BANKS:
     SCRATCH[_n] = ("psum", [128, 512], "float32")
 
-POOL = ["c%d" % _b for _b in range(130)]
-SEMAPHORES = (POOL + ["la", "lx", "lu", "lv", "lw", "out", "left"]
-              + ["%s%d" % (n, t) for n in ("aq", "au", "al") for t in range(3)])
+POOL = ["c%d" % _b for _b in range(126)]
+SEMAPHORES = (POOL + ["la", "lx", "lu", "lv", "lw", "lp", "out", "left"]
+              + ["%s%d" % (n, t) for n in ("aq", "au", "am", "al") for t in range(3)])
 
 
 def rank_program(g, core, T, topo):
@@ -90,546 +85,486 @@ def rank_program(g, core, T, topo):
     V, S, PE, SY = g.vector, g.scalar, g.tensor, g.sync
     queue = {"g": g, "v": V, "s": S, "p": PE, "y": SY}
 
-    cnt = {n: 0 for n in SEMAPHORES}
-    known = {q: {} for q in queue}
-    calls = {q: 0 for q in queue}
-    free = list(POOL)
-    user = {}
+    def at(name, a=0, e=None, step=1):
+        return (name, slice(a, e, step), None)
 
-    def wait(q, *marks):
-        flat = []
-        for m in marks:
-            flat += [x for y in m for x in (y if isinstance(y, list) else [y])] if isinstance(m, list) else [m]
-        for name, count, done, key in sorted(flat, key=lambda m: -m[2][m[3]]):
-            if known[q].get(key, 0) < done[key]:
-                queue[q].wait_ge(T.sem[name], count)
-                for n, c in done.items():
-                    known[q][n] = max(known[q].get(n, 0), c)
+    def one(name, j):
+        return at(name, j, j + 1)
 
-    def mark(q, ins, name=None, n=1):
-        key = name or q
-        if name is None:
-            calls[q] += 1
-            name = [s for s in free if s not in user or known[q].get(user[s][0], 0) >= user[s][1]][0]
-            free.remove(name)
-            free.append(name)
-            user[name] = (q, calls[q])
-        ins.then_inc(T.sem[name], n)
-        cnt[name] += n
-        return (name, cnt[name], dict(known[q], **{key: calls[q] if key == q else cnt[name]}), key)
+    def by(window, offsets):
+        return (window[0], window[1], offsets)
+
+    def ap(x, cast=None):
+        if not isinstance(x, tuple):
+            return x
+        a = T[x[0]][:, x[1]]
+        a = a.bitcast(cast) if cast else a
+        return a.indirect(ap(x[2])) if x[2] else a
+
+    calls, seen, total = [], {}, {n: 0 for n in SEMAPHORES}
+
+    def call(q, issue, outs, ins, after=(), sem=None):
+        c = {"q": q, "issue": issue, "after": list(after), "sem": sem, "n": len(calls)}
+        if sem:
+            total[sem] += 16
+            c["count"] = total[sem]
+        views = [(x, True) for x in outs] + [(x, False) for x in ins if isinstance(x, tuple)]
+        views += [(x[2], False) for x, _ in views if x[2]]
+        for x, write in views:
+            psum = SCRATCH[x[0]][0] == "psum"
+            mask = sum(1 << j for j in range(SCRATCH[x[0]][1][1])[slice(None) if psum else x[1]])
+            old = seen.setdefault(x[0], [])
+            c["after"] += [o for m, w, o in old if m & mask and o is not c and (w or write or psum and o["q"] != q)]
+            seen[x[0]] = [r for r in old if not write or r[0] & ~mask] + [(mask, write, c)]
+        calls.append(c)
+        return c
 
     def ts(out, in0, s1, op0, s2=None, op1=None):
-        if op1 is None:
-            return mark("v", V.tensor_scalar(out, in0, s1, None, op0))
-        return mark("v", V.tensor_scalar(out, in0, s1, s2, op0, op1))
+        ops = (op0,) if op1 is None else (op0, op1)
+        return call("v", lambda: V.tensor_scalar(ap(out), ap(in0), ap(s1), ap(s2), *ops), [out], [in0, s1, s2])
 
     def tt(out, in0, in1, op):
-        return mark("v", V.tensor_tensor(out, in0, in1, op))
+        return call("v", lambda: V.tensor_tensor(ap(out), ap(in0), ap(in1), op), [out], [in0, in1])
 
     def scan(out, d0, d1, init, op0, op1):
-        return mark("v", V.tensor_tensor_scan(out, d0, d1, init, op0, op1))
+        return call("v", lambda: V.tensor_tensor_scan(ap(out), ap(d0), ap(d1), ap(init), op0, op1), [out], [d0, d1, init])
 
-    def copy(out, in_):
-        return mark("v", V.tensor_copy(out, in_))
+    def copy(out, in_, cast=None):
+        return call("v", lambda: V.tensor_copy(ap(out, cast), ap(in_, cast)), [out], [in_])
 
-    def fill(ap, c):
-        return mark("v", V.memset(ap, c))
+    def fill(out, c):
+        return call("v", lambda: V.memset(ap(out), c), [out], [])
 
-    def quant(q, a, e, tile):
-        return mark("v", V.quantize_mx(q[0][:, a:e], q[1][:, a:e], tile[:, 4 * a:4 * e]))
+    def quant(q, tile):
+        return call("v", lambda: V.quantize_mx(ap(q[0]), ap(q[1]), ap(tile)), q, [tile])
 
     def turn(out, in_):
-        return mark("v", V.transpose(out, in_))
+        return call("v", lambda: V.transpose(ap(out), ap(in_)), [out], [in_])
 
     def act(out, in_, func, **kw):
-        return mark("s", S.activation(out, in_, func, **kw))
+        return call("s", lambda: S.activation(ap(out), ap(in_), func, **{k: ap(x) for k, x in kw.items()}),
+                    [out], [in_] + list(kw.values()))
 
     def iota(out, pattern, base):
-        return mark("g", g.iota(out, pattern, base, 0, allow_small_or_imprecise_dtypes=True))
+        small = {} if out[0] == "oi" else {"allow_small_or_imprecise_dtypes": True}
+        return call("g", lambda: g.iota(ap(out), pattern, base, 0, **small), [out], [])
 
-    def mx(out, a, b):
-        return mark("p", PE.matmul_mx(out, a[0], a[1], b[0], b[1], True, True))
+    def mx(out, a, b, after=()):
+        return call("p", lambda: PE.matmul_mx(ap(out), ap(a[0]), ap(a[1]), ap(b[0]), ap(b[1]), True, True),
+                    [out], list(a + b), after)
 
-    def dma(q, out, in_, name):
-        return mark(q, queue[q].dma_start(out, in_), name, 16)
+    def dma(q, out, in_, name, outs=(), ins=(), after=()):
+        return call(q, lambda: queue[q].dma_start(out, in_), outs, ins, after, name)
 
-    def cols(q, a, b):
-        return (q[0][:, a:b], q[1][:, a:b])
+    def load(q, out, in_, name, after=()):
+        return dma(q, ap(out, dt.uint8 if SCRATCH[out[0]][2] == X4 else None), in_, name, [out], [], after)
+
+    def cols(q, a, e):
+        return (at(q[0], a, e), at(q[1], a, e))
 
     def run(tile, a, e):
-        return tile[:, 4 * a:4 * e]
+        return at(tile, 4 * a, 4 * e)
 
     def elem(tile, b, a, e):
-        return tile[:, 4 * a + b:4 * e:4]
+        return at(tile, 4 * a + b, 4 * e, 4)
 
-    sc_col, nq_col, zb_col, sc4_col = (T.pf[:, j:j + 1] for j in (0, 1, 2, 8))
-    half_col = [T.pf[:, j:j + 1] for j in (3, 4)]
-    c16, c16_1, c32, c4 = (T.rows[:, 32 * j:32 * j + 32] for j in range(4))
-    r1_col, x_col, t_col, q1_col = (T.cols[:, 32 * j:32 * j + 1] for j in range(1, 5))
-    bank = [T[n] for n in BANKS]
-    win = T.win
-    eq, wq, zq, vq = (T.eq, T.es), (T.wq, T.wp), (T.zq, T.zs), (T.vq, T.vs)
-    even32, odd32, sign16 = (cols((T.pq, T.ps), 128 * j, 128 * j + 128) for j in range(3))
-    plain = cols((T.uq, T.us), 0, 128)
-    xqs = [(T["xq%d" % t], T["xs%d" % t]) for t in range(4)]
+    def bank(k, n):
+        return at(BANKS[k], 0, n)
 
-    ka, members, steps = [T.ka[:, NB * j:NB * j + NB] for j in range(6)], T.wb[:, 15:C:16], []
+    sc4_col, nq_col, zb_col = (one("pf", j) for j in (8, 1, 2))
+    half_col = [one("pf", j) for j in (3, 4)]
+    r1_col, x_col, t_col, q1_col = (one("cols", 32 * j) for j in range(1, 5))
+    eq, wq, zq, vq = ("eq", "es"), ("wq", "wp"), ("zq", "zs"), ("vq", "vs")
+    even32, odd32, sign16 = (cols(("pq", "ps"), 128 * j, 128 * j + 128) for j in range(3))
+    plain = cols(("uq", "us"), 0, 128)
+    xqs = [("xq%d" % t, "xs%d" % t) for t in range(4)]
+
+    def ka(j, a=0, e=NB, step=1):
+        return at("ka", NB * j + a, NB * j + e, step)
 
     def thresholds(j):
-        wait("s", wb, steps)
+        members = at("wb", 15, C, 16)
         if j == 0:
-            act(ka[4], members, AF.Identity, bias=(UNDER - KAPPA0) * UNIT, scale=GROW * UNIT)
+            act(ka(4), members, AF.Identity, bias=(UNDER - KAPPA0) * UNIT, scale=GROW * UNIT)
         bias, scale = ((MAGIC, 1.0 / 512), (-512.0 * MAGIC, 512.0), (257.5 * UNIT, GROW * UNIT))[j]
-        steps.append(act(ka[j], ka[j - 1] if j else members, AF.Identity, bias=bias, scale=scale))
+        act(ka(j), ka(j - 1) if j else members, AF.Identity, bias=bias, scale=scale)
 
     def picks(a, e):
-        return copy(T.pq[:, a:e].bitcast(dt.uint32), T.uq[:].bitcast(dt.uint32).indirect(T.off[:, a // 16:e // 16]))
+        copy(at("pq", a, e), by(at("uq"), at("off", a // 16, e // 16)), dt.uint32)
 
     def scales(a, e):
-        wait("s", uq, of)
-        return act(T.ps[:, a:e], T.us[:].indirect(T.off[:, a // 16:e // 16]), AF.Copy)
-
-    def holds(bs):
-        return [act(T.hold[:, e - LEN[b] - n:e], T.lead[:, 3 - n:3 + LEN[b]], AF.Identity, bias=STEP)
-                for b in bs for n, e in [(3 * (b < LOW), HOLD - sum(RUN[:b]) - 1)]]
-
-    lu = dma("s", T.ut[:], T.u[:], "lu")
-    lx = [dma("y", run(T.x0, a, e), run(T.x, a, e), name) for (a, e), name in zip(PARTS, ("la", "lx"))]
-    wait("y", lx)
-    dma("y", T.wq[:].bitcast(dt.uint8), T.wc[:], "lw")
-    lw = dma("y", T.wp[:], T.ws[:], "lw")
-    lv = dma("y", T.vt[:], T.v[:], "lv")
-
-    mark("g", g.iota(T.oi[:, 0:16], [[16, 2], [32, 4], [0, 2]], 0, 0))
-    g1 = mark("g", g.iota(T.oi[:, 16:24], [[16, 8]], 1, 0))
-    iota(T.rows[:, 0:64], [[1, 2], [0, 2], [1, 16]], 0)
-    g0 = iota(c32, [[1, 32]], 0)
-    iota(T.inc[:, 1:32:2], [[SL - SU, 2], [0, 8]], SU)
-    iota(T.inc[:, 0:8:2], [[0, NT]], -RUN[TOP] - SU)
-    iota(T.inc[:, 8:9], [[0, 1]], SU - 1 - END[TOP][1])
-    iota(T.inc[:, 10:16:2], [[-32, NT - 1]], -RUN[0] - SU)
-    iota(T.inc[:, 16:17], [[0, 1]], END[0][0] - 2 * SU + TOPS - LEN[NT - 1])
-    g2 = iota(T.inc[:, 18:32:2], [[-32, 7]], -RUN[0] - SL)
-    iota(c4, [[0, 8], [1, 4]], 0)
-    g3 = iota(T.rows[:, 128:160], [[0, 2], [1, 4], [0, 4]], 1)
-    gz = iota(T.zb[:], [[0, 516]], 0)
-    wait("s", fill(T.lead[:, 35:U + 3], 0.0))
-    fill(T.mul[:], GROW)
-    fill(T.rp[:], 0.0)
-    rz = fill(T.rz[:], -100.0)
-    un = []
-    for out, n, c in ((T.un[:, 0:H], H, FAR), (T.un[:, H:C], H, FAR), (T.mid[:], 32, MID),
-                      (T.lead[:, 0:1], 1, -BASE), (T.lead[:, 1:2], 1, OVER), (T.lead[:, 2:3], 1, HIGH - OVER),
-                      (T.hold[:, U + 1:HOLD:SL], 2, -BASE), (T.hold[:, 0:1], 1, BASE),
-                      (T.hold[:, 1:U // 2], U // 2 - 1, STEP), (T.hold[:, U // 2:U + 1], U // 2 + 1, STEP)):
-        un.append(act(out, T.lead[:, 35:35 + n], AF.Identity, bias=float(c)))
-    wait("v", g1)
-    of = copy(T.off[:], T.oi[:])
-    wait("v", g0)
-    m = turn(T.cols[:, 32:96], T.rows[:, 32:96])
-    wait("v", un[1], rz)
-    scan(T.cap[:], T.un[:], T.rz[:], -CAP * FAR, OP.add, OP.max)
-    wait("v", m)
-    lead = ts(T.lead[:, 3:35], c32[:, ::-1], x_col, OP.is_equal, BASE - HIGH, OP.mult)
-    ts(T.w32[:, 32:64], c16, r1_col, OP.is_gt)
-    ts(T.w32[:, 64:96], c16, r1_col, OP.is_equal, 2.0 ** 40, OP.mult)
-    m = ts(T.cc[:], c16_1[:, 15::-1], r1_col, OP.is_gt, 1.0 - GROW, OP.mult)
-    ts(sc_col, r1_col, 16.0, OP.is_equal, 2.0 ** -40, OP.max)
-    wait("v", lu)
-    uq = quant((T.uq, T.us), 0, 128, T.ut)
-    wait("v", m, g2)
-    tt(T.w32[:, 0:32], T.w32[:, 32:64], T.w32[:, 64:96], OP.add)
-    m = scan(T.ends[:], T.inc[:], c16, float(END[LOW + 1][0] + RUN[TOP] + SU), OP.add, OP.max)
-    ts(T.mul[:, 0:16], T.cc[:], GROW, OP.add)
-    wait("s", lead, un[5])
-    holds([LOW, LOW - 1])
-    pks = [scales(a, e) for a, e in ((0, 256), (256, 384))]
-    held = holds(range(LOW - 2, -1, -1))
-    wait("v", uq, of)
-    pk = [picks(0, 256)]
-    wait("v", m)
-    m = scan(T.ew[:], T.w32[:, 0:32], T.ends[:], 0.0, OP.mult, OP.add)
+        act(at("ps", a, e), by(at("us"), at("off", a // 16, e // 16)), AF.Copy)
 
     def own(b, h):
-        return T.tc[:, 32 * b + 16 * h:32 * b + 16 * h + 1]
-
-    def top_end(b, h):
-        return SU * (h + 1) - 1 - sum(RUN[:b - LOW - 1])
+        return one("tc", 32 * b + 16 * h)
 
     def sides(b, h, top):
-        if top:
-            n, e = LEN[b - LOW - 1] + 2 * (b < TOP), top_end(b, h)
-            return T.sg[:, e - n:e], bank[1 + h][:, n - 1::-1]
-        n, e = LEN[b] + 2 * (b < LOW), END[b][h]
-        return T.sg[:, e - n:e], bank[5 + h][:, n - 1::-1]
+        n, e = 32 * b + 32, WIDE * (2 * b + h + 1) - 1
+        if b >= A // 32:
+            n, e = (n - A, e - A) if top else (A, e)
+        return at("sg", e - n, e), at(BANKS[(1 if top else 5) + h], n - 1, None, -1)
 
     def compare(bs, h, top=0):
-        return [ts(*sides(b, h, top), own(b, h), OP.is_lt) for b in bs]
+        for b in bs:
+            ts(*sides(b, h, top), own(b, h), OP.is_lt)
 
     def sign(bs, h, top=0):
-        return [act(*sides(b, h, top), AF.Sign, bias=own(b, h), scale=-1.0) for b in bs]
+        for b in bs:
+            act(*sides(b, h, top), AF.Sign, bias=own(b, h), scale=-1.0)
 
-    def count_tops(h):
-        e = SU * (h + 1)
-        return scan(T.cnu[:, e - TOPS:e], T.sg[:, e - TOPS:e], T.hold[:, HOLD - TOPS:HOLD], HIGH, OP.add, OP.add)
+    def count(bs, h):
+        for b in bs:
+            n, e = 32 * b + 34, WIDE * (2 * b + h + 1) + 1
+            scan(at("cn", ROW + 2 * b + h - NB * (n - 1), None, NB), at("sg", e - n, e), at("hold", 0, n), HIGH, OP.add, OP.add)
 
-    def count_upper(b, h):
-        a, e = END[b][h] + 1 - RUN[b], END[b][h] + 1
-        return scan(T.cnu[:, a:e], T.sg[:, a:e], T.hold[:, 0:RUN[b]], T.cnu[:, top_end(b, h):top_end(b, h) + 1],
-                    OP.add, OP.add)
+    def scores(xq, j, ks):
+        a, e = LAY[j]
+        for k in ks:
+            mx(bank(4 * j + k, e - a), (plain, even32, odd32, sign16)[k], cols(xq, a, e))
 
-    def count_lower(a, b, h):
-        s, e = sum(RUN[a + 1:LOW + 1]), sum(RUN[b:LOW + 1])
-        o = 2 * SU + SL * h
-        return scan(T.cnl[:, SL * h + s:SL * h + e], T.sg[:, o + s:o + e], T.hold[:, RUN[TOP] + s:RUN[TOP] + e],
-                    HIGH * (a == LOW), OP.add, OP.add)
+    def owns(j):
+        a, e = LAY[j]
+        turn(at("tc", a, e), bank(4 * j, e - a))
 
-    def first_scores(xq, made):
-        wait("p", uq, made)
-        m = [mx(bank[0][:, 0:C - U], plain, cols(xq, U, C))]
-        for j, side in enumerate((even32, odd32, sign16)):
-            wait("p", pk[j // 2], pks[j // 2])
-            m.append(mx(bank[1 + j][:, 0:C - U], side, cols(xq, U, C)))
-        return m
+    def want(j):
+        a, e = LAY[j]
+        ts(at("want", a, e), bank(4 * j + 3, e - a), 0.0, OP.is_le, FAR, OP.mult)
 
-    lower, upper = range(LOW, -1, -1), range(TOP, LOW, -1)
+    upper, middle, lower = (list(range(e // 32 - 1, a // 32 - 1, -1)) for a, e in PARTS)
 
-    wait("v", lx[0])
-    xa = quant(xqs[0], U, C, T.x0)
-    pk.append(picks(256, 384))
-    first = first_scores(xqs[0], xa)
-    wait("v", m)
-    eo = ts(T.eo[:], T.ew[:, 15:32:16], sc_col, OP.mult)
-    ts(T.ep[:, 0:1], T.ew[:, 31:32], sc_col, OP.mult, -2.0 * SU, OP.add)
-    wait("v", lx[1])
-    xb = quant(xqs[0], 0, U, T.x0)
-    wait("v", eo, un)
-    slots = copy(T.sg[:].indirect(T.eo[:]), T.mid[:])
-    wait("v", first[0])
-    tu = turn(T.tc[:, U:C], bank[0][:, 0:C - U])
-    wb = scan(T.wb[:], T.mul[:, 0:C], T.mul[:, 0:C], W0, OP.mult, OP.max)
-    wait("s", slots)
-    slots = [act(T.sg[:, SU * h:SU * h + NT * RUN[TOP]:RUN[TOP]], T.mid[:, 0:NT], AF.Copy, scale=-1.0) for h in range(2)]
+    load("y", at("ut"), T.u[:], "lu")
+    lx = [load("y", run("x0", a, e), T.x[:, 4 * a:4 * e], name) for (a, e), name in zip(LAY, ("la", "lx"))]
+    load("y", at("wq"), T.wc[:], "lw", lx)
+    load("y", at("wp"), T.ws[:], "lp")
+    load("y", at("vt"), T.v[:], "lv")
+
+    iota(at("rows", 64, 96), [[1, 32]], 0)
+    iota(at("rows", 0, 64), [[1, 2], [0, 2], [1, 16]], 0)
+    iota(at("oi", 0, 16), [[16, 2], [32, 4], [0, 2]], 0)
+    iota(at("oi", 16, 24), [[16, 8]], 1)
+    iota(at("rows", 96, 128), [[0, 8], [1, 4]], 0)
+    iota(at("rows", 128, 160), [[0, 2], [1, 4], [0, 4]], 1)
+    iota(at("sg", WIDE, None, WIDE), [[0, NB]], MID + 3)
+    iota(at("sg", WIDE - 1, None, WIDE), [[0, NB]], -int(BASE))
+    iota(at("n4"), [[0, C // 4], [1, 4]], 1)
+    fill(at("lead", 32, C + 2), 0.0)
+    fill(at("mul"), GROW)
+    fill(at("rp"), 0.0)
+    fill(at("rz"), -100.0)
+    fill(one("cum", 0), 0.0)
+    fill(one("mb", C), LAST)
+    for a in (0, H):
+        act(at("un", a, a + H), at("lead", 32, 32 + H), AF.Identity, bias=FAR)
+    for a in (0, 258):
+        act(at("zb", a, a + 258), at("lead", 32, 290), AF.Copy)
+    turn(at("cols", 32, 96), at("rows", 32, 96))
+    ts(at("stp", 0, STEPS, STEPS - 1), at("rows", 0, 2), -LAST_BASE, OP.mult)
+    ts(at("cc"), at("rows", 47, 31, -1), r1_col, OP.is_gt, 1.0 - GROW, OP.mult)
+    copy(at("off"), at("oi"))
+    ts(at("lead", 0, 32), at("rows", 95, 63, -1), x_col, OP.is_equal, BASE - HIGH, OP.mult)
+    ts(half_col[0], x_col, 16.0, OP.is_lt)
+    ts(half_col[1], x_col, 16.0, OP.is_ge)
+    ts(at("mul", 0, 16), at("cc"), GROW, OP.add)
+    scan(at("cap"), at("un"), at("rz"), -CAP * FAR, OP.add, OP.max)
+    ts(at("ca"), at("rows", 0, 16), r1_col, OP.is_ge, GROW - 1.0, OP.mult)
+    quant(plain, at("ut"))
+    scan(at("wb"), at("mul", 0, C), at("mul", 0, C), W0, OP.mult, OP.max)
+    quant(cols(xqs[0], A, C), run("x0", A, C))
+    picks(0, 256)
+    scales(0, 256)
+    thresholds(0)
+    scales(256, 384)
+    thresholds(1)
+    act(at("hold"), at("lead"), AF.Identity, bias=STEP)
+    thresholds(2)
+    scores(xqs[0], 0, (0, 1, 2))
+    quant(cols(xqs[0], 0, A), run("x0", 0, A))
+    scores(xqs[0], 1, (1, 2, 0))
+    ts(at("cb"), at("rows", 32, 48), r1_col, OP.not_equal, 2.0 ** -12, OP.max)
+    turn(at("cols", 96, 160), at("rows", 96, 160))
+    owns(0)
+    picks(256, 384)
+    scores(xqs[0], 0, (3,))
+    scores(xqs[0], 1, (3,))
 
     for t, mask_t in enumerate(ROUNDS):
         peer = T.cores[rank ^ mask_t]
         rid, pid = topo.addr(peer)[0:2]
         mask, ne = topo.mask(core, peer), len(topo.engines(core, peer))
         xq, xn = xqs[t], xqs[t + 1]
-        aq = (T["aq%d" % t], T["as%d" % t])
-        snd, land = T["snd%d" % t], T["land%d" % t]
+        aq = ("aq%d" % t, "as%d" % t)
+        snd, land = "snd%d" % t, "land%d" % t
         last = t == len(ROUNDS) - 1
 
-        def send(out, in_, to):
-            g.remote_dma(out, in_, T.sem[to], T.sem.left, pid, rid, mask)
-            cnt[to] += ne
-            cnt["left"] += ne
-            return (to, cnt[to], {to: cnt[to]}, to)
+        def send(out, in_, to, cast=None, w=(pid, rid, mask)):
+            call("g", lambda: g.remote_dma(ap(out, cast), ap(in_, cast), T.sem[to], T.sem.left, *w), [], [in_])
+            total[to] += ne
+            total["left"] += ne
+            return {"q": None, "sem": to, "count": total[to], "known": {to: total[to]}}
 
-        wait("g", xa)
-        send(aq[0][:, U:C].bitcast(dt.uint8), xq[0][:, U:C].bitcast(dt.uint8), "aq%d" % t)
-        wait("g", xb)
-        send(aq[1][:], xq[1][:], "aq%d" % t)
-        if t == 0:
-            wait("g", gz)
-            et = mark("g", g.affine_select(T.et[:], T.zb[:], [[-1, 516]], OP.not_equal, 1.0, 3, 4))
-            g4 = iota(T.n4[:], [[0, C // 4], [1, 4]], 1)
+        def codes(j):
+            return send(at(aq[0], *LAY[j]), at(xq[0], *LAY[j]), "aq%d" % t, dt.uint8)
 
-        wait("p", xb)
-        second = {k: mx(bank[k][:, 0:U], side, cols(xq, 0, U)) for k, side in ((5, even32), (4, plain), (6, odd32), (7, sign16))}
+        def compact(name, j, o=0, of=SIDES):
+            return at(name, o + of[j][0] // 16, o + of[j][1] // 16)
 
-        wait("s", tu, first[1])
-        s_top = sign(upper, 0, 1)
-        wait("v", tu, first[2])
-        v_top = compare(upper, 1, 1)
-        wait("v", first[3])
-        ts(T.want[:, U:C], bank[3][:, 0:C - U], 0.0, OP.is_le, FAR, OP.mult)
-        if t == 0:
-            ts(half_col[0], x_col, 16.0, OP.is_lt)
-            ts(half_col[1], x_col, 16.0, OP.is_ge)
-        wait("v", s_top, held)
-        tops = [count_tops(0)]
-        wait("v", v_top)
-        tops.append(count_tops(1))
-        wait("v", second[4])
-        tl = turn(T.tc[:, 0:U], bank[4][:, 0:U])
-        wait("s", second[5], slots)
-        s_even = sign(upper, 0)
-        wait("s", second[6])
-        s_odd = sign(upper, 1)
-        wait("s", tl)
-        s_low = []
-        for j, b in enumerate(lower):
-            if t == 0 and j % 2 == 0:
-                thresholds(j // 2)
-            s_low += sign([b], 1)
+        def heads(name, j, of=SIDES):
+            return at(name, *of[j], 16)
 
-        def counts(js, h, made):
-            for j in js:
-                wait("v", made[j], tops[h])
-                m = count_upper(upper[j], h)
-            return m
+        def table(j):
+            ts(compact(snd, j, 0, PARTS), compact("cn", j, ROW, PARTS), -0.5 * UNIT, OP.mult, (MID / 2 - UNDER) * UNIT, OP.add)
+            return send(compact(land, j, 0, PARTS), compact(snd, j, 0, PARTS), ("au%d", "am%d", "al%d")[j] % t)
 
-        def part(j):
-            a, e = PARTS[j]
-            return snd[:, 16 * j:16 * j + (e - a) // 16]
-
-        def table(j, to):
-            a, e = PARTS[j]
-            sn.append(ts(snd[:, 16 * j:16 * j + 16], (T.cnu, T.cnl)[j][:].indirect((T.eo, T.ep)[j][:, 0:1]),
-                         -0.5 * UNIT, OP.mult, (MID / 2 - UNDER) * UNIT, OP.add))
-            wait("g", sn)
-            at.append(send(land[:, a // 16:e // 16], part(j), to))
+        def flags(j, step):
+            a, e = SIDES[j]
+            if step == 0:
+                scan(at("take", a, e), at("cum", a + 1, e + 1), at("cum", a, e), 0.0, OP.max, OP.subtract)
+            else:
+                turn(at("tkt", a, e), at("take", a, e))
 
         def entries(j):
-            a, e = PARTS[j]
-            return ts(T.lo[:, a // 16:e // 16], part(j), -FAR, OP.add, 1.0 / FAR, OP.mult)
-
-        sn, at = [], []
-        if t == 0:
-            ts(T.cum[:, 0:1], c16[:, 0:1], 0.0, OP.add)
-        counts(range(2), 0, s_even)
-        wait("v", second[7])
-        want = ts(T.want[:, 0:U], bank[7][:, 0:U], 0.0, OP.is_le, FAR, OP.mult)
-        counts(range(2, NT), 0, s_even)
-        wait("v", tl)
-        v_low = compare(lower[:1], 0)
-        counts(range(2), 1, s_odd)
-        v_low += compare(lower[1:VE], 0)
-        wait("s", v_low)
-        signs = sign(lower[VE:], 0)
-        counted = counts(range(2, NT), 1, s_odd)
-        wait("v", want)
-        cum = scan(T.cum[:, 1:C + 1], T.want[:], T.cap[:], 0.0, OP.add, OP.max)
-        wait("v", counted)
-        table(0, "au%d" % t)
-        count_lower(LOW, LOW + 1 - VE, 0)
-        if t == 0:
-            wait("v", steps)
-            wait("s", tt(ka[5], ka[4], ka[2], OP.subtract), lx)
-            half = [act(ka[h][:, 0:NR], ka[5][:, h:NB:2], AF.Copy, scale=half_col[h]) for h in range(2)]
-            k0 = act(T.k0[:], ka[2], AF.Identity, bias=-2.0 ** 12 * UNIT, scale=2.0 ** 12)
-            act(run(win, 0, C), run(T.x0, 0, C), AF.Copy, scale=32.0)
-        wait("v", cum)
-        take = [scan(T.take[:, a:e], T.cum[:, a + 1:e + 1], T.cum[:, a:e], 0.0, OP.max, OP.subtract) for a, e in PARTS]
-        wait("v", s_low)
-        count_lower(LOW, 0, 1)
-        wait("v", signs)
-        counted = count_lower(LOW - VE, 0, 0)
-        wait("v", take)
-        tkt = [turn(T.tkt[:, a:e], T.take[:, a:e]) for a, e in PARTS]
-        lo = entries(0)
-        wait("v", counted)
-        table(1, "al%d" % t)
-        arrived = send(aq[0][:, 0:U].bitcast(dt.uint8), xq[0][:, 0:U].bitcast(dt.uint8), "aq%d" % t)
-
-        def unit_codes(b):
-            if t == 0:
-                wait("v", et)
-                eqm.append(mark("v", V.quantize_mx(*cols(eq, 128 * b, 128 * b + 128), T.et[:, 3 - b:515 - b])))
+            ts(compact("lo", j), compact(snd, j), -FAR, OP.add, 1.0 / FAR, OP.mult)
 
         def bound(j):
-            a, e = PARTS[j]
-            return tt(T.hi[:, a // 16:e // 16], T.lo[:, a // 16:e // 16], T.tkt[:, a:e:16], OP.mult)
+            tt(compact("hi", j), compact("lo", j), heads("tkt", j), OP.mult)
 
         def back(j):
-            a, e = PARTS[j]
-            return tt(T.rz[:, a:e:16], T.tkt[:, a:e:16], T.kr[:, a // 16:e // 16], OP.add)
+            tt(heads("rz", j), heads("tkt", j), compact("kr", j), OP.add)
 
         def names():
-            return scan(T.val[:], T.iou[:], T.take[:], 0.0, OP.max, OP.subtract)
-
-        if t == 0:
-            eqm = []
-            wait("v", half)
-            kr = [tt(T.kr[:, h:NB:2], ka[0][:, 0:NR], ka[1][:, 0:NR], OP.add) for h in range(2)]
-        else:
-            val = names()
-        wait("v", tkt[0], lo)
-        m = [bound(0)]
-        if t == 0:
-            wait("v", g3)
-            turned = turn(T.cols[:, 96:160], T.rows[:, 96:160])
-            ts(T.ca[:], c16[:, 0:16], r1_col, OP.is_ge, GROW - 1.0, OP.mult)
-        wait("v", kr)
-        back(0)
-        wait("v", sn, tkt)
-        lo = entries(1)
-        back(1)
+            scan(at("val"), at("iou"), at("take"), 0.0, OP.max, OP.subtract)
 
         def mix(j, step):
             a, e = PARTS[j]
-            wait("v", m[j], at[j])
-            m[j] = (lambda: tt(T.rp[:, a:e:16], land[:, a // 16:e // 16], T.hi[:, a // 16:e // 16], OP.min),
-                    lambda: scan(T.bc[:, a:e], T.rz[:, a:e], T.rp[:, a:e], -4.0, OP.max, OP.add),
-                    lambda: turn(T.mb[:, a:e], T.bc[:, a:e]),
-                    lambda: scan(T.stp[:, a + 1:e + 1], T.mb[:, a:e], T.mb[:, a + 1:e + 1], 0.0, OP.min, OP.subtract))[step]()
+            if step == 0:
+                m = tt(heads("rp", j, PARTS), compact(land, j, 0, PARTS), compact("hi", j, 0, PARTS), OP.min)
+                m["after"].append(landed[j])
+            if step == 1:
+                scan(at("bc", a, e), at("rz", a, e), at("rp", a, e), -4.0, OP.max, OP.add)
+            if step == 2:
+                turn(at("mb", a, e), at("bc", a, e))
+            if step == 3:
+                scan(at("stp", a + 1, e + 1), at("mb", a, e), at("mb", a + 1, e + 1), 0.0, OP.min, OP.subtract)
 
-        def order_scans(ks):
-            return [scan(T.so[:, STEPS * k + 16 * k:STEPS * (k + 1)], T.stp[:, 16 * k:STEPS], T.mul[:, 0:STEPS - 16 * k],
-                         T.k0[:, k:k + 1], OP.add, OP.mult) for k in ks]
+        def order(ks):
+            for k in ks:
+                scan(at("so", STEPS * k + 16 * k, STEPS * (k + 1)), at("stp", 16 * k, STEPS), at("mul", 0, STEPS - 16 * k),
+                     one("k0", k), OP.add, OP.mult)
 
-        def places(a, b):
-            return ts(T.po[:, a:b], T.so[:, STEPS * (a + 1) - 1:STEPS * b:STEPS], 1.0 / (UNIT * GROW), OP.mult, float(H), OP.add)
+        def places(a, e):
+            ts(at("po", a, e), at("so", STEPS * (a + 1) - 1, STEPS * e, STEPS), 1.0 / UNIT, OP.mult, float(H), OP.add)
 
-        def scatter(a, b):
-            return copy(T.nm[:].indirect(T.po[:, a:b]), T.val[:, 16 * a:16 * b])
+        def scatter(a, e):
+            copy(by(at("nm"), at("po", a, e)), at("val", 16 * a, 16 * e))
+
+        def unit_codes(bs):
+            for b in bs if t == 0 else ():
+                quant(cols(eq, 128 * b, 128 * b + 128), at("et", 3 - b, 515 - b))
 
         def unpack(b):
-            wait("p", eqm[b], arrived, sn, signs)
-            wait("s", mx(bank[4 + b][:, 0:C], cols(eq, 128 * b, 128 * b + 128), cols(aq, 0, C)))
-            return act(elem(win, b, C, 2 * C), bank[4 + b][:, 0:C], AF.Copy, scale=32.0)
+            mx(bank(4 + b, C), cols(eq, 128 * b, 128 * b + 128), cols(aq, 0, C), [arrived])
+            act(elem("win", b, C, 2 * C), bank(4 + b, C), AF.Copy, scale=32.0)
 
+        codes(0)
+        send(at(aq[1]), at(xq[1]), "aq%d" % t)
+        if t == 0:
+            call("g", lambda: g.affine_select(T.et[:], T.zb[:], [[-1, 516]], OP.not_equal, 1.0, 3, 4), [at("et")], [at("zb")])
+
+        if t:
+            scores(xq, 1, (1, 2, 0, 3))
+        sign(upper, 0, 1)
+        if t:
+            want(0)
+        compare(upper, 1, 1)
+        compare(upper[:VE], 1)
+        owns(1)
+        if t == 0:
+            want(0)
+        sign(upper, 0)
+        sign(upper[VE:], 1)
+        sign(middle, 1)
+        sign(middle, 0)
+        sign(lower, 0)
+        sign(lower, 1)
+        want(1)
+        count(upper[:VE], 1)
+        count(upper, 0)
+        count(upper[VE:], 1)
+        scan(at("cum", 1, C + 1), at("want"), at("cap"), 0.0, OP.add, OP.max)
+        for h in range(2):
+            compare(middle[:1], h, 1)
+        landed = [table(0)]
+        if t == 0:
+            tt(ka(5), ka(4), ka(2), OP.subtract)
+            for h in range(2):
+                act(ka(h, 0, NR), ka(5, h, NB, 2), AF.Copy, scale=half_col[h])
+        count(middle[1:2], 1)
+        flags(0, 0)
+        count(middle[::2], 1)
+        count(middle, 0)
+        flags(0, 1)
+        entries(0)
+        count(lower, 0)
+        landed.append(table(1))
+        count(lower, 1)
+        bound(0)
+        if t:
+            back(0)
+        flags(1, 0)
+        landed.append(table(2))
+        arrived = codes(1)
+
+        if t == 0:
+            for h in range(2):
+                tt(at("kr", h, NB, 2), ka(0, 0, NR), ka(1, 0, NR), OP.add)
+            act(at("k0"), ka(2), AF.Identity, bias=-2.0 ** 12 * UNIT, scale=2.0 ** 12)
+            act(run("win", 0, C), run("x0", 0, C), AF.Copy, scale=32.0)
+            flags(1, 1)
+            ts(at("iou"), at("cap"), 1.0 / C, OP.mult, (CAP + C + NAME0 - 1) * UNIT, OP.add)
+            back(0)
         mix(0, 0)
-        if t == 0:
-            ts(T.mb[:, C:C + 1], c16[:, 0:1], LAST * UNIT, OP.add)
-        wait("v", lo)
-        m.append(bound(1))
-        if t == 0:
-            ts(T.cb[:], c16_1[:, 0:16], r1_col, OP.not_equal, 2.0 ** -12, OP.max)
+        if t:
+            flags(1, 1)
+        entries(1)
+        unit_codes([0])
         mix(0, 1)
-        if t == 0:
-            ts(T.iou[:], T.cap[:], 1.0 / C, OP.mult, (CAP + C + NAME0 - 1) * UNIT, OP.add)
-        unit_codes(0)
+        back(1)
+        bound(1)
+        unit_codes([1])
         mix(0, 2)
+        names()
         if t == 0:
-            tt(T.mul[:, 0:16], T.ca[:], T.cb[:], OP.add)
-            ts(T.stp[:, 0:STEPS:STEPS - 1], c16[:, 0:2], LEAVE * UNIT, OP.mult)
-            wait("s", turned, g4)
-            wait("s", act(nq_col, q1_col, AF.Copy, scale=-1.0))
-            wait("s", act(T.s4[:], T.n4[:], AF.Sign, bias=nq_col))
+            tt(at("mul", 0, 16), at("ca"), at("cb"), OP.add)
+            act(nq_col, q1_col, AF.Copy, scale=-1.0)
+            act(at("s4"), at("n4"), AF.Sign, bias=nq_col)
             act(zb_col, t_col, AF.Identity, bias=-4.0 * NAME0)
-            wn4 = act(T.wn4[:], T.s4[:], AF.Relu, scale=BIG)
-        unit_codes(1)
-        mix(0, 3)
+            act(at("wn4"), at("s4"), AF.Relu, scale=BIG)
         mix(1, 0)
-        if t == 0:
-            val = names()
-        wait("v", m[0], k0)
-        order_scans(range(NB - 1, NB - 5, -1))
+        mix(0, 3)
+        unit_codes([2])
         mix(1, 1)
-        done = order_scans(range(NB - 5, CU, -1))
+        order([19, 18])
+        mix(2, 0)
+        order([17])
         mix(1, 2)
-        unit_codes(2)
-        wait("v", done[1])
-        p = places(CU + 2, NB)
-        unit_codes(3)
-        window = [unpack(b) for b in range(4)]
+        order([16, 15, 14])
+        mix(2, 1)
         mix(1, 3)
-        wait("v", p, val)
-        nm = scatter(CU + 2, NB)
-        wait("v", m)
-        done = order_scans(range(CU, 5, -1))
-        order_scans([5, 4])
-        wait("v", done)
-        p = places(6, CU + 2)
-        m = order_scans([3, 2, 1, 0])
-        wait("v", p, nm)
-        nm = scatter(6, CU + 2)
-        wait("v", m)
-        p = places(0, 6)
+        order([13])
+        unit_codes([3])
+        for b in range(4):
+            unpack(b)
+        places(CU + 2, NB)
+        mix(2, 2)
+        order([12, 11, 10, 9])
+        mix(2, 3)
+        scatter(CU + 2, NB)
+        order(range(8, 3, -1))
+        places(6, CU + 2)
+        order([3, 2, 1, 0])
+        scatter(6, CU + 2)
+        places(0, 6)
         if t == 0:
-            wait("v", wn4)
-            m = ts(T.w4[:], T.n4[:, 0:4], q1_col, OP.is_le, 1.0 / BIG, OP.max)
+            ts(at("w4"), at("n4", 0, 4), q1_col, OP.is_le, 1.0 / BIG, OP.max)
         if t == 1:
-            wait("v", lv)
-            vqm = quant(vq, 0, 128, T.vt)
-        wait("v", p, nm)
-        nm = scatter(0, 6)
+            quant(cols(vq, 0, 128), at("vt"))
+        scatter(0, 6)
         if t == 0:
-            wait("v", m)
-            scan(T.pf[:, 5:9], T.w4[:], T.rz[:, 1:5], 4.0 / UNIT, OP.mult, OP.max)
-        wait("v", nm)
-        pieces = ((GATHER[0], C), (U, GATHER[0]), (0, U))
-        m = [scan(T.ns[:, a:e], T.wn4[:, a:e], T.nm[:, a:e], 0.0, OP.mult, OP.add) for a, e in pieces]
-        zo = []
-        for j, (a, e) in enumerate(pieces):
-            wait("v", m[j])
-            zo.append(ts(T.zo[:, a // 4:e // 4], T.ns[:, a + 3:e:4], sc4_col, OP.mult, zb_col, OP.add))
+            scan(at("pf", 5, 9), at("w4"), at("lead", 40, 44), 4.0 / UNIT, OP.mult, OP.max)
+        pieces = ((GATHER[0], C), (A, GATHER[0]), (0, A))
+        for a, e in pieces:
+            scan(at("ns", a, e), at("wn4", a, e), at("nm", a, e), 0.0, OP.mult, OP.add)
+        for a, e in pieces:
+            ts(at("zo", a // 4, e // 4), at("ns", a + 3, e, 4), sc4_col, OP.mult, zb_col, OP.add)
         if last:
-            wait("s", nm)
-            wait("y", act(T.odb[:], T.nm[:], AF.Identity, bias=-float(NAME0), scale=1.0 / UNIT))
+            act(at("odb"), at("nm"), AF.Identity, bias=-float(NAME0), scale=1.0 / UNIT)
             for k in range(8):
-                dma("y", T.od[k:k + 1, :], T.odb[16 * k:16 * k + 1, :], "out")
+                dma("y", T.od[k:k + 1, :], T.odb[16 * k:16 * k + 1, :], "out", ins=[at("odb")])
 
-        zv, zs = [], []
-        for j, (a, e) in enumerate(PARTS):
+        for j, (a, e) in enumerate(LAY):
             c = GATHER[j]
-            wait("s", zo[2 * j], window)
-            zs.append(act(run(T.zt, c, e), win[:].indirect(T.zo[:, c // 4:e // 4]), AF.Copy, scale=2.0 ** -5))
-            wait("v", zo[j + 1], window)
-            zv.append(ts(run(T.zt, a, c), win[:].indirect(T.zo[:, a // 4:c // 4]), 2.0 ** -5, OP.mult))
+            act(run("zt", c, e), by(at("win"), at("zo", c // 4, e // 4)), AF.Copy, scale=2.0 ** -5)
+            ts(run("zt", a, c), by(at("win"), at("zo", a // 4, c // 4)), 2.0 ** -5, OP.mult)
 
-        def products(j, made):
-            a, e = PARTS[j]
-            wait("p", made)
-            return [mx(bank[4 * j + b][:, 0:e - a], cols(wq, 128 * b, 128 * b + 128), cols(zq, a, e)) for b in range(4)]
+        def products(j):
+            a, e = LAY[j]
+            quant(cols(zq, a, e), run("zt", a, e))
+            for b in range(4):
+                mx(bank(4 * j + b, e - a), cols(wq, 128 * b, 128 * b + 128), cols(zq, a, e))
 
         def scaled(j):
-            (a, e), c = PARTS[j], GATHER[j]
-            wait("s", zs[j])
-            wait("v", zv[j])
-            return [act(run(T.z32, c, e), run(T.zt, c, e), AF.Copy, scale=32.0),
-                    ts(run(T.z32, a, c), run(T.zt, a, c), 32.0, OP.mult)]
+            (a, e), c = LAY[j], GATHER[j]
+            act(run("z32", c, e), run("zt", c, e), AF.Copy, scale=32.0)
+            ts(run("z32", a, c), run("zt", a, c), 32.0, OP.mult)
 
-        def add(j, b):
-            a, e = PARTS[j]
-            wait("v", r[j][b], z32[j])
-            m = tt(elem(win, b, a, e), bank[4 * j + b][:, 0:e - a], elem(T.z32, b, a, e), OP.add)
-            if b == 3:
-                return m
-            wait("s", m)
-            return act(elem(T.xn, b, a, e), elem(win, b, a, e), AF.Copy, scale=2.0 ** -5)
+        def add(j, bs):
+            a, e = LAY[j]
+            for b in bs:
+                tt(elem("win", b, a, e), bank(4 * j + b, e - a), elem("z32", b, a, e), OP.add)
+                if b < 3:
+                    act(elem("xn", b, a, e), elem("win", b, a, e), AF.Copy, scale=2.0 ** -5)
 
-        def last_element(j, m):
-            a, e = PARTS[j]
-            wait("v", m)
-            return ts(elem(T.xn, 3, a, e), elem(win, 3, a, e), 2.0 ** -5, OP.mult)
+        def last_element(j):
+            a, e = LAY[j]
+            ts(elem("xn", 3, a, e), elem("win", 3, a, e), 2.0 ** -5, OP.mult)
 
-        wait("p", lw, window)
-        wait("v", zv[0], zs[0])
-        r = [products(0, quant(zq, U, C, T.zt))]
-        z32 = [scaled(0), scaled(1)]
-        wait("v", zs[1])
-        r.append(products(1, quant(zq, 0, U, T.zt)))
-        na = [add(0, b) for b in range(4)]
-        nb = [add(1, 0)]
-        na[3] = last_element(0, na[3])
-        nb += [add(1, 1), add(1, 2)]
-        if last:
-            m = add(1, 3)
-        wait("v", na)
-        xa = quant(xn, U, C, T.xn)
+        products(0)
+        scaled(0)
+        scaled(1)
+        products(1)
+        add(0, range(4))
+        add(1, [0, 1])
+        last_element(0)
+        add(1, [2, 3])
+        quant(cols(xn, A, C), run("xn", A, C))
         if not last:
-            first = first_scores(xn, xa)
-            m = add(1, 3)
-        nb.append(last_element(1, m))
+            scores(xn, 0, (0, 1, 3, 2))
+        last_element(1)
+        quant(cols(xn, 0, A), run("xn", 0, A))
         if not last:
-            wait("v", first[0])
-            tu = turn(T.tc[:, U:C], bank[0][:, 0:C - U])
-        wait("v", nb)
-        xb = quant(xn, 0, U, T.xn)
+            owns(0)
 
-    wait("p", vqm, xa)
-    my = mx(bank[0][:, 0:C - U], cols(vq, 0, 128), cols(xn, U, C))
-    wait("y", xa)
-    dma("y", run(T.oc, U, C), T.xq3[:, U:C].bitcast(dt.uint8), "out")
-    wait("s", my)
-    wait("y", act(T.ysb[:, U:C], bank[0][:, 0:C - U], AF.Copy))
-    dma("y", T.y[:, U:C], T.ysb[:, U:C], "out")
-    wait("p", xb)
-    my = [mx(bank[k][:, 0:128], cols(vq, 0, 128), cols(xn, a, a + 128)) for k, a in ((1, 0), (2, U - 128))]
-    wait("v", my[0])
-    m = copy(T.ysb[:, 0:112], bank[1][:, 0:112])
-    wait("s", xb)
-    wait("y", xb)
-    dma("s", run(T.oc, 0, U), T.xq3[:, 0:U].bitcast(dt.uint8), "out")
+    def store(q, out, x):
+        dma(q, out, ap(x, dt.uint8 if SCRATCH[x[0]][2] == X4 else None), "out", ins=[x])
+
+    mx(bank(0, C - A), cols(vq, 0, 128), cols(xn, A, C))
+    store("y", T.oc[:, 4 * A:4 * C], at(xn[0], A, C))
+    act(at("ysb", A, C), bank(0, C - A), AF.Copy)
+    store("y", T.y[:, A:C], at("ysb", A, C))
+    mx(bank(1, A), cols(vq, 0, 128), cols(xn, 0, A))
+    copy(at("ysb", 0, A), bank(1, A))
+    store("s", T.oc[:, 0:4 * A], at(xn[0], 0, A))
     for k in range(4):
-        dma("sy"[k % 2], T.osc[4 * k:4 * k + 4, :], T.xs3[32 * k:32 * k + 4, :], "out")
-    wait("y", m)
-    dma("y", T.y[:, 0:112], T.ysb[:, 0:112], "out")
-    wait("s", my[1])
-    wait("s", act(T.ysb[:, 112:U], bank[2][:, 240 - U:128], AF.Copy))
-    dma("s", T.y[:, 112:U], T.ysb[:, 112:U], "out")
-    for n in sorted(SEMAPHORES, key=lambda n: n == "out"):
-        wait("g", (n, cnt[n], {n: cnt[n]}, n))
+        dma("sy"[k % 2], T.osc[4 * k:4 * k + 4, :], T.xs3[32 * k:32 * k + 4, :], "out", ins=[at(xn[1])])
+    store("y", T.y[:, 0:A], at("ysb", 0, A))
+    call("g", None, [], [], [{"q": None, "sem": n, "count": total[n], "known": {n: total[n]}} for n in ("left", "out")])
+
+    known, done = {q: {} for q in queue}, {q: 0 for q in queue}
+    for c in calls:
+        q, c["waits"] = c["q"], []
+        for o in sorted(c["after"], key=lambda o: -o.get("n", len(calls))):
+            key = o["sem"] or o["q"]
+            if known[q].get(key, 0) < o["known"][key]:
+                c["waits"].append(o)
+                o["awaited"] = True
+                for n, m in o["known"].items():
+                    known[q][n] = max(known[q].get(n, 0), m)
+        done[q] += not c["sem"]
+        c["before"] = dict(known[q])
+        c["known"] = dict(known[q], **({c["sem"]: c["count"]} if c["sem"] else {q: done[q]}))
+    free, user = list(POOL), {}
+    for c in calls:
+        for o in c["waits"]:
+            queue[c["q"]].wait_ge(T.sem[o.get("pool") or o["sem"]], o["count"])
+        ins = c["issue"]() if c["issue"] else None
+        if c["sem"]:
+            ins.then_inc(T.sem[c["sem"]], 16)
+        elif c.get("awaited"):
+            q = c["q"]
+            name = [s for s in free if s not in user or c["before"].get(user[s][0], 0) >= user[s][1]][0]
+            free.remove(name)
+            free.append(name)
+            total[name] += 1
+            user[name] = (q, c["known"][q])
+            c["pool"], c["count"] = name, total[name]
+            ins.then_inc(T.sem[name], 1)

import numpy as np
from concourse.mybir import dt, AluOpType as OP, ActivationFunctionType as AF

C = 320
U = 192
H = C // 2
NB = C // 16
CU = U // 16
NR = C // 32
LOW = U // 32
ROUNDS = [1, 2, 3]
CAP = 128
NAME0 = 1
HALF = "float16"
PARTS = ((U, C), (U // 2, U), (0, U // 2))
SIDES = ((U, C), (0, U))
A = 160
LAY = ((A, C), (0, A))

GROW = 513.0 / 512.0
UNIT = 2.0 ** -9
FAR = C * UNIT
W0 = 8522306.0
KAPPA0 = 1152
UNDER = KAPPA0 + 514
STEPS = C + 2
BIG = 2.0 ** 36
MAGIC = 1.5 * 2.0 ** 23


def _behind(j, middle):
    f = np.float32
    x, w = f(W0), []
    for _ in range(STEPS):
        x = f(f(GROW) * x)
        w.append(int(x))
    b1 = int(f(f(513 * int(np.rint(w[j] / 512.0))) + f(257.5)))
    behind = (b1 - 1 + middle) % 8192
    return (behind + w[j + 1] - b1 - KAPPA0) * UNIT, (b1 - 1 - behind + middle) * UNIT


LAST, LAST_BASE = _behind(C, H)

HIGH, BASE, STEP, MID = 2.0 ** 26, 3 * 2.0 ** 22, -1.5, 252
WIDE = C + 4
ROW = NB * (C + 1)
VE = 1
GATHER = (248, 48)

X4 = "float8_e4m3fn_x4"
SCRATCH = {}
for _dt, _list in (
        ("bfloat16", (("x0", 4 * C), ("xn", 4 * C), ("ut", 512), ("vt", 512), ("et", 516), ("zt", 4 * C), ("z32", 4 * C),
                      ("zb", 516), ("rows", 160), ("cols", 160), ("lead", C + 2),
                      ("w4", 4), ("un", C), ("n4", C), ("s4", C), ("wn4", C), ("hold", C + 2), ("sg", WIDE * NB + 1),
                      ("cn", ROW + NB), ("so", NB * STEPS), ("win", 8 * C))),
        ("float32", (("pf", 9), ("wb", C), ("ka", 6 * NB), ("kr", NB),
                     ("k0", NB), ("ca", 16), ("cb", 16), ("cc", 16),
                     ("tc", C), ("lo", NB), ("hi", NB), ("nm", C), ("ns", C), ("odb", C), ("ysb", C),
                     ("snd0", NB), ("snd1", NB), ("snd2", NB), ("land0", NB), ("land1", NB), ("land2", NB))),
        (HALF, (("mul", STEPS), ("bc", C), ("mb", C + 2), ("stp", STEPS), ("rp", C), ("rz", C), ("val", C), ("iou", C),
                ("cap", C), ("want", C), ("cum", C + 2), ("take", C), ("tkt", C))),
        ("int32", (("oi", 24),)),
        ("uint16", (("off", 24), ("po", NB), ("zo", C // 4)))):
    for _n, _w in _list:
        SCRATCH[_n] = ("sbuf", [128, _w], _dt)
for _q, _s, _w in (("uq", "us", 128), ("pq", "ps", 384), ("vq", "vs", 128), ("wq", "wp", 512), ("eq", "es", 512),
                   ("zq", "zs", C), ("xq0", "xs0", C), ("xq1", "xs1", C),
                   ("xq2", "xs2", C), ("xq3", "xs3", C), ("aq0", "as0", C), ("aq1", "as1", C), ("aq2", "as2", C)):
    SCRATCH[_q] = ("sbuf", [128, _w], X4)
    SCRATCH[_s] = ("sbuf", [128, _w], "uint8")
BANKS = ["p%d" % _b for _b in range(8)]
for _n in BANKS:
    SCRATCH[_n] = ("psum", [128, 512], "float32")

POOL = ["c%d" % _b for _b in range(126)]
SEMAPHORES = (POOL + ["la", "lx", "lu", "lv", "lw", "lp", "out", "left"]
              + ["%s%d" % (n, t) for n in ("aq", "au", "am", "al") for t in range(3)])


def rank_program(g, core, T, topo):
    rank = T.rank_of(core)
    if rank is None:
        return
    V, S, PE, SY = g.vector, g.scalar, g.tensor, g.sync
    queue = {"g": g, "v": V, "s": S, "p": PE, "y": SY}

    def at(name, a=0, e=None, step=1):
        return (name, slice(a, e, step), None)

    def one(name, j):
        return at(name, j, j + 1)

    def by(window, offsets):
        return (window[0], window[1], offsets)

    def ap(x, cast=None):
        if not isinstance(x, tuple):
            return x
        a = T[x[0]][:, x[1]]
        a = a.bitcast(cast) if cast else a
        return a.indirect(ap(x[2])) if x[2] else a

    calls, seen, total = [], {}, {n: 0 for n in SEMAPHORES}

    def call(q, issue, outs, ins, after=(), sem=None):
        c = {"q": q, "issue": issue, "after": list(after), "sem": sem, "n": len(calls)}
        if sem:
            total[sem] += 16
            c["count"] = total[sem]
        views = [(x, True) for x in outs] + [(x, False) for x in ins if isinstance(x, tuple)]
        views += [(x[2], False) for x, _ in views if x[2]]
        for x, write in views:
            psum = SCRATCH[x[0]][0] == "psum"
            mask = sum(1 << j for j in range(SCRATCH[x[0]][1][1])[slice(None) if psum else x[1]])
            old = seen.setdefault(x[0], [])
            c["after"] += [o for m, w, o in old if m & mask and o is not c and (w or write or psum and o["q"] != q)]
            seen[x[0]] = [r for r in old if not write or r[0] & ~mask] + [(mask, write, c)]
        calls.append(c)
        return c

    def ts(out, in0, s1, op0, s2=None, op1=None):
        ops = (op0,) if op1 is None else (op0, op1)
        return call("v", lambda: V.tensor_scalar(ap(out), ap(in0), ap(s1), ap(s2), *ops), [out], [in0, s1, s2])

    def tt(out, in0, in1, op):
        return call("v", lambda: V.tensor_tensor(ap(out), ap(in0), ap(in1), op), [out], [in0, in1])

    def scan(out, d0, d1, init, op0, op1):
        return call("v", lambda: V.tensor_tensor_scan(ap(out), ap(d0), ap(d1), ap(init), op0, op1), [out], [d0, d1, init])

    def copy(out, in_, cast=None):
        return call("v", lambda: V.tensor_copy(ap(out, cast), ap(in_, cast)), [out], [in_])

    def fill(out, c):
        return call("v", lambda: V.memset(ap(out), c), [out], [])

    def quant(q, tile):
        return call("v", lambda: V.quantize_mx(ap(q[0]), ap(q[1]), ap(tile)), q, [tile])

    def turn(out, in_):
        return call("v", lambda: V.transpose(ap(out), ap(in_)), [out], [in_])

    def act(out, in_, func, **kw):
        return call("s", lambda: S.activation(ap(out), ap(in_), func, **{k: ap(x) for k, x in kw.items()}),
                    [out], [in_] + list(kw.values()))

    def iota(out, pattern, base):
        small = {} if out[0] == "oi" else {"allow_small_or_imprecise_dtypes": True}
        return call("g", lambda: g.iota(ap(out), pattern, base, 0, **small), [out], [])

    def mx(out, a, b, after=()):
        return call("p", lambda: PE.matmul_mx(ap(out), ap(a[0]), ap(a[1]), ap(b[0]), ap(b[1]), True, True),
                    [out], list(a + b), after)

    def dma(q, out, in_, name, outs=(), ins=(), after=()):
        return call(q, lambda: queue[q].dma_start(out, in_), outs, ins, after, name)

    def load(q, out, in_, name, after=()):
        return dma(q, ap(out, dt.uint8 if SCRATCH[out[0]][2] == X4 else None), in_, name, [out], [], after)

    def cols(q, a, e):
        return (at(q[0], a, e), at(q[1], a, e))

    def run(tile, a, e):
        return at(tile, 4 * a, 4 * e)

    def elem(tile, b, a, e):
        return at(tile, 4 * a + b, 4 * e, 4)

    def bank(k, n):
        return at(BANKS[k], 0, n)

    sc4_col, nq_col, zb_col = (one("pf", j) for j in (8, 1, 2))
    half_col = [one("pf", j) for j in (3, 4)]
    r1_col, x_col, t_col, q1_col = (one("cols", 32 * j) for j in range(1, 5))
    eq, wq, zq, vq = ("eq", "es"), ("wq", "wp"), ("zq", "zs"), ("vq", "vs")
    even32, odd32, sign16 = (cols(("pq", "ps"), 128 * j, 128 * j + 128) for j in range(3))
    plain = cols(("uq", "us"), 0, 128)
    xqs = [("xq%d" % t, "xs%d" % t) for t in range(4)]

    def ka(j, a=0, e=NB, step=1):
        return at("ka", NB * j + a, NB * j + e, step)

    def thresholds(j):
        members = at("wb", 15, C, 16)
        if j == 0:
            act(ka(4), members, AF.Identity, bias=(UNDER - KAPPA0) * UNIT, scale=GROW * UNIT)
        bias, scale = ((MAGIC, 1.0 / 512), (-512.0 * MAGIC, 512.0), (257.5 * UNIT, GROW * UNIT))[j]
        act(ka(j), ka(j - 1) if j else members, AF.Identity, bias=bias, scale=scale)

    def picks(a, e):
        copy(at("pq", a, e), by(at("uq"), at("off", a // 16, e // 16)), dt.uint32)

    def scales(a, e):
        act(at("ps", a, e), by(at("us"), at("off", a // 16, e // 16)), AF.Copy)

    def own(b, h):
        return one("tc", 32 * b + 16 * h)

    def sides(b, h, top):
        n, e = 32 * b + 32, WIDE * (2 * b + h + 1) - 1
        if b >= A // 32:
            n, e = (n - A, e - A) if top else (A, e)
        return at("sg", e - n, e), at(BANKS[(1 if top else 5) + h], n - 1, None, -1)

    def compare(bs, h, top=0):
        for b in bs:
            ts(*sides(b, h, top), own(b, h), OP.is_lt)

    def sign(bs, h, top=0):
        for b in bs:
            act(*sides(b, h, top), AF.Sign, bias=own(b, h), scale=-1.0)

    def count(bs, h):
        for b in bs:
            n, e = 32 * b + 34, WIDE * (2 * b + h + 1) + 1
            scan(at("cn", ROW + 2 * b + h - NB * (n - 1), None, NB), at("sg", e - n, e), at("hold", 0, n), HIGH, OP.add, OP.add)

    def scores(xq, j, ks):
        a, e = LAY[j]
        for k in ks:
            mx(bank(4 * j + k, e - a), (plain, even32, odd32, sign16)[k], cols(xq, a, e))

    def owns(j):
        a, e = LAY[j]
        turn(at("tc", a, e), bank(4 * j, e - a))

    def want(j):
        a, e = LAY[j]
        ts(at("want", a, e), bank(4 * j + 3, e - a), 0.0, OP.is_le, FAR, OP.mult)

    upper, middle, lower = (list(range(e // 32 - 1, a // 32 - 1, -1)) for a, e in PARTS)

    load("y", at("ut"), T.u[:], "lu")
    lx = [load("y", run("x0", a, e), T.x[:, 4 * a:4 * e], name) for (a, e), name in zip(LAY, ("la", "lx"))]
    load("y", at("wq"), T.wc[:], "lw", lx)
    load("y", at("wp"), T.ws[:], "lp")
    load("y", at("vt"), T.v[:], "lv")

    iota(at("rows", 64, 96), [[1, 32]], 0)
    iota(at("rows", 0, 64), [[1, 2], [0, 2], [1, 16]], 0)
    iota(at("oi", 0, 16), [[16, 2], [32, 4], [0, 2]], 0)
    iota(at("oi", 16, 24), [[16, 8]], 1)
    iota(at("rows", 96, 128), [[0, 8], [1, 4]], 0)
    iota(at("rows", 128, 160), [[0, 2], [1, 4], [0, 4]], 1)
    iota(at("sg", WIDE, None, WIDE), [[0, NB]], MID + 3)
    iota(at("sg", WIDE - 1, None, WIDE), [[0, NB]], -int(BASE))
    iota(at("n4"), [[0, C // 4], [1, 4]], 1)
    fill(at("lead", 32, C + 2), 0.0)
    fill(at("mul"), GROW)
    fill(at("rp"), 0.0)
    fill(at("rz"), -100.0)
    fill(one("cum", 0), 0.0)
    fill(one("mb", C), LAST)
    for a in (0, H):
        act(at("un", a, a + H), at("lead", 32, 32 + H), AF.Identity, bias=FAR)
    for a in (0, 258):
        act(at("zb", a, a + 258), at("lead", 32, 290), AF.Copy)
    turn(at("cols", 32, 96), at("rows", 32, 96))
    ts(at("stp", 0, STEPS, STEPS - 1), at("rows", 0, 2), -LAST_BASE, OP.mult)
    ts(at("cc"), at("rows", 47, 31, -1), r1_col, OP.is_gt, 1.0 - GROW, OP.mult)
    copy(at("off"), at("oi"))
    ts(at("lead", 0, 32), at("rows", 95, 63, -1), x_col, OP.is_equal, BASE - HIGH, OP.mult)
    ts(half_col[0], x_col, 16.0, OP.is_lt)
    ts(half_col[1], x_col, 16.0, OP.is_ge)
    ts(at("mul", 0, 16), at("cc"), GROW, OP.add)
    scan(at("cap"), at("un"), at("rz"), -CAP * FAR, OP.add, OP.max)
    ts(at("ca"), at("rows", 0, 16), r1_col, OP.is_ge, GROW - 1.0, OP.mult)
    quant(plain, at("ut"))
    scan(at("wb"), at("mul", 0, C), at("mul", 0, C), W0, OP.mult, OP.max)
    quant(cols(xqs[0], A, C), run("x0", A, C))
    picks(0, 256)
    scales(0, 256)
    thresholds(0)
    scales(256, 384)
    thresholds(1)
    act(at("hold"), at("lead"), AF.Identity, bias=STEP)
    thresholds(2)
    scores(xqs[0], 0, (0, 1, 2))
    quant(cols(xqs[0], 0, A), run("x0", 0, A))
    scores(xqs[0], 1, (1, 2, 0))
    ts(at("cb"), at("rows", 32, 48), r1_col, OP.not_equal, 2.0 ** -12, OP.max)
    turn(at("cols", 96, 160), at("rows", 96, 160))
    owns(0)
    picks(256, 384)
    scores(xqs[0], 0, (3,))
    scores(xqs[0], 1, (3,))

    for t, mask_t in enumerate(ROUNDS):
        peer = T.cores[rank ^ mask_t]
        rid, pid = topo.addr(peer)[0:2]
        mask, ne = topo.mask(core, peer), len(topo.engines(core, peer))
        xq, xn = xqs[t], xqs[t + 1]
        aq = ("aq%d" % t, "as%d" % t)
        snd, land = "snd%d" % t, "land%d" % t
        last = t == len(ROUNDS) - 1

        def send(out, in_, to, cast=None, w=(pid, rid, mask)):
            call("g", lambda: g.remote_dma(ap(out, cast), ap(in_, cast), T.sem[to], T.sem.left, *w), [], [in_])
            total[to] += ne
            total["left"] += ne
            return {"q": None, "sem": to, "count": total[to], "known": {to: total[to]}}

        def codes(j):
            return send(at(aq[0], *LAY[j]), at(xq[0], *LAY[j]), "aq%d" % t, dt.uint8)

        def compact(name, j, o=0, of=SIDES):
            return at(name, o + of[j][0] // 16, o + of[j][1] // 16)

        def heads(name, j, of=SIDES):
            return at(name, *of[j], 16)

        def table(j):
            ts(compact(snd, j, 0, PARTS), compact("cn", j, ROW, PARTS), -0.5 * UNIT, OP.mult, (MID / 2 - UNDER) * UNIT, OP.add)
            return send(compact(land, j, 0, PARTS), compact(snd, j, 0, PARTS), ("au%d", "am%d", "al%d")[j] % t)

        def flags(j, step):
            a, e = SIDES[j]
            if step == 0:
                scan(at("take", a, e), at("cum", a + 1, e + 1), at("cum", a, e), 0.0, OP.max, OP.subtract)
            else:
                turn(at("tkt", a, e), at("take", a, e))

        def entries(j):
            ts(compact("lo", j), compact(snd, j), -FAR, OP.add, 1.0 / FAR, OP.mult)

        def bound(j):
            tt(compact("hi", j), compact("lo", j), heads("tkt", j), OP.mult)

        def back(j):
            tt(heads("rz", j), heads("tkt", j), compact("kr", j), OP.add)

        def names():
            scan(at("val"), at("iou"), at("take"), 0.0, OP.max, OP.subtract)

        def mix(j, step):
            a, e = PARTS[j]
            if step == 0:
                m = tt(heads("rp", j, PARTS), compact(land, j, 0, PARTS), compact("hi", j, 0, PARTS), OP.min)
                m["after"].append(landed[j])
            if step == 1:
                scan(at("bc", a, e), at("rz", a, e), at("rp", a, e), -4.0, OP.max, OP.add)
            if step == 2:
                turn(at("mb", a, e), at("bc", a, e))
            if step == 3:
                scan(at("stp", a + 1, e + 1), at("mb", a, e), at("mb", a + 1, e + 1), 0.0, OP.min, OP.subtract)

        def order(ks):
            for k in ks:
                scan(at("so", STEPS * k + 16 * k, STEPS * (k + 1)), at("stp", 16 * k, STEPS), at("mul", 0, STEPS - 16 * k),
                     one("k0", k), OP.add, OP.mult)

        def places(a, e):
            ts(at("po", a, e), at("so", STEPS * (a + 1) - 1, STEPS * e, STEPS), 1.0 / UNIT, OP.mult, float(H), OP.add)

        def scatter(a, e):
            copy(by(at("nm"), at("po", a, e)), at("val", 16 * a, 16 * e))

        def unit_codes(bs):
            for b in bs if t == 0 else ():
                quant(cols(eq, 128 * b, 128 * b + 128), at("et", 3 - b, 515 - b))

        def unpack(b):
            mx(bank(4 + b, C), cols(eq, 128 * b, 128 * b + 128), cols(aq, 0, C), [arrived])
            act(elem("win", b, C, 2 * C), bank(4 + b, C), AF.Copy, scale=32.0)

        codes(0)
        send(at(aq[1]), at(xq[1]), "aq%d" % t)
        if t == 0:
            call("g", lambda: g.affine_select(T.et[:], T.zb[:], [[-1, 516]], OP.not_equal, 1.0, 3, 4), [at("et")], [at("zb")])

        if t:
            scores(xq, 1, (1, 2, 0, 3))
        sign(upper, 0, 1)
        if t:
            want(0)
        compare(upper, 1, 1)
        compare(upper[:VE], 1)
        owns(1)
        if t == 0:
            want(0)
        sign(upper, 0)
        sign(upper[VE:], 1)
        sign(middle, 1)
        sign(middle, 0)
        sign(lower, 0)
        sign(lower, 1)
        want(1)
        count(upper[:VE], 1)
        count(upper, 0)
        count(upper[VE:], 1)
        scan(at("cum", 1, C + 1), at("want"), at("cap"), 0.0, OP.add, OP.max)
        for h in range(2):
            compare(middle[:1], h, 1)
        landed = [table(0)]
        if t == 0:
            tt(ka(5), ka(4), ka(2), OP.subtract)
            for h in range(2):
                act(ka(h, 0, NR), ka(5, h, NB, 2), AF.Copy, scale=half_col[h])
        count(middle[1:2], 1)
        flags(0, 0)
        count(middle[::2], 1)
        count(middle, 0)
        flags(0, 1)
        entries(0)
        count(lower, 0)
        landed.append(table(1))
        count(lower, 1)
        bound(0)
        if t:
            back(0)
        flags(1, 0)
        landed.append(table(2))
        arrived = codes(1)

        if t == 0:
            for h in range(2):
                tt(at("kr", h, NB, 2), ka(0, 0, NR), ka(1, 0, NR), OP.add)
            act(at("k0"), ka(2), AF.Identity, bias=-2.0 ** 12 * UNIT, scale=2.0 ** 12)
            act(run("win", 0, C), run("x0", 0, C), AF.Copy, scale=32.0)
            flags(1, 1)
            ts(at("iou"), at("cap"), 1.0 / C, OP.mult, (CAP + C + NAME0 - 1) * UNIT, OP.add)
            back(0)
        mix(0, 0)
        if t:
            flags(1, 1)
        entries(1)
        unit_codes([0])
        mix(0, 1)
        back(1)
        bound(1)
        unit_codes([1])
        mix(0, 2)
        names()
        if t == 0:
            tt(at("mul", 0, 16), at("ca"), at("cb"), OP.add)
            act(nq_col, q1_col, AF.Copy, scale=-1.0)
            act(at("s4"), at("n4"), AF.Sign, bias=nq_col)
            act(zb_col, t_col, AF.Identity, bias=-4.0 * NAME0)
            act(at("wn4"), at("s4"), AF.Relu, scale=BIG)
        mix(1, 0)
        mix(0, 3)
        unit_codes([2])
        mix(1, 1)
        order([19, 18])
        mix(2, 0)
        order([17])
        mix(1, 2)
        order([16, 15, 14])
        mix(2, 1)
        mix(1, 3)
        order([13])
        unit_codes([3])
        for b in range(4):
            unpack(b)
        places(CU + 2, NB)
        mix(2, 2)
        order([12, 11, 10, 9])
        mix(2, 3)
        scatter(CU + 2, NB)
        order(range(8, 3, -1))
        places(6, CU + 2)
        order([3, 2, 1, 0])
        scatter(6, CU + 2)
        places(0, 6)
        if t == 0:
            ts(at("w4"), at("n4", 0, 4), q1_col, OP.is_le, 1.0 / BIG, OP.max)
        if t == 1:
            quant(cols(vq, 0, 128), at("vt"))
        scatter(0, 6)
        if t == 0:
            scan(at("pf", 5, 9), at("w4"), at("lead", 40, 44), 4.0 / UNIT, OP.mult, OP.max)
        pieces = ((GATHER[0], C), (A, GATHER[0]), (0, A))
        for a, e in pieces:
            scan(at("ns", a, e), at("wn4", a, e), at("nm", a, e), 0.0, OP.mult, OP.add)
        for a, e in pieces:
            ts(at("zo", a // 4, e // 4), at("ns", a + 3, e, 4), sc4_col, OP.mult, zb_col, OP.add)
        if last:
            act(at("odb"), at("nm"), AF.Identity, bias=-float(NAME0), scale=1.0 / UNIT)
            for k in range(8):
                dma("y", T.od[k:k + 1, :], T.odb[16 * k:16 * k + 1, :], "out", ins=[at("odb")])

        for j, (a, e) in enumerate(LAY):
            c = GATHER[j]
            act(run("zt", c, e), by(at("win"), at("zo", c // 4, e // 4)), AF.Copy, scale=2.0 ** -5)
            ts(run("zt", a, c), by(at("win"), at("zo", a // 4, c // 4)), 2.0 ** -5, OP.mult)

        def products(j):
            a, e = LAY[j]
            quant(cols(zq, a, e), run("zt", a, e))
            for b in range(4):
                mx(bank(4 * j + b, e - a), cols(wq, 128 * b, 128 * b + 128), cols(zq, a, e))

        def scaled(j):
            (a, e), c = LAY[j], GATHER[j]
            act(run("z32", c, e), run("zt", c, e), AF.Copy, scale=32.0)
            ts(run("z32", a, c), run("zt", a, c), 32.0, OP.mult)

        def add(j, bs):
            a, e = LAY[j]
            for b in bs:
                tt(elem("win", b, a, e), bank(4 * j + b, e - a), elem("z32", b, a, e), OP.add)
                if b < 3:
                    act(elem("xn", b, a, e), elem("win", b, a, e), AF.Copy, scale=2.0 ** -5)

        def last_element(j):
            a, e = LAY[j]
            ts(elem("xn", 3, a, e), elem("win", 3, a, e), 2.0 ** -5, OP.mult)

        products(0)
        scaled(0)
        scaled(1)
        products(1)
        add(0, range(4))
        add(1, [0, 1])
        last_element(0)
        add(1, [2, 3])
        quant(cols(xn, A, C), run("xn", A, C))
        if not last:
            scores(xn, 0, (0, 1, 3, 2))
        last_element(1)
        quant(cols(xn, 0, A), run("xn", 0, A))
        if not last:
            owns(0)

    def store(q, out, x):
        dma(q, out, ap(x, dt.uint8 if SCRATCH[x[0]][2] == X4 else None), "out", ins=[x])

    mx(bank(0, C - A), cols(vq, 0, 128), cols(xn, A, C))
    store("y", T.oc[:, 4 * A:4 * C], at(xn[0], A, C))
    act(at("ysb", A, C), bank(0, C - A), AF.Copy)
    store("y", T.y[:, A:C], at("ysb", A, C))
    mx(bank(1, A), cols(vq, 0, 128), cols(xn, 0, A))
    copy(at("ysb", 0, A), bank(1, A))
    store("s", T.oc[:, 0:4 * A], at(xn[0], 0, A))
    for k in range(4):
        dma("sy"[k % 2], T.osc[4 * k:4 * k + 4, :], T.xs3[32 * k:32 * k + 4, :], "out", ins=[at(xn[1])])
    store("y", T.y[:, 0:A], at("ysb", 0, A))
    call("g", None, [], [], [{"q": None, "sem": n, "count": total[n], "known": {n: total[n]}} for n in ("left", "out")])

    known, done = {q: {} for q in queue}, {q: 0 for q in queue}
    for c in calls:
        q, c["waits"] = c["q"], []
        for o in sorted(c["after"], key=lambda o: -o.get("n", len(calls))):
            key = o["sem"] or o["q"]
            if known[q].get(key, 0) < o["known"][key]:
                c["waits"].append(o)
                o["awaited"] = True
                for n, m in o["known"].items():
                    known[q][n] = max(known[q].get(n, 0), m)
        done[q] += not c["sem"]
        c["before"] = dict(known[q])
        c["known"] = dict(known[q], **({c["sem"]: c["count"]} if c["sem"] else {q: done[q]}))
    free, user = list(POOL), {}
    for c in calls:
        for o in c["waits"]:
            queue[c["q"]].wait_ge(T.sem[o.get("pool") or o["sem"]], o["count"])
        ins = c["issue"]() if c["issue"] else None
        if c["sem"]:
            ins.then_inc(T.sem[c["sem"]], 16)
        elif c.get("awaited"):
            q = c["q"]
            name = [s for s in free if s not in user or c["before"].get(user[s][0], 0) >= user[s][1]][0]
            free.remove(name)
            free.append(name)
            total[name] += 1
            user[name] = (q, c["known"][q])
            c["pool"], c["count"] = name, total[name]
            ins.then_inc(T.sem[name], 1)
